import numpy as np, ml_dtypes
CORES = [16,18,20,22]
N = 4
BF = ml_dtypes.bfloat16
def gentries(a):
    return np.ascontiguousarray(a.reshape(8, 16, -1).transpose(0, 2, 1)).reshape(8, -1)
def gtable(e):
    e = np.asarray(e); return np.ascontiguousarray(e.reshape(8, -1, 16).transpose(0, 2, 1)).reshape(128, -1).astype(np.int32)
NV, NT, NL, RO = 2560, 2560, 256, 4
def graphs(rng):
    tp = np.zeros((N, 8, 16, NT), np.int64); oc = np.zeros((N, 8, 16, NV), np.int64); c = 16 * NT // NV
    for n in range(N):
        for g in range(8):
            e = rng.permutation(16 * NT) % NV
            o = rng.permuted(np.argsort(e.astype(np.uint16), kind="stable").reshape(NV, c), axis=1)
            tp[n, g] = e.reshape(NT, 16).T; oc[n, g] = (o[:, np.arange(16) % c] // 16).T
    return tp, oc
def levels(rng, n):
    return np.floor(rng.random((N, 8, 16, n)) * rng.integers(65, 257, (N, 8, 1, n))).astype(np.int64)
def pack(dom, val, tp, oc, q):
    return {"dom": dom.reshape(N, 128, NV).astype(np.float32).astype(BF), "val": val.reshape(N, 128, NT).astype(np.float32).astype(BF),
            "tp": np.ascontiguousarray(tp.reshape(N, 128, NT)).astype(np.int32), "oc": np.ascontiguousarray(oc.reshape(N, 128, NV)).astype(np.int32), "q": np.stack([gtable(a) for a in q])}
def setup_inputs(rng):
    tp, oc = graphs(rng)
    return pack(levels(rng, NV), levels(rng, NT), tp, oc, rng.integers(0, NT, (N, 8, NL)))
def rolled(rng, n):
    base = rng.integers(0, 250, (N, 8, 16)); sh = rng.integers(0, 16, (N, 8, 1, n))
    x = np.take_along_axis(base, ((np.arange(16)[:, None] + sh) % 16).reshape(N, 8, 16 * n), 2).reshape(N, 8, 16, n)
    x[:, :, 3] += rng.random((N, 8, n)) < 0.1
    return x
def setup_inputs_ties(rng):
    tp, oc = graphs(rng)
    return pack(rolled(rng, NV), rolled(rng, NT), tp, oc, rng.integers(0, NT, (N, 8, NL)))
def setup_inputs_alike(rng):
    tp, oc = graphs(rng); dom = levels(rng, NV); val = levels(rng, NT); q = rng.integers(0, NT, (N, 8, NL))
    q[:, 0] = rng.integers(0, NT, (N, 1)); q[:, 1] = rng.choice(np.array([0, 5, NT - 1, NT - 2, NT // 2]), (N, NL)); q[:, 5] = rng.choice(np.array([0, NT - 1]), (N, NL))
    tp[:, 2] = tp[:, 2, :1]; oc[:, 3] = rng.choice(np.array([0, NT - 1]), (N, 16, NV)); tp[:, 4] = rng.choice(np.array([0, NV - 1, NV // 2]), (N, 16, NT))
    dom[:, 6, :, 7] = 255; np.put_along_axis(tp[:, 6], rng.integers(0, 16, (N, 1, NT)), 7, 1)
    q[:, 7] = 16 * np.argsort(rng.random((N, NT // 16)), axis=1)[:, np.arange(NL) % (NT // 16)] + rng.integers(0, 16, (N, 1))
    tp[:, 7] = 16 * (np.arange(NT) // 16 % (NV // 16)) + rng.integers(0, 16, (N, 1, 1))
    return pack(dom, val, tp, oc, q)
def setup_inputs_full(rng):
    p = np.argsort(rng.random((3, N, 8, NL)), axis=-1); cv = np.arange(NV); ct = np.arange(NT); dom = levels(rng, NV); val = levels(rng, NT)
    bt = rng.integers(0, NV // NL, (N, 8, 16, NT)); bo = rng.integers(0, NT // NL, (N, 8, 16, NV)); bq = rng.integers(0, NT // NL, (N, 8, NL))
    bt[:, 0] = 2 * rng.integers(0, NV // NL // 2, (N, 16, NT)) + (np.arange(N) % 2)[:, None, None]
    bt[:, 1] = rng.integers(0, NV // NL); bq[:, 1] = rng.integers(0, NT // NL); val[:, 1] //= 2
    lt = NT // NL // (RO + 1); lv = NV // NL // RO
    bq[:, 4] = rng.integers(0, lt, (N, NL))
    bt[:, 4] = lv * np.minimum(ct // NL // lt, RO - 1) + rng.integers(0, lv, (N, 16, NT))
    bo[:, 4] = lt * (np.minimum(cv // NL // lv, RO - 1) + 1) + rng.integers(0, lt, (N, 16, NV))
    tp = NL * bt + p[0][:, :, ct % NL][:, :, None, :]
    oc = NL * bo + p[1][:, :, cv % NL][:, :, None, :]
    q = NL * bq + p[2]
    tab = NL * rng.integers(0, NV // NL, (N, 16, NL // 2)) + np.arange(NL // 2)
    tp[:, 2] = np.take_along_axis(tab, (p[0][:, 2][:, ct % NL] // 2)[:, None, :], 2)
    k = (rng.integers(0, NL, (N, 1, NV)) + (NL // 16) * np.arange(16)[:, None]) % NL
    oc[:, 3] = np.take_along_axis(np.repeat(q[:, 3][:, None, :], 16, axis=1), k, 2)
    return pack(dom, val, tp, oc, q)
def setup_inputs_ends(rng):
    tp, oc = graphs(rng)
    dom = 255 * (rng.random((N, 8, 16, NV)) < rng.random((N, 8, 1, NV))).astype(np.int64); val = 255 * (rng.random((N, 8, 16, NT)) < 0.3 * rng.random((N, 8, 1, NT))).astype(np.int64)
    dom[:, 1] = 0; val[:, 2] = 0; val[:, 3] = 255; dom[:, 5] = 255
    dom[:, 4] *= rng.random((N, 1, NV)) < 0.1; val[:, 6] *= rng.random((N, 1, NT)) < 0.1
    dom[:, 7] = rng.integers(240, 256, (N, 16, NV)); val[:, 7] = rng.integers(240, 256, (N, 16, NT))
    return pack(dom, val, tp, oc, rng.integers(0, NT, (N, 8, NL)))
def uneven(rng, n):
    return np.floor(np.exp2(8 * rng.random((N, 8, 1, n)) - 2 * rng.random((N, 8, 16, 1))) * rng.random((N, 8, 16, n))).astype(np.int64)
def setup_inputs_spread(rng):
    tp, oc = graphs(rng)
    return pack(uneven(rng, NV), uneven(rng, NT), tp, oc, np.minimum((NT * rng.random((N, 8, NL)) ** 3).astype(np.int64), NT - 1))
def check_inputs(d):
    bad = []
    for k, hi in (("dom", 255), ("val", 255), ("tp", NV - 1), ("oc", NT - 1), ("q", NT - 1)):
        v = np.asarray(d[k]).astype(np.float64)
        if not (np.all(v >= 0) and np.all(v <= hi) and np.all(v == np.floor(v))): bad.append("range of " + k)
    return bad
def pick(a, ix):
    return np.take_along_axis(a, ix[:, :, None, :], 3)
def reference(dom, val, tp, oc, q):
    dm = dom.astype(np.float32).astype(np.int64).reshape(N, 8, 16, NV); vl = val.astype(np.float32).astype(np.int64).reshape(N, 8, 16, NT)
    tpl = tp.astype(np.int64).reshape(N, 8, 16, NT); occ = oc.astype(np.int64).reshape(N, 8, 16, NV)
    cur = np.stack([gentries(a) for a in q]).astype(np.int64)
    for t in range(RO):
        p = pick(tpl, cur)
        x = pick(dm, p.reshape(N, 8, 16 * NL)).reshape(N, 8, 16, 16, NL)
        best = np.argmax(np.add.reduce(x, axis=2), axis=2)
        a = np.take_along_axis(p, best[:, :, None, :], 2)[:, :, 0]
        np.put_along_axis(vl, cur[:, :, None, :], np.min(x, axis=3), 3)
        p = pick(occ, a)
        x = pick(vl, p.reshape(N, 8, 16 * NL)).reshape(N, 8, 16, 16, NL)
        m = np.minimum(pick(dm, a), np.max(x, axis=3))
        best = np.argmax(np.add.reduce(x, axis=2), axis=2)
        cur = np.take_along_axis(p, best[:, :, None, :], 2)[:, :, 0]
        np.put_along_axis(dm, a[:, :, None, :], m, 3)
        d = 1 + t % (N - 1); ain = np.roll(a, d, axis=0); got = np.roll(m, d, axis=0)
        np.put_along_axis(dm, ain[:, :, None, :], np.minimum(pick(dm, ain), got), 3)
    s = np.stack([np.add.reduce(dm, axis=3), np.add.reduce(vl, axis=3)], axis=-1)
    return {"yt": cur.astype(np.float32), "yv": m.reshape(N, 128, NL).astype(np.float32).astype(BF), "ys": s.reshape(N, 128, 2).astype(np.float32)}

@@ -1,0 +1,374 @@
+from concourse.mybir import AluOpType, AxisListType, ActivationFunctionType
+
+NV, NL, RO, N = 2560, 256, 4, 4
+W = NV + 64
+DW = 320
+MID = 1280.0
+H = "float16"
+CUT = ((0, 52, 128, 192, 240, 256), (0, 28, 76, 128, 128, 192, 240, 256))
+SENDS = ((0, 64), (64, 192), (192, 256))
+MW = 16 * max(b - a for c in CUT for a, b in zip(c[:-1], c[1:]))
+ORDER = """
+SGo1 G01 D00 G00 D01 G02 S00 S01 K00 D02 Aa00 D03 Ab00 D04 Ac00 B10 G03 W1 E10 G04 Q10 S02 W0 U10 W2 Pn10 S03 S04 K01 W3
+SG10 Aa01 Fn10 Ab01 Pf10 Ac01 G10 E11 G11 S10 B11 S11 U11 Q11 G12 SG11 N0 Ff10 P11 S12 D10 K10 M10 Aa10 D11 D12 Ab10 G14
+D13 Ac10 D14 G15 E20 G16 O0 S14 F11 SV N1 B20 U20 T1 O1 S15 O2 S16 N2 M11 K11 O3 YV T0 T2 Aa11 Ab11 R0 Q20 Ac11 I0 E21 R1
+U21 I2 T3 P2 I1 YT YU SG20 B21 F2 Z0 SB SA R2 Q21 RL Z1 M20 Z2 Z3 I3 M21
+""".split()
+
+SCRATCH = {
+    "domt": ("sbuf", [128, W], "bfloat16"), "valt": ("sbuf", [128, W], "bfloat16"),
+    "tpt": ("sbuf", [128, NV], "int32"), "oct": ("sbuf", [128, NV], "int32"),
+    "qi": ("sbuf", [128, 16], "int32"), "qf": ("sbuf", [128, 16], "float32"),
+    "zmin": ("sbuf", [128, MW], "bfloat16"), "zmax": ("sbuf", [128, MW], "bfloat16"),
+    "pi": ("sbuf", [128, 8], "int32"), "pf": ("sbuf", [128, 16], "float32"),
+    "jc": ("sbuf", [128, 128], "float32"), "jr": ("sbuf", [128, 128], "float32"), "jd": ("sbuf", [128, 136], "float32"),
+    "ident": ("sbuf", [128, 128], "float32"), "mask": ("sbuf", [128, 128], "float32"),
+    "b8": ("sbuf", [128, 8], "float32"), "g8": ("sbuf", [128, 8], "bfloat16"), "h8": ("sbuf", [128, 8], H),
+    "dmat": ("sbuf", [128, 136], H), "t1": ("sbuf", [128, 136], "float32"), "t2": ("sbuf", [128, 136], "float32"),
+    "rb": ("sbuf", [128, 136], "float32"),
+    "r1": ("sbuf", [128, DW], "float32"), "r2": ("sbuf", [128, DW], H),
+    "d1": ("sbuf", [128, 2 * DW], "bfloat16"), "dsc": ("sbuf", [128, 2 * DW], "bfloat16"),
+    "sti": ("sbuf", [128, 24], "int32"), "stu": ("sbuf", [128, 24], "uint16"), "endu": ("sbuf", [128, 2], "uint16"),
+    "dump": ("sbuf", [128, 16], "float32"), "dt1": ("sbuf", [128, 16], "float32"), "dt2": ("sbuf", [128, 16], "float32"),
+    "dt3": ("sbuf", [128, 16], "float32"),
+    "offc": ("sbuf", [128, 16], "uint16"), "mr": ("sbuf", [128, NL], "bfloat16"),
+    "yts": ("sbuf", [8, NL], "float32"), "yss": ("sbuf", [128, 2], "float32"), "part": ("sbuf", [128, 4], "float32"),
+    "yq": ("psum", [128, 512], "float32"),
+}
+for _k in range(2):
+    SCRATCH["x%d" % _k] = ("sbuf", [128, 16 * NL], "bfloat16")
+    SCRATCH["y%d" % _k] = ("sbuf", [128, 16 * NL], "bfloat16")
+    SCRATCH["pu%d" % _k] = ("sbuf", [128, NL], "uint16")
+    SCRATCH["pw%d" % _k] = ("sbuf", [128, NL], H)
+    SCRATCH["li%d" % _k] = ("sbuf", [128, 16], "uint16")
+    SCRATCH["sg%d" % _k] = ("sbuf", [128, 2 * DW], "bfloat16")
+    SCRATCH["mm%d" % _k] = ("sbuf", [128, 144], "float32")
+    SCRATCH["ll%d" % _k] = ("sbuf", [128, 136], "float32")
+    SCRATCH["ss%d" % _k] = ("sbuf", [128, 136], "float32")
+    SCRATCH["ee%d" % _k] = ("sbuf", [128, 128], H)
+    SCRATCH["bc%d" % _k] = ("sbuf", [128, 128], "float32")
+    for _n in ("kd", "lp", "dd"):
+        SCRATCH["%s%d" % (_n, _k)] = ("psum", [128, 512], "float32")
+for _k in range(RO):
+    SCRATCH["m%d" % _k] = ("sbuf", [128, NL], "bfloat16")
+    SCRATCH["offa%d" % _k] = ("sbuf", [128, 16], "uint16")
+    SCRATCH["inm%d" % _k] = ("sbuf", [128, NL], "bfloat16")
+    SCRATCH["ino%d" % _k] = ("sbuf", [128, 16], "uint16")
+
+SEMAPHORES = (["v", "a", "t", "p", "loc"] + ["ld%d" % k for k in range(5)] + ["st%d" % k for k in range(3)]
+              + ["in%d_%d" % (t, k) for t in range(RO) for k in range(len(SENDS) + 1)])
+PSUM = ("yq", "kd0", "kd1", "lp0", "lp1", "dd0", "dd1")
+BIG = 1 << 20
+A = AluOpType
+F = ActivationFunctionType
+
+
+def rank_program(g, core, T, topo):
+    rank = T.rank_of(core)
+    if rank is None:
+        return
+    Q = {"v": g.vector, "a": g.scalar, "t": g.tensor, "p": g, "s": g.sync}
+    V, S, PE = g.vector, g.scalar, g.tensor
+    done = []
+    count = {}
+    waited = {k: {} for k in Q}
+
+    def spans(xs):
+        return [(x, 0, BIG) if isinstance(x, str) else x for x in xs]
+
+    def meet(xs, ys):
+        return any(a[0] == b[0] and a[1] < b[2] and b[1] < a[2] for a in xs for b in ys)
+
+    def op(q, call, r=(), w=(), sem=None, n=1):
+        r, w = spans(r), spans(w)
+        banks = [(x[0], 0, BIG) for x in r + w if x[0] in PSUM]
+        need = {}
+        for (q0, s0, c0, r0, w0) in done:
+            dep = meet(r, w0) or meet(w, w0) or meet(w, r0)
+            if q0 == q and s0 == q:
+                dep = dep and q != "t"
+            else:
+                dep = dep or meet(banks, r0 + w0)
+            if dep:
+                need[s0] = max(need.get(s0, 0), c0)
+        for s0, c0 in need.items():
+            if waited[q].get(s0, 0) < c0:
+                Q[q].wait_ge(T.sem[s0], c0)
+                waited[q][s0] = c0
+        sem = sem or q
+        count[sem] = count.get(sem, 0) + n
+        ins = call()
+        if ins is not None:
+            ins.then_inc(T.sem[sem], n)
+        done.append((q, sem, count[sem], r, w))
+
+    def ts(out, in0, s1, o0, s2=None, o1=None):
+        if o1 is None:
+            return V.tensor_scalar(out, in0, s1, None, o0)
+        return V.tensor_scalar(out, in0, s1, s2, o0, o1)
+
+    op("a", lambda: S.dma_start(T.qi[:], T.q[:]), w=["qi"], sem="ld0", n=16)
+    op("s", lambda: g.sync.dma_start(T.tpt[:], T.tp[:]), w=["tpt"], sem="ld1", n=16)
+    op("s", lambda: g.sync.dma_start(T.domt[:, 0:NV], T.dom[:]), w=[("domt", 0, NV)], sem="ld2", n=16)
+    op("s", lambda: g.sync.dma_start(T.valt[:, 0:NV], T.val[:]), w=[("valt", 0, NV)], sem="ld4", n=16)
+    op("s", lambda: g.sync.dma_start(T.oct[:], T.oc[:]), w=["oct"], sem="ld3", n=16)
+
+    fl = {"allow_small_or_imprecise_dtypes": True}
+    op("p", lambda: g.iota(T.pi[:, 0:1], [[0, 1]], 0, 1), w=[("pi", 0, 1)])
+    op("p", lambda: g.iota(T.sti[:, 0:16], [[1, 16]], 0, 0), w=[("sti", 0, 16)])
+    op("p", lambda: g.iota(T.sti[:, 16:24], [[17, 8]], 16, 0), w=[("sti", 16, 24)])
+    op("p", lambda: g.iota(T.jr[:], [[0, 8], [1, 16]], 0, 0, **fl), w=["jr"])
+    op("p", lambda: g.iota(T.jc[:], [[1, 128]], 0, 0, **fl), w=["jc"])
+    op("p", lambda: g.iota(T.jd[:], [[16, 8], [1, 17]], 0, 0, **fl), w=["jd"])
+    op("p", lambda: g.iota(T.dump[:], [[0, 4], [16, 4]], NV - int(MID), 1, **fl), w=["dump"])
+    op("v", lambda: V.memset(T.zmin[:], 0.0), w=["zmin"])
+    op("v", lambda: V.memset(T.d1[:, 0:DW], 0.0), w=["d1"])
+    op("v", lambda: V.memset(T.rb[:], 0.0), w=["rb"])
+    op("v", lambda: V.memset(T.domt[:, NV:W], 0.0), w=[("domt", NV, W)])
+    op("v", lambda: V.memset(T.valt[:, NV:W], 0.0), w=[("valt", NV, W)])
+    op("v", lambda: V.memset(T.zmin[:, 0:MW:16], 255.0), w=["zmin"])
+    op("v", lambda: ts(T.pi[:, 1:2], T.pi[:, 0:1], 15, A.bitwise_and), r=[("pi", 0, 1)], w=[("pi", 1, 2)])
+    op("v", lambda: ts(T.pi[:, 2:3], T.pi[:, 0:1], 4, A.arith_shift_right), r=[("pi", 0, 1)], w=[("pi", 2, 3)])
+    op("v", lambda: ts(T.pi[:, 3:4], T.pi[:, 0:1], 3, A.bitwise_and), r=[("pi", 0, 1)], w=[("pi", 3, 4)])
+    op("v", lambda: ts(T.pi[:, 4:5], T.pi[:, 0:1], 15, A.bitwise_and, 2, A.arith_shift_right), r=[("pi", 0, 1)], w=[("pi", 4, 5)])
+    op("v", lambda: V.tensor_copy(T.stu[:], T.sti[:]), r=["sti"], w=["stu"])
+    op("v", lambda: V.tensor_copy(T.pf[:, 0:5], T.pi[:, 0:5]), r=["pi"], w=[("pf", 0, 5)])
+    for h in range(2):
+        op("v", lambda: V.memset(T["ss%d" % h][:], 0.0), w=["ss%d" % h])
+        op("v", lambda: V.memset(T["mm%d" % h][:, 0:1], -1.0), w=["mm%d" % h])
+        op("v", lambda: V.memset(T["kd%d" % h][:, 16:136:17], -1.0), w=["kd%d" % h])
+    op("v", lambda: V.memset(T.rb[:, 16:136:17], -10000.0), w=["rb"])
+    pc = [("pf", 0, 5)]
+    op("v", lambda: ts(T.mask[:], T.jr[:], T.pf[:, 1:2], A.is_equal), r=["jr"] + pc, w=["mask"])
+    op("v", lambda: ts(T.ident[:], T.jc[:], T.pf[:, 0:1], A.is_equal), r=["jc"] + pc, w=["ident"])
+    for nm in ("b8", "g8", "h8"):
+        op("v", lambda: ts(T[nm][:], T.jc[:, 0:8], T.pf[:, 2:3], A.is_equal), r=["jc"] + pc, w=[nm])
+    segs = []
+    for b in range(8):
+        segs.append((segs[-1][1] if segs else 0, (segs[-1][1] if segs else 0) + 64 - 16 * (b % 4)))
+    for b, (lo, hi) in enumerate(segs):
+        op("a", lambda: S.activation(T.r1[:, lo:hi], T.ident[:, 16 * b:16 * b + hi - lo], F.Copy), r=["ident"], w=[("r1", lo, hi)])
+    for b, (lo, hi) in enumerate(segs):
+        op("a", lambda: S.activation(T.d1[:, lo:lo + 16], T.mask[:, 0:16], F.Copy), r=["mask"], w=[("d1", lo, lo + 16)])
+    op("v", lambda: V.tensor_copy(T.li0[:], T.qi[:]), r=["qi"], w=["li0"])
+    op("v", lambda: ts(T.qf[:], T.qi[:], -MID, A.add), r=["qi"], w=["qf"])
+    for b, (lo, hi) in enumerate(segs):
+        op("v", lambda: ts(T.r2[:, lo:hi], T.jc[:, 0:hi - lo], 0.0, A.mult, T.b8[:, b:b + 1], A.subtract),
+           r=["jc", "b8"], w=[("r2", lo, hi)])
+    for h in range(2):
+        op("v", lambda: V.tensor_tensor(T["ee%d" % h][:], T.qf[:, 0:16].indirect(T.stu[:, 8 * h:8 * h + 8]), T.mask[:], A.mult),
+           r=["qf", "stu", "mask"], w=["ee%d" % h])
+        op("t", lambda: PE.matmul(T.yq[:, 8 * h:8 * h + 8], T["ee%d" % h][:], T.h8[:], True, True), r=["ee%d" % h, "h8"], w=["yq"])
+    op("v", lambda: ts(T.t2[:], T.jd[:], T.pf[:, 0:1], A.is_equal), r=["jd"] + pc, w=["t2"])
+    op("v", lambda: ts(T.t1[:], T.jd[:], -1.0, A.add, T.pf[:, 0:1], A.is_equal), r=["jd"] + pc, w=["t1"])
+    for h in range(2):
+        op("v", lambda: V.tensor_copy(T["ss%d" % h][:, 16:136:17], T.yq[:, 8 * h:8 * h + 8]), r=["yq"], w=["ss%d" % h])
+    op("v", lambda: V.memset(T.t2[:, 16:136:17], 0.0), w=["t2"])
+    op("a", lambda: S.activation(T.d1[:, DW:2 * DW], T.d1[:, 0:DW], F.Copy), r=[("d1", 0, DW)], w=[("d1", DW, 2 * DW)])
+
+    def consts2():
+        op("v", lambda: ts(T.pf[:, 8:9], T.pf[:, 3:4], -8.0, A.mult, 56.0, A.add), r=pc, w=[("pf", 8, 9)])
+        op("v", lambda: ts(T.pf[:, 9:10], T.pf[:, 4:5], 160.0, A.mult, 63.0, A.add), r=pc, w=[("pf", 9, 10)])
+        op("v", lambda: ts(T.pf[:, 10:11], T.pf[:, 2:3], -16.0, A.mult), r=pc, w=[("pf", 10, 11)])
+        op("v", lambda: V.tensor_tensor(T.dmat[:], T.t1[:], T.t2[:], A.subtract), r=["t1", "t2"], w=["dmat"])
+        op("v", lambda: ts(T.endu[:, 0:1], T.pf[:, 8:9], T.pf[:, 3:4], A.mult, T.pf[:, 9:10], A.add), r=["pf"], w=["endu"])
+        op("v", lambda: ts(T.dump[:], T.dump[:], T.pf[:, 10:11], A.add), r=["dump", "pf"], w=["dump"])
+        op("a", lambda: S.activation(T.zmax[:], T.zmin[:], F.Identity, bias=255.0, scale=-1.0), r=["zmin"], w=["zmax"])
+
+    def PG(s, lo, hi):
+        k = s % 2
+        tab = "oct" if k else "tpt"
+        op("v", lambda: V.tensor_copy(T["pu%d" % k][:, lo:hi], T[tab][:, 0:NV].indirect(T["li%d" % k][:, lo // 16:hi // 16])),
+           r=[tab, ("li%d" % k, lo // 16, hi // 16)], w=[("pu%d" % k, lo, hi)])
+
+    def PF(s, lo, hi):
+        k = s % 2
+        op("v", lambda: ts(T["pw%d" % k][:, lo:hi], T["pu%d" % k][:, lo:hi], -MID, A.add), r=[("pu%d" % k, lo, hi)], w=[("pw%d" % k, lo, hi)])
+
+    def DM(s, h):
+        k = s % 2
+        op("t", lambda: PE.matmul(T["kd%d" % h][:, 256:392], T["pw%d" % k][:, 128 * h:128 * h + 128], T.dmat[:], True, True),
+           r=[("pw%d" % k, 128 * h, 128 * h + 128), "dmat"], w=[("kd%d" % h, 256, 392)])
+
+    def G(s, j):
+        k = s % 2
+        lo, hi = CUT[k][j:j + 2]
+        tab = "valt" if k else "domt"
+        src = T[tab][:, 0:W].indirect(T["pu%d" % k][:, lo:hi])
+        out = T["x%d" % k][:, 16 * lo:16 * hi]
+        op("a" if j else "v", (lambda: S.activation(out, src, F.Copy)) if j else (lambda: V.tensor_copy(out, src)),
+           r=[tab, ("pu%d" % k, lo, hi)], w=[("x%d" % k, lo, hi)])
+
+    def SC(s, j):
+        k = s % 2
+        lo, hi = CUT[k][j:j + 2]
+        z = "zmax" if k else "zmin"
+        op("v", lambda: V.tensor_tensor_scan(T["y%d" % k][:, 16 * lo:16 * hi], T[z][:, 0:16 * (hi - lo)], T["x%d" % k][:, 16 * lo:16 * hi],
+                                             0.0, A.min if k else A.max, A.max if k else A.min),
+           r=[z, ("x%d" % k, lo, hi)], w=[("y%d" % k, lo, hi)])
+
+    def KEY(s, h):
+        k = s % 2
+        for i in range(16):
+            op("t", lambda: PE.matmul(T["kd%d" % h][:, i:136:17], T["x%d" % k][:, 2048 * h + i:2048 * h + 2048:16], T.g8[:], True, True),
+               r=[("x%d" % k, 128 * h, 128 * h + 128), "g8"], w=[("kd%d" % h, 0, 136)])
+
+    def A1(h):
+        op("v", lambda: V.tensor_tensor_scan(T["mm%d" % h][:, 1:137], T.rb[:], T["kd%d" % h][:, 0:136], -1.0, A.add, A.max),
+           r=["rb", ("kd%d" % h, 0, 136)], w=["mm%d" % h])
+
+    def A2(h):
+        op("v", lambda: V.tensor_tensor(T["ll%d" % h][:], T["kd%d" % h][:, 0:136], T["mm%d" % h][:, 0:136], A.is_le),
+           r=[("kd%d" % h, 0, 136), "mm%d" % h], w=["ll%d" % h])
+
+    def A3(h):
+        op("v", lambda: V.tensor_tensor_scan(T["ss%d" % h][:], T["kd%d" % h][:, 256:392], T["ll%d" % h][:], 0.0, A.add, A.mult),
+           r=[("kd%d" % h, 256, 392), "ll%d" % h], w=["ss%d" % h])
+
+    def E(s, h):
+        k = s % 2
+        op("v", lambda: V.tensor_tensor(T["ee%d" % h][:], T["ss%d" % h][:, 0:136].indirect(T.stu[:, 16:24]), T.mask[:], A.mult),
+           r=["ss%d" % h, "stu", "mask"], w=["ee%d" % h])
+        op("t", lambda: PE.matmul(T["lp%d" % k][:, 8 * h:8 * h + 8], T["ee%d" % h][:], T.h8[:], True, True),
+           r=["ee%d" % h, "h8"], w=[("lp%d" % k, 8 * h, 8 * h + 8)])
+
+    def U(s, h):
+        k = s % 2
+        op("v", lambda: ts(T["li%d" % k][:, 8 * h:8 * h + 8], T["lp%d" % k][:, 8 * h:8 * h + 8], MID, A.add),
+           r=[("lp%d" % k, 8 * h, 8 * h + 8)], w=[("li%d" % k, 8 * h, 8 * h + 8)])
+
+    def BC(h):
+        op("a", lambda: S.activation(T["bc%d" % h][:], T["ss%d" % h][:, 0:136].indirect(T.stu[:, 16:24]), F.Copy),
+           r=["ss%d" % h, "stu"], w=["bc%d" % h])
+
+    def BP(h):
+        op("t", lambda: PE.matmul(T["dd%d" % h][:, 0:DW], T["ee%d" % h][:], T.r2[:], True, False), r=["ee%d" % h, "r2"], w=["dd%d" % h])
+        op("t", lambda: PE.matmul(T["dd%d" % h][:, 0:DW], T["bc%d" % h][:], T.r1[:], False, True), r=["bc%d" % h, "r1"], w=["dd%d" % h])
+
+    def SG(s, h):
+        k = s % 2
+        op("a", lambda: S.activation(T["sg%d" % k][:, DW * h:DW * h + DW], T["dd%d" % h][:, 0:DW], F.Sign),
+           r=["dd%d" % h], w=[("sg%d" % k, DW * h, DW * h + DW)])
+
+    def off(s):
+        return "offa%d" % (s // 2) if s % 2 else "offc"
+
+    def DS(s, j):
+        k = s % 2
+        if j == 0:
+            op("v", lambda: V.tensor_tensor_scan(T.dsc[:], T["sg%d" % k][:], T.d1[:], 1.0, A.mult, A.add), r=["sg%d" % k, "d1"], w=["dsc"])
+        elif j == 1:
+            op("v", lambda: ts(T.dt1[:], T.dsc[:, 0:2 * DW].indirect(T.endu[:, 0:1]), 0.0, A.is_equal, 4096.0, A.mult),
+               r=["dsc", "endu"], w=["dt1"])
+        elif j == 2:
+            op("v", lambda: V.tensor_tensor(T.dt2[:], T["lp%d" % k][:, 0:16], T.dt1[:], A.add), r=["dt1", "lp%d" % k], w=["dt2"])
+        elif j == 3:
+            op("v", lambda: V.tensor_tensor(T.dt3[:], T.dt2[:], T.dump[:], A.min), r=["dt2", "dump"], w=["dt3"])
+        else:
+            op("v", lambda: ts(T[off(s)][:], T.dt3[:], MID, A.add), r=["dt3"], w=[off(s)])
+
+    def SW(b):
+        op("v", lambda: V.tensor_copy(T.valt[:, 0:W].indirect(T.offc[:, 4 * b:4 * b + 4]), T.y0[:, 1024 * b + 15:1024 * b + 1024:16]),
+           r=["offc", ("y0", 64 * b, 64 * b + 64)], w=["valt"])
+
+    def GM(t, j):
+        lo, hi = SENDS[j]
+        op("v", lambda: V.tensor_tensor(T["m%d" % t][:, lo:hi], T.domt[:, 0:W].indirect(T.li1[:, lo // 16:hi // 16]),
+                                        T.y1[:, 16 * lo + 15:16 * hi:16], A.min),
+           r=["domt", ("li1", lo // 16, hi // 16), ("y1", lo, hi)], w=[("m%d" % t, lo, hi)])
+
+    def SD(offs, src, b):
+        op("v", lambda: V.tensor_copy(T.domt[:, 0:W].indirect(T[offs][:, 4 * b:4 * b + 4]), T[src][:, 64 * b:64 * b + 64]),
+           r=[offs, (src, 64 * b, 64 * b + 64)], w=["domt"])
+
+    def SEND(t, j):
+        dst = T.cores[(rank + 1 + t % (N - 1)) % N]
+        rid, pid, _ = topo.addr(dst)
+        src, land = ("offa%d" % t, "ino%d" % t) if j == 0 else ("m%d" % t, "inm%d" % t)
+        lo, hi = (0, 16) if j == 0 else SENDS[j - 1]
+        sem = "in%d_%d" % (t, j)
+
+        def call():
+            g.remote_dma(T[land][:, lo:hi], T[src][:, lo:hi], T.sem[sem], T.sem.loc, pid, rid, topo.mask(core, dst))
+        op("p", call, r=[(src, lo, hi)], sem="loc", n=len(topo.engines(core, dst)))
+        count[sem] = len(topo.engines(T.cores[(rank - 1 - t % (N - 1)) % N], core))
+        done.append(("far", sem, count[sem], [], [(land, lo, hi)]))
+
+    def RG(t, j, o=A.min):
+        lo, hi = SENDS[j]
+        op("v", lambda: V.tensor_tensor(T.mr[:, lo:hi], T.domt[:, 0:W].indirect(T["ino%d" % t][:, lo // 16:hi // 16]),
+                                        T["inm%d" % t][:, lo:hi], o),
+           r=["domt", "ino%d" % t, ("inm%d" % t, lo, hi)], w=[("mr", lo, hi)])
+
+    HF = 1536
+
+    def END(n, t):
+        if n == "YV":
+            op("s", lambda: g.sync.dma_start(T.yv[:], T["m%d" % t][:]), r=["m%d" % t], sem="st0", n=16)
+        elif n == "SV":
+            op("a", lambda: S.activation(T.x0[:, 0:NV], T.valt[:, 0:NV], F.Copy, accum_out=T.yss[:, 1:2]),
+               r=["valt"], w=["x0", ("yss", 1, 2)])
+        elif n == "Z0":
+            op("v", lambda: V.memset(T.domt[:, NV:W], 0.0), w=[("domt", NV, W)])
+        elif n == "SA":
+            op("a", lambda: S.activation(T.x0[:, 0:HF], T.domt[:, 0:HF], F.Copy, accum_out=T.part[:, 0:1]),
+               r=[("domt", 0, HF)], w=["x0", ("part", 0, 1)])
+        elif n == "SB":
+            op("v", lambda: V.tensor_reduce(T.part[:, 1:2], T.domt[:, HF:NV], AxisListType.X, A.add), r=[("domt", HF, NV)], w=[("part", 1, 2)])
+        elif n == "YT":
+            for h in range(2):
+                op("t", lambda: PE.matmul(T.yq[0:8, 128 * h:128 * h + 128], T["ss%d" % h][:, 16:136:17], T.ident[:], True, True),
+                   r=["ss%d" % h, "ident"], w=["yq"])
+        elif n == "RL":
+            RG(t, 2, A.subtract)
+        elif n == "Z1":
+            op("v", lambda: ts(T.dsc[:, 0:64], T.mr[:, 192:256], 0.0, A.max, -1.0, A.mult), r=[("mr", 192, 256)], w=["dsc"])
+        elif n == "Z2":
+            op("v", lambda: V.tensor_reduce(T.part[:, 2:3], T.dsc[:, 0:64], AxisListType.X, A.add), r=["dsc"], w=[("part", 2, 3)])
+        elif n == "Z3":
+            op("v", lambda: V.tensor_reduce(T.yss[:, 0:1], T.part[:, 0:3], AxisListType.X, A.add), r=["part"], w=[("yss", 0, 1)])
+            op("s", lambda: g.sync.dma_start(T.ys[:], T.yss[:]), r=["yss"], sem="st2", n=16)
+        else:
+            op("a", lambda: S.activation(T.yts[:], T.yq[0:8, 0:NL], F.Identity, bias=MID), r=["yq"], w=["yts"])
+            op("a", lambda: S.dma_start(T.yt[:], T.yts[:]), r=["yts"], sem="st1", n=16)
+
+    def part(n, t):
+        first, last = t == 0, t == RO - 1
+        name = n.rstrip("0123456789")
+        d = [int(c) for c in n[len(name):]]
+        s = 2 * t + d[0] if d else None
+        if n in ("YV", "SV", "Z0", "SA", "SB", "YT", "RL", "Z1", "Z2", "Z3", "YU"):
+            if last:
+                END(n, t)
+        elif name in ("E", "U", "B", "Q", "SG", "P", "F", "M") and d[0] == 2 and last or n in ("R2", "I3") and last:
+            pass
+        elif name in ("Pn", "Fn", "SGo") and first or name in ("Pf", "Ff") and not first:
+            pass
+        elif name == "SGo":
+            SG(2 * t, d[0])
+        elif name in ("G", "S", "K", "D", "E", "U", "SG", "M"):
+            {"G": G, "S": SC, "K": KEY, "D": DS, "E": E, "U": U, "SG": SG, "M": DM}[name](s, d[1])
+        elif name in ("Aa", "Ab", "Ac", "B", "Q"):
+            {"Aa": A1, "Ab": A2, "Ac": A3, "B": BC, "Q": BP}[name](d[1])
+        elif name[0] in "PF":
+            lo, hi = (128 * d[1], 128 * d[1] + 128) if len(d) > 1 else (0, NL)
+            (PG if name[0] == "P" else PF)(s, lo, hi)
+        elif name == "W":
+            SW(d[0])
+        elif name == "O":
+            SD("offa%d" % t, "m%d" % t, d[0])
+        elif name == "I":
+            SD("ino%d" % t, "mr", d[0])
+        else:
+            {"N": GM, "T": SEND, "R": RG}[name](t, d[0])
+
+    E(0, 0); BC(0); BP(0); E(0, 1); BC(1); BP(1)
+    PG(0, 0, NL)
+    consts2()
+    SG(0, 0); SG(0, 1)
+    PF(0, 0, NL); DM(0, 0); DM(0, 1)
+    for t in range(RO):
+        for n in ORDER:
+            part(n, t)
+    for sem, c in count.items():
+        g.wait_ge(T.sem[sem], c)

@@ -1,63 +1,75 @@
 from concourse.mybir import AluOpType, AxisListType, ActivationFunctionType
 
 NV, NL, RO, N = 2560, 256, 4, 4
-W = NV + 64
+DC = 64
+W = DC + NV
 DW = 320
 MID = 1280.0
+FAR = 4096.0
 H = "float16"
-CUT = ((0, 52, 128, 192, 240, 256), (0, 28, 76, 128, 128, 192, 240, 256))
-SENDS = ((0, 64), (64, 192), (192, 256))
-MW = 16 * max(b - a for c in CUT for a, b in zip(c[:-1], c[1:]))
+CUT = ((0, 64, 128, 192, 240, 256), (0, 40, 84, 128, 192, 240, 256))
+ONV = ((0,), (0,))
+SCUT = CUT
+SENDS = ((0, 64), (64, 128), (128, 192), (192, 256))
+BLK = ((0, 64), (64, 128), (128, 192), (192, 256))
+SUMS = (768, 1536)
+SO = 17 * 32
+WBLK = BLK
+ENG = {"U": "aaaa", "J": "a", "P": "a", "F": "aavv", "B": "a"}
 ORDER = """
-SGo1 G01 D00 G00 D01 G02 S00 S01 K00 D02 Aa00 D03 Ab00 D04 Ac00 B10 G03 W1 E10 G04 Q10 S02 W0 U10 W2 Pn10 S03 S04 K01 W3
-SG10 Aa01 Fn10 Ab01 Pf10 Ac01 G10 E11 G11 S10 B11 S11 U11 Q11 G12 SG11 N0 Ff10 P11 S12 D10 K10 M10 Aa10 D11 D12 Ab10 G14
-D13 Ac10 D14 G15 E20 G16 O0 S14 F11 SV N1 B20 U20 T1 O1 S15 O2 S16 N2 M11 K11 O3 YV T0 T2 Aa11 Ab11 R0 Q20 Ac11 I0 E21 R1
-U21 I2 T3 P2 I1 YT YU SG20 B21 F2 Z0 SB SA R2 Q21 RL Z1 M20 Z2 Z3 I3 M21
+B01 U01 P01 F01 G01 G00 M01 Q01 K00 S00 S01 Aa00 C01 D00 Ab00 G03 D01 Ac00 W0 S03 W1 G02 S02 E10 B10 Q10 G04 K01 U10 C10 P10 S04 W2 W3
+Aa01 Ab01 Ac01 D12 G11 E11 B11 G12 U11 Q11 P11 C11 G13 G14 G15 G10 D13 S11 F10 S10 S12 N0 N1 M10 K10 D14 O0 Aa10 O1 Ab10 D15 Ac10 S13
+N2 F11 O2 SV M11 E20 K11 J0 S14 T8 T1 T2 T9 T3 S15 Z0 R1 R0 N3 T4 I1 Aa11 Ab11 I0 Ac11 H0 O3 R2 I2 SW YT YU SP B20 SA SQ U20 Q20 SG YV
+R3 I3 SB SR P20 F20 RL E21 C20 SX Z3 M20
 """.split()
+FINAL = []
+FIRST = "E20 E21 B20 B21 Q20 Q21 U20 U21 P20 P21 F20 F21 M20 M21 C20 C21 D20 D21 D22 D23 D24 D25".split()
+ENDS = ("YV", "SV", "SW", "SX", "Z0", "SA", "SB", "SP", "SQ", "SR", "SG", "YT", "RL", "Z3", "YU")
+TAG = [[""]]
 
 SCRATCH = {
     "domt": ("sbuf", [128, W], "bfloat16"), "valt": ("sbuf", [128, W], "bfloat16"),
-    "tpt": ("sbuf", [128, NV], "int32"), "oct": ("sbuf", [128, NV], "int32"),
+    "tpt": ("sbuf", [128, W], "int32"), "oct": ("sbuf", [128, W], "int32"),
     "qi": ("sbuf", [128, 16], "int32"), "qf": ("sbuf", [128, 16], "float32"),
-    "zmin": ("sbuf", [128, MW], "bfloat16"), "zmax": ("sbuf", [128, MW], "bfloat16"),
+    "zmin": ("sbuf", [128, 2048], "bfloat16"), "zmax": ("sbuf", [128, 2048], "bfloat16"),
     "pi": ("sbuf", [128, 8], "int32"), "pf": ("sbuf", [128, 16], "float32"),
     "jc": ("sbuf", [128, 128], "float32"), "jr": ("sbuf", [128, 128], "float32"), "jd": ("sbuf", [128, 136], "float32"),
-    "ident": ("sbuf", [128, 128], "float32"), "mask": ("sbuf", [128, 128], "float32"),
+    "ident": ("sbuf", [128, 128], "float32"), "identb": ("sbuf", [128, 128], "bfloat16"), "mask": ("sbuf", [128, 128], "float32"),
+    "ones": ("sbuf", [128, 2], "float32"), "sb": ("sbuf", [128, 128], "float32"),
     "b8": ("sbuf", [128, 8], "float32"), "g8": ("sbuf", [128, 8], "bfloat16"), "h8": ("sbuf", [128, 8], H),
-    "dmat": ("sbuf", [128, 136], H), "t1": ("sbuf", [128, 136], "float32"), "t2": ("sbuf", [128, 136], "float32"),
+    "dmat": ("sbuf", [128, 136], H), "t1": ("sbuf", [128, 144], "float32"),
     "rb": ("sbuf", [128, 136], "float32"),
-    "r1": ("sbuf", [128, DW], "float32"), "r2": ("sbuf", [128, DW], H),
-    "d1": ("sbuf", [128, 2 * DW], "bfloat16"), "dsc": ("sbuf", [128, 2 * DW], "bfloat16"),
+    "r2": ("sbuf", [128, DW], H), "identh": ("sbuf", [128, 128], H), "gs": ("sbuf", [128, 128], H),
+    "jg": ("sbuf", [128, 128], "float32"), "nid": ("sbuf", [128, 8], "float32"),
+    "zd": ("sbuf", [128, 2 * DW], "bfloat16"), "dsc": ("sbuf", [128, 2 * DW], "bfloat16"),
     "sti": ("sbuf", [128, 24], "int32"), "stu": ("sbuf", [128, 24], "uint16"), "endu": ("sbuf", [128, 2], "uint16"),
-    "dump": ("sbuf", [128, 16], "float32"), "dt1": ("sbuf", [128, 16], "float32"), "dt2": ("sbuf", [128, 16], "float32"),
-    "dt3": ("sbuf", [128, 16], "float32"),
-    "offc": ("sbuf", [128, 16], "uint16"), "mr": ("sbuf", [128, NL], "bfloat16"),
-    "yts": ("sbuf", [8, NL], "float32"), "yss": ("sbuf", [128, 2], "float32"), "part": ("sbuf", [128, 4], "float32"),
-    "yq": ("psum", [128, 512], "float32"),
+    "offc": ("sbuf", [128, 32], "uint16"), "mr": ("sbuf", [128, NL], "bfloat16"),
+    "da": ("sbuf", [128, 64], "bfloat16"), "mo": ("sbuf", [128, NL], "bfloat16"),
+    "yts": ("sbuf", [8, NL], "float32"), "yss": ("sbuf", [128, 2], "float32"), "fb": ("sbuf", [128, 72], "float32"),
+    "yq": ("psum", [128, 512], "float32"), "sp": ("psum", [128, 512], "float32"),
 }
 for _k in range(2):
     SCRATCH["x%d" % _k] = ("sbuf", [128, 16 * NL], "bfloat16")
     SCRATCH["y%d" % _k] = ("sbuf", [128, 16 * NL], "bfloat16")
     SCRATCH["pu%d" % _k] = ("sbuf", [128, NL], "uint16")
     SCRATCH["pw%d" % _k] = ("sbuf", [128, NL], H)
-    SCRATCH["li%d" % _k] = ("sbuf", [128, 16], "uint16")
+    SCRATCH["li%d" % _k] = ("sbuf", [128, 32], "uint16")
     SCRATCH["sg%d" % _k] = ("sbuf", [128, 2 * DW], "bfloat16")
     SCRATCH["mm%d" % _k] = ("sbuf", [128, 144], "float32")
     SCRATCH["ll%d" % _k] = ("sbuf", [128, 136], "float32")
-    SCRATCH["ss%d" % _k] = ("sbuf", [128, 136], "float32")
-    SCRATCH["ee%d" % _k] = ("sbuf", [128, 128], H)
-    SCRATCH["bc%d" % _k] = ("sbuf", [128, 128], "float32")
+    SCRATCH["ss%d" % _k] = ("sbuf", [128, SO + 136], H)
+    SCRATCH["lt%d" % _k] = ("sbuf", [128, 128], H)
     for _n in ("kd", "lp", "dd"):
         SCRATCH["%s%d" % (_n, _k)] = ("psum", [128, 512], "float32")
 for _k in range(RO):
     SCRATCH["m%d" % _k] = ("sbuf", [128, NL], "bfloat16")
-    SCRATCH["offa%d" % _k] = ("sbuf", [128, 16], "uint16")
+    SCRATCH["offa%d" % _k] = ("sbuf", [128, 32], "uint16")
     SCRATCH["inm%d" % _k] = ("sbuf", [128, NL], "bfloat16")
-    SCRATCH["ino%d" % _k] = ("sbuf", [128, 16], "uint16")
+    SCRATCH["ino%d" % _k] = ("sbuf", [128, 32], "uint16")
 
 SEMAPHORES = (["v", "a", "t", "p", "loc"] + ["ld%d" % k for k in range(5)] + ["st%d" % k for k in range(3)]
-              + ["in%d_%d" % (t, k) for t in range(RO) for k in range(len(SENDS) + 1)])
-PSUM = ("yq", "kd0", "kd1", "lp0", "lp1", "dd0", "dd1")
+              + ["in%d_%d" % (t, k) for t in range(RO) for k in range(10)])
+PSUM = ("yq", "sp", "kd0", "kd1", "lp0", "lp1", "dd0", "dd1")
 BIG = 1 << 20
 A = AluOpType
 F = ActivationFunctionType
@@ -101,89 +113,114 @@ def rank_program(g, core, T, topo):
         if ins is not None:
             ins.then_inc(T.sem[sem], n)
         done.append((q, sem, count[sem], r, w))
+        TAG.append((TAG[0][0], q, r, w))
 
     def ts(out, in0, s1, o0, s2=None, o1=None):
         if o1 is None:
             return V.tensor_scalar(out, in0, s1, None, o0)
         return V.tensor_scalar(out, in0, s1, s2, o0, o1)
 
+    def fill(name, ap, c):
+        op("a", lambda: S.activation(ap, T.jd[:, 0:ap.shape[1]], F.Identity, bias=c, scale=0.0), r=["jd"], w=[name])
+
     op("a", lambda: S.dma_start(T.qi[:], T.q[:]), w=["qi"], sem="ld0", n=16)
-    op("s", lambda: g.sync.dma_start(T.tpt[:], T.tp[:]), w=["tpt"], sem="ld1", n=16)
-    op("s", lambda: g.sync.dma_start(T.domt[:, 0:NV], T.dom[:]), w=[("domt", 0, NV)], sem="ld2", n=16)
-    op("s", lambda: g.sync.dma_start(T.valt[:, 0:NV], T.val[:]), w=[("valt", 0, NV)], sem="ld4", n=16)
-    op("s", lambda: g.sync.dma_start(T.oct[:], T.oc[:]), w=["oct"], sem="ld3", n=16)
+    op("s", lambda: g.sync.dma_start(T.tpt[:, DC:W], T.tp[:]), w=[("tpt", DC, W)], sem="ld1", n=16)
+    op("s", lambda: g.sync.dma_start(T.domt[:, DC:W], T.dom[:]), w=[("domt", DC, W)], sem="ld2", n=16)
+    op("s", lambda: g.sync.dma_start(T.valt[:, DC:W], T.val[:]), w=[("valt", DC, W)], sem="ld4", n=16)
+    op("s", lambda: g.sync.dma_start(T.oct[:, DC:W], T.oc[:]), w=[("oct", DC, W)], sem="ld3", n=16)
 
     fl = {"allow_small_or_imprecise_dtypes": True}
-    op("p", lambda: g.iota(T.pi[:, 0:1], [[0, 1]], 0, 1), w=[("pi", 0, 1)])
-    op("p", lambda: g.iota(T.sti[:, 0:16], [[1, 16]], 0, 0), w=[("sti", 0, 16)])
-    op("p", lambda: g.iota(T.sti[:, 16:24], [[17, 8]], 16, 0), w=[("sti", 16, 24)])
-    op("p", lambda: g.iota(T.jr[:], [[0, 8], [1, 16]], 0, 0, **fl), w=["jr"])
-    op("p", lambda: g.iota(T.jc[:], [[1, 128]], 0, 0, **fl), w=["jc"])
-    op("p", lambda: g.iota(T.jd[:], [[16, 8], [1, 17]], 0, 0, **fl), w=["jd"])
-    op("p", lambda: g.iota(T.dump[:], [[0, 4], [16, 4]], NV - int(MID), 1, **fl), w=["dump"])
-    op("v", lambda: V.memset(T.zmin[:], 0.0), w=["zmin"])
-    op("v", lambda: V.memset(T.d1[:, 0:DW], 0.0), w=["d1"])
-    op("v", lambda: V.memset(T.rb[:], 0.0), w=["rb"])
-    op("v", lambda: V.memset(T.domt[:, NV:W], 0.0), w=[("domt", NV, W)])
-    op("v", lambda: V.memset(T.valt[:, NV:W], 0.0), w=[("valt", NV, W)])
-    op("v", lambda: V.memset(T.zmin[:, 0:MW:16], 255.0), w=["zmin"])
-    op("v", lambda: ts(T.pi[:, 1:2], T.pi[:, 0:1], 15, A.bitwise_and), r=[("pi", 0, 1)], w=[("pi", 1, 2)])
-    op("v", lambda: ts(T.pi[:, 2:3], T.pi[:, 0:1], 4, A.arith_shift_right), r=[("pi", 0, 1)], w=[("pi", 2, 3)])
-    op("v", lambda: ts(T.pi[:, 3:4], T.pi[:, 0:1], 3, A.bitwise_and), r=[("pi", 0, 1)], w=[("pi", 3, 4)])
-    op("v", lambda: ts(T.pi[:, 4:5], T.pi[:, 0:1], 15, A.bitwise_and, 2, A.arith_shift_right), r=[("pi", 0, 1)], w=[("pi", 4, 5)])
-    op("v", lambda: V.tensor_copy(T.stu[:], T.sti[:]), r=["sti"], w=["stu"])
-    op("v", lambda: V.tensor_copy(T.pf[:, 0:5], T.pi[:, 0:5]), r=["pi"], w=[("pf", 0, 5)])
-    for h in range(2):
-        op("v", lambda: V.memset(T["ss%d" % h][:], 0.0), w=["ss%d" % h])
-        op("v", lambda: V.memset(T["mm%d" % h][:, 0:1], -1.0), w=["mm%d" % h])
-        op("v", lambda: V.memset(T["kd%d" % h][:, 16:136:17], -1.0), w=["kd%d" % h])
-    op("v", lambda: V.memset(T.rb[:, 16:136:17], -10000.0), w=["rb"])
-    pc = [("pf", 0, 5)]
-    op("v", lambda: ts(T.mask[:], T.jr[:], T.pf[:, 1:2], A.is_equal), r=["jr"] + pc, w=["mask"])
-    op("v", lambda: ts(T.ident[:], T.jc[:], T.pf[:, 0:1], A.is_equal), r=["jc"] + pc, w=["ident"])
-    for nm in ("b8", "g8", "h8"):
-        op("v", lambda: ts(T[nm][:], T.jc[:, 0:8], T.pf[:, 2:3], A.is_equal), r=["jc"] + pc, w=[nm])
+    zw = 16 * max(b - a for c in SCUT for a, b in zip(c[:-1], c[1:]))
     segs = []
     for b in range(8):
         segs.append((segs[-1][1] if segs else 0, (segs[-1][1] if segs else 0) + 64 - 16 * (b % 4)))
-    for b, (lo, hi) in enumerate(segs):
-        op("a", lambda: S.activation(T.r1[:, lo:hi], T.ident[:, 16 * b:16 * b + hi - lo], F.Copy), r=["ident"], w=[("r1", lo, hi)])
-    for b, (lo, hi) in enumerate(segs):
-        op("a", lambda: S.activation(T.d1[:, lo:lo + 16], T.mask[:, 0:16], F.Copy), r=["mask"], w=[("d1", lo, lo + 16)])
-    op("v", lambda: V.tensor_copy(T.li0[:], T.qi[:]), r=["qi"], w=["li0"])
-    op("v", lambda: ts(T.qf[:], T.qi[:], -MID, A.add), r=["qi"], w=["qf"])
-    for b, (lo, hi) in enumerate(segs):
-        op("v", lambda: ts(T.r2[:, lo:hi], T.jc[:, 0:hi - lo], 0.0, A.mult, T.b8[:, b:b + 1], A.subtract),
-           r=["jc", "b8"], w=[("r2", lo, hi)])
-    for h in range(2):
-        op("v", lambda: V.tensor_tensor(T["ee%d" % h][:], T.qf[:, 0:16].indirect(T.stu[:, 8 * h:8 * h + 8]), T.mask[:], A.mult),
-           r=["qf", "stu", "mask"], w=["ee%d" % h])
-        op("t", lambda: PE.matmul(T.yq[:, 8 * h:8 * h + 8], T["ee%d" % h][:], T.h8[:], True, True), r=["ee%d" % h, "h8"], w=["yq"])
-    op("v", lambda: ts(T.t2[:], T.jd[:], T.pf[:, 0:1], A.is_equal), r=["jd"] + pc, w=["t2"])
-    op("v", lambda: ts(T.t1[:], T.jd[:], -1.0, A.add, T.pf[:, 0:1], A.is_equal), r=["jd"] + pc, w=["t1"])
-    for h in range(2):
-        op("v", lambda: V.tensor_copy(T["ss%d" % h][:, 16:136:17], T.yq[:, 8 * h:8 * h + 8]), r=["yq"], w=["ss%d" % h])
-    op("v", lambda: V.memset(T.t2[:, 16:136:17], 0.0), w=["t2"])
-    op("a", lambda: S.activation(T.d1[:, DW:2 * DW], T.d1[:, 0:DW], F.Copy), r=[("d1", 0, DW)], w=[("d1", DW, 2 * DW)])
+    pc = [("pf", 0, 5)]
+
+    def consts():
+        op("p", lambda: g.iota(T.pi[:, 0:1], [[0, 1]], 0, 1), w=[("pi", 0, 1)])
+        op("p", lambda: g.iota(T.jd[:], [[16, 8], [1, 17]], 0, -1, **fl), w=["jd"])
+        op("p", lambda: g.iota(T.jc[:], [[1, 128]], 0, -1, **fl), w=["jc"])
+        op("p", lambda: g.iota(T.jr[:], [[0, 8], [1, 16]], 0, 0, **fl), w=["jr"])
+        op("p", lambda: g.iota(T.sti[:, 0:16], [[1, 16]], 0, 0), w=[("sti", 0, 16)])
+        op("p", lambda: g.iota(T.jg[:], [[1, 8], [0, 16]], 32, -1, **fl), w=["jg"])
+        op("v", lambda: V.memset(T.zmin[:, 0:zw], 0.0), w=["zmin"])
+        for j, (m, sh) in enumerate(((15, 0), (127, 4), (3, 0), (7, 2))):
+            op("v", lambda: ts(T.pi[:, j + 1:j + 2], T.pi[:, 0:1], m, A.bitwise_and, sh, A.arith_shift_right), r=[("pi", 0, 1)], w=[("pi", j + 1, j + 2)])
+        op("v", lambda: ts(T.ident[:], T.jc[:], 0.0, A.is_equal), r=["jc"], w=["ident"])
+        op("v", lambda: V.tensor_copy(T.pf[:, 0:5], T.pi[:, 0:5]), r=["pi"], w=[("pf", 0, 5)])
+        op("v", lambda: V.memset(T.zd[:, 0:DW], 0.0), w=["zd"])
+        op("v", lambda: V.memset(T.zmin[:, 0:zw:16], 255.0), w=["zmin"])
+        op("v", lambda: ts(T.mask[:], T.jr[:], T.pf[:, 1:2], A.is_equal), r=["jr"] + pc, w=["mask"])
+        op("v", lambda: ts(T.b8[:], T.jr[:, 0:8], T.pf[:, 2:3], A.is_equal), r=["jr"] + pc, w=["b8"])
+        op("v", lambda: ts(T.h8[:], T.jr[:, 0:8], T.pf[:, 2:3], A.is_equal), r=["jr"] + pc, w=["h8"])
+        op("v", lambda: ts(T.nid[:], T.jc[:, 0:8], 0.0, A.is_equal, -1.0, A.mult), r=["jc"], w=["nid"])
+        op("v", lambda: V.tensor_copy(T.stu[:, 0:16], T.sti[:, 0:16]), r=["sti"], w=[("stu", 0, 16)])
+        op("v", lambda: ts(T.gs[:], T.jg[:], 0.0, A.is_equal), r=["jg"], w=["gs"])
+        for h in range(2):
+            fill("ss%d" % h, T["ss%d" % h][:, 16:SO:17], 0.0)
+        op("a", lambda: S.activation(T.identh[:], T.ident[:], F.Copy), r=["ident"], w=["identh"])
+        for b, (lo, hi) in enumerate(segs):
+            op("a", lambda: S.activation(T.r2[:, lo:hi], T.jc[:, 0:hi - lo], F.Identity, bias=T.nid[:, b:b + 1], scale=0.0),
+               r=["jc", "nid"], w=[("r2", lo, hi)])
+        for k in range(2):
+            op("v", lambda: V.memset(T["li%d" % k][:], 0), w=["li%d" % k])
+        for h in range(2):
+            op("v", lambda: ts(T.li0[:, 16 * h:16 * h + 8], T.qi[:, 8 * h:8 * h + 8], float(DC), A.add), r=["qi"], w=[("li0", 16 * h, 16 * h + 8)])
+        op("v", lambda: ts(T.qf[:], T.qi[:], -MID, A.add), r=["qi"], w=["qf"])
+        for h in range(2):
+            op("v", lambda: V.tensor_tensor(T.pw1[:, 128 * h:128 * h + 128], T.qf[:, 0:16].indirect(T.stu[:, 8 * h:8 * h + 8]), T.mask[:], A.mult),
+               r=["qf", ("stu", 0, 16), "mask"], w=[("pw1", 128 * h, 128 * h + 128)])
+            op("t", lambda: PE.matmul(T.yq[:, 8 * h:8 * h + 8], T.pw1[:, 128 * h:128 * h + 128], T.h8[:], True, True),
+               r=[("pw1", 128 * h, 128 * h + 128), "h8"], w=["yq"])
+        op("v", lambda: ts(T.t1[:, 1:137], T.jd[:], 0.0, A.is_equal), r=["jd"], w=["t1"])
+        for h in range(2):
+            op("v", lambda: V.tensor_copy(T["ss%d" % h][:, SO + 16:SO + 136:17], T.yq[:, 8 * h:8 * h + 8]), r=["yq"], w=["ss%d" % h])
+        op("v", lambda: V.memset(T.t1[:, 0:137:17], 0.0), w=["t1"])
+        for b, (lo, hi) in enumerate(segs):
+            op("a", lambda: S.activation(T.zd[:, lo:lo + 16], T.mask[:, 0:16], F.Copy, scale=FAR), r=["mask"], w=[("zd", lo, lo + 16)])
+        op("a", lambda: S.activation(T.g8[:], T.b8[:], F.Copy), r=["b8"], w=["g8"])
 
     def consts2():
+        op("v", lambda: V.tensor_tensor(T.dmat[:], T.t1[:, 0:136], T.t1[:, 1:137], A.subtract), r=["t1"], w=["dmat"])
+        for c in range(4):
+            e = segs[c][1] - 1
+            op("v", lambda: ts(T.zd[:, e:DW:160], T.zd[:, e:DW:160], T.pf[:, 1:2], A.max, 16.0 * c, A.add), r=[("zd", e, e + 161)] + pc, w=[("zd", e, e + 1), ("zd", e + 160, e + 161)])
         op("v", lambda: ts(T.pf[:, 8:9], T.pf[:, 3:4], -8.0, A.mult, 56.0, A.add), r=pc, w=[("pf", 8, 9)])
         op("v", lambda: ts(T.pf[:, 9:10], T.pf[:, 4:5], 160.0, A.mult, 63.0, A.add), r=pc, w=[("pf", 9, 10)])
-        op("v", lambda: ts(T.pf[:, 10:11], T.pf[:, 2:3], -16.0, A.mult), r=pc, w=[("pf", 10, 11)])
-        op("v", lambda: V.tensor_tensor(T.dmat[:], T.t1[:], T.t2[:], A.subtract), r=["t1", "t2"], w=["dmat"])
-        op("v", lambda: ts(T.endu[:, 0:1], T.pf[:, 8:9], T.pf[:, 3:4], A.mult, T.pf[:, 9:10], A.add), r=["pf"], w=["endu"])
-        op("v", lambda: ts(T.dump[:], T.dump[:], T.pf[:, 10:11], A.add), r=["dump", "pf"], w=["dump"])
-        op("a", lambda: S.activation(T.zmax[:], T.zmin[:], F.Identity, bias=255.0, scale=-1.0), r=["zmin"], w=["zmax"])
+        op("v", lambda: V.memset(T.rb[:], 0.0), w=["rb"])
+        op("v", lambda: V.memset(T.domt[:, 0:DC], 0.0), w=[("domt", 0, DC)])
+        op("v", lambda: ts(T.pf[:, 10:11], T.pf[:, 8:9], T.pf[:, 3:4], A.mult, T.pf[:, 9:10], A.add), r=[("pf", 0, 10)], w=[("pf", 10, 11)])
+        for tab in ("tpt", "oct"):
+            op("v", lambda: V.memset(T[tab][:, 0:DC], 0), w=[(tab, 0, DC)])
+        op("v", lambda: ts(T.endu[:], T.jr[:, 0:2], float(DW), A.mult, T.pf[:, 10:11], A.add), r=["jr", ("pf", 10, 11)], w=["endu"])
+        op("v", lambda: V.tensor_copy(T.zd[:, DW:2 * DW], T.zd[:, 0:DW]), r=[("zd", 0, DW)], w=[("zd", DW, 2 * DW)])
+        op("v", lambda: V.memset(T.rb[:, 16:136:17], -10000.0), w=["rb"])
+        for h in range(2):
+            op("v", lambda: V.memset(T["mm%d" % h][:, 0:1], -1.0), w=["mm%d" % h])
+            op("v", lambda: V.memset(T["kd%d" % h][:, 16:136:17], -1.0), w=["kd%d" % h])
+        op("a", lambda: S.activation(T.zmax[:, 0:zw], T.zmin[:, 0:zw], F.Identity, bias=255.0, scale=-1.0), r=["zmin"], w=["zmax"])
+        op("a", lambda: S.activation(T.identb[:], T.ident[:], F.Copy), r=["ident"], w=["identb"])
+        fill("ones", T.ones[:], 1.0)
 
-    def PG(s, lo, hi):
-        k = s % 2
+    def gather(q, out, src, r, w):
+        op(q, (lambda: S.activation(out, src, F.Copy)) if q == "a" else (lambda: V.tensor_copy(out, src)), r=r, w=w)
+
+    def by(tab, name, lo, hi):
+        a, b = lo // 16 + 8 * (lo // 128), hi // 16 + 8 * (lo // 128)
+        return T[tab][:, 0:W].indirect(T[name][:, a:b]), (name, a, b)
+
+    def PG(s, h):
+        k, lo, hi = s % 2, 128 * h, 128 * h + 128
         tab = "oct" if k else "tpt"
-        op("v", lambda: V.tensor_copy(T["pu%d" % k][:, lo:hi], T[tab][:, 0:NV].indirect(T["li%d" % k][:, lo // 16:hi // 16])),
-           r=[tab, ("li%d" % k, lo // 16, hi // 16)], w=[("pu%d" % k, lo, hi)])
+        src, span = by(tab, "li%d" % k, lo, hi)
+        gather(ENG["P"], T["pu%d" % k][:, lo:hi], src, [tab, span], [("pu%d" % k, lo, hi)])
 
-    def PF(s, lo, hi):
-        k = s % 2
-        op("v", lambda: ts(T["pw%d" % k][:, lo:hi], T["pu%d" % k][:, lo:hi], -MID, A.add), r=[("pu%d" % k, lo, hi)], w=[("pw%d" % k, lo, hi)])
+    def PF(s, h):
+        k, lo, hi = s % 2, 128 * h, 128 * h + 128
+        out, src = T["pw%d" % k][:, lo:hi], T["pu%d" % k][:, lo:hi]
+        q = ENG["F"][2 * k + h]
+        op(q, (lambda: ts(out, src, -MID, A.add)) if q == "v" else (lambda: S.activation(out, src, F.Identity, bias=-MID)),
+           r=[("pu%d" % k, lo, hi)], w=[("pw%d" % k, lo, hi)])
 
     def DM(s, h):
         k = s % 2
@@ -194,14 +231,12 @@ def rank_program(g, core, T, topo):
         k = s % 2
         lo, hi = CUT[k][j:j + 2]
         tab = "valt" if k else "domt"
-        src = T[tab][:, 0:W].indirect(T["pu%d" % k][:, lo:hi])
-        out = T["x%d" % k][:, 16 * lo:16 * hi]
-        op("a" if j else "v", (lambda: S.activation(out, src, F.Copy)) if j else (lambda: V.tensor_copy(out, src)),
-           r=[tab, ("pu%d" % k, lo, hi)], w=[("x%d" % k, lo, hi)])
+        gather("v" if j in ONV[k] else "a", T["x%d" % k][:, 16 * lo:16 * hi], T[tab][:, DC:W].indirect(T["pu%d" % k][:, lo:hi]),
+               [tab, ("pu%d" % k, lo, hi)], [("x%d" % k, lo, hi)])
 
     def SC(s, j):
         k = s % 2
-        lo, hi = CUT[k][j:j + 2]
+        lo, hi = SCUT[k][j:j + 2]
         z = "zmax" if k else "zmin"
         op("v", lambda: V.tensor_tensor_scan(T["y%d" % k][:, 16 * lo:16 * hi], T[z][:, 0:16 * (hi - lo)], T["x%d" % k][:, 16 * lo:16 * hi],
                                              0.0, A.min if k else A.max, A.max if k else A.min),
@@ -213,79 +248,103 @@ def rank_program(g, core, T, topo):
             op("t", lambda: PE.matmul(T["kd%d" % h][:, i:136:17], T["x%d" % k][:, 2048 * h + i:2048 * h + 2048:16], T.g8[:], True, True),
                r=[("x%d" % k, 128 * h, 128 * h + 128), "g8"], w=[("kd%d" % h, 0, 136)])
 
-    def A1(h):
+    def A1(s, h):
         op("v", lambda: V.tensor_tensor_scan(T["mm%d" % h][:, 1:137], T.rb[:], T["kd%d" % h][:, 0:136], -1.0, A.add, A.max),
            r=["rb", ("kd%d" % h, 0, 136)], w=["mm%d" % h])
 
-    def A2(h):
+    def A2(s, h):
         op("v", lambda: V.tensor_tensor(T["ll%d" % h][:], T["kd%d" % h][:, 0:136], T["mm%d" % h][:, 0:136], A.is_le),
            r=[("kd%d" % h, 0, 136), "mm%d" % h], w=["ll%d" % h])
 
-    def A3(h):
-        op("v", lambda: V.tensor_tensor_scan(T["ss%d" % h][:], T["kd%d" % h][:, 256:392], T["ll%d" % h][:], 0.0, A.add, A.mult),
+    def A3(s, h):
+        op("v", lambda: V.tensor_tensor_scan(T["ss%d" % h][:, SO:SO + 136], T["kd%d" % h][:, 256:392], T["ll%d" % h][:], 0.0, A.add, A.mult),
            r=[("kd%d" % h, 256, 392), "ll%d" % h], w=["ss%d" % h])
 
     def E(s, h):
         k = s % 2
-        op("v", lambda: V.tensor_tensor(T["ee%d" % h][:], T["ss%d" % h][:, 0:136].indirect(T.stu[:, 16:24]), T.mask[:], A.mult),
-           r=["ss%d" % h, "stu", "mask"], w=["ee%d" % h])
-        op("t", lambda: PE.matmul(T["lp%d" % k][:, 8 * h:8 * h + 8], T["ee%d" % h][:], T.h8[:], True, True),
-           r=["ee%d" % h, "h8"], w=[("lp%d" % k, 8 * h, 8 * h + 8)])
+        ss, dd = T["ss%d" % h], T["dd%d" % h]
+        op("t", lambda: PE.matmul(dd[0:40, DW:DW + 128], ss[:, 16:SO + 136:17], T.identh[:], True, True),
+           r=["ss%d" % h, "identh"], w=[("dd%d" % h, DW, DW + 128)])
+        for r in range(16):
+            op("t", lambda: PE.matmul(dd[0:8, DW + r:DW + 128:16], T.identh[:, r:128:16], ss[:, SO + 16:SO + 136:17], True, True),
+               r=["ss%d" % h, "identh"], w=[("dd%d" % h, DW, DW + 128)])
+
+    def BC(s, h):
+        k = s % 2
+        out, src = T["lt%d" % h][0:40, :], T["dd%d" % h][0:40, DW:DW + 128]
+        op(ENG["B"], (lambda: V.tensor_copy(out, src)) if ENG["B"] == "v" else (lambda: S.activation(out, src, F.Copy)),
+           r=[("dd%d" % h, DW, DW + 128)], w=["lt%d" % h])
+        op("t", lambda: PE.matmul(T["lp%d" % k][:, 8 * h:8 * h + 8], T["lt%d" % h][0:40, :], T.identh[0:40, 0:8], True, True),
+           r=["lt%d" % h, "identh"], w=[("lp%d" % k, 8 * h, 8 * h + 8)])
 
     def U(s, h):
         k = s % 2
-        op("v", lambda: ts(T["li%d" % k][:, 8 * h:8 * h + 8], T["lp%d" % k][:, 8 * h:8 * h + 8], MID, A.add),
-           r=[("lp%d" % k, 8 * h, 8 * h + 8)], w=[("li%d" % k, 8 * h, 8 * h + 8)])
+        if s == 0:
+            return
+        out, src = T["li%d" % k][:, 16 * h:16 * h + 8], T["lp%d" % k][:, 8 * h:8 * h + 8]
+        q = ENG["U"][2 * k + h]
+        op(q, (lambda: ts(out, src, MID + DC, A.add)) if q == "v" else (lambda: S.activation(out, src, F.Identity, bias=MID + DC)),
+           r=[("lp%d" % k, 8 * h, 8 * h + 8)], w=[("li%d" % k, 16 * h, 16 * h + 8)])
 
-    def BC(h):
-        op("a", lambda: S.activation(T["bc%d" % h][:], T["ss%d" % h][:, 0:136].indirect(T.stu[:, 16:24]), F.Copy),
-           r=["ss%d" % h, "stu"], w=["bc%d" % h])
-
-    def BP(h):
-        op("t", lambda: PE.matmul(T["dd%d" % h][:, 0:DW], T["ee%d" % h][:], T.r2[:], True, False), r=["ee%d" % h, "r2"], w=["dd%d" % h])
-        op("t", lambda: PE.matmul(T["dd%d" % h][:, 0:DW], T["bc%d" % h][:], T.r1[:], False, True), r=["bc%d" % h, "r1"], w=["dd%d" % h])
+    def BP(s, h):
+        lt, dd = T["lt%d" % h], T["dd%d" % h]
+        op("t", lambda: PE.matmul(dd[:, 0:DW], lt[0:40, :], T.r2[0:40, :], True, False), r=["lt%d" % h, "r2"], w=[("dd%d" % h, 0, DW)])
+        for b, (lo, hi) in enumerate(segs):
+            op("t", lambda: PE.matmul(dd[:, lo:hi], T.gs[0:40, :], lt[0:40, 16 * b:16 * b + hi - lo], False, b == 7),
+               r=["lt%d" % h, "gs"], w=[("dd%d" % h, 0, DW)])
 
     def SG(s, h):
         k = s % 2
-        op("a", lambda: S.activation(T["sg%d" % k][:, DW * h:DW * h + DW], T["dd%d" % h][:, 0:DW], F.Sign),
-           r=["dd%d" % h], w=[("sg%d" % k, DW * h, DW * h + DW)])
-
-    def off(s):
-        return "offa%d" % (s // 2) if s % 2 else "offc"
+        op("a", lambda: S.activation(T["sg%d" % k][:, DW * h:DW * h + DW], T["dd%d" % h][:, 0:DW], F.Abs, scale=FAR),
+           r=[("dd%d" % h, 0, DW)], w=[("sg%d" % k, DW * h, DW * h + DW)])
 
     def DS(s, j):
         k = s % 2
-        if j == 0:
-            op("v", lambda: V.tensor_tensor_scan(T.dsc[:], T["sg%d" % k][:], T.d1[:], 1.0, A.mult, A.add), r=["sg%d" % k, "d1"], w=["dsc"])
-        elif j == 1:
-            op("v", lambda: ts(T.dt1[:], T.dsc[:, 0:2 * DW].indirect(T.endu[:, 0:1]), 0.0, A.is_equal, 4096.0, A.mult),
-               r=["dsc", "endu"], w=["dt1"])
-        elif j == 2:
-            op("v", lambda: V.tensor_tensor(T.dt2[:], T["lp%d" % k][:, 0:16], T.dt1[:], A.add), r=["dt1", "lp%d" % k], w=["dt2"])
-        elif j == 3:
-            op("v", lambda: V.tensor_tensor(T.dt3[:], T.dt2[:], T.dump[:], A.min), r=["dt2", "dump"], w=["dt3"])
+        off = "offa%d" % (s // 2) if k else "offc"
+        h0, h1 = ((0, 2), (0, 1), (1, 2))[j // 2]
+        lo, hi = DW * h0, DW * h1
+        if j % 2 == 0:
+            op("v", lambda: V.tensor_tensor_scan(T.dsc[:, lo:hi], T["sg%d" % k][:, lo:hi], T.zd[:, lo:hi], 1.0, A.min, A.max),
+               r=[("sg%d" % k, lo, hi), "zd"], w=[("dsc", lo, hi)])
         else:
-            op("v", lambda: ts(T[off(s)][:], T.dt3[:], MID, A.add), r=["dt3"], w=[off(s)])
+            op("v", lambda: V.tensor_tensor(T[off][:, 16 * h0:16 * h1], T.dsc[:, lo:hi].indirect(T.endu[:, 0:h1 - h0]), T["li%d" % k][:, 16 * h0:16 * h1], A.min),
+               r=[("dsc", lo, hi), "endu", ("li%d" % k, 16 * h0, 16 * h1)], w=[(off, 16 * h0, 16 * h1)])
 
-    def SW(b):
-        op("v", lambda: V.tensor_copy(T.valt[:, 0:W].indirect(T.offc[:, 4 * b:4 * b + 4]), T.y0[:, 1024 * b + 15:1024 * b + 1024:16]),
-           r=["offc", ("y0", 64 * b, 64 * b + 64)], w=["valt"])
+    def SW(t, b):
+        lo, hi = WBLK[b]
+        out, span = by("valt", "offc", lo, hi)
+        op("v", lambda: V.tensor_copy(out, T.y0[:, 16 * lo + 15:16 * hi:16]), r=[span, ("y0", lo, hi)], w=["valt"])
+
+    LAST = len(SENDS) - 1
+
+    def DA(t, j):
+        lo, hi = SENDS[LAST]
+        src, span = by("domt", "li1", lo, hi)
+        gather(ENG["J"], T.da[:, 0:hi - lo], src, ["domt", span], ["da"])
 
     def GM(t, j):
         lo, hi = SENDS[j]
-        op("v", lambda: V.tensor_tensor(T["m%d" % t][:, lo:hi], T.domt[:, 0:W].indirect(T.li1[:, lo // 16:hi // 16]),
-                                        T.y1[:, 16 * lo + 15:16 * hi:16], A.min),
-           r=["domt", ("li1", lo // 16, hi // 16), ("y1", lo, hi)], w=[("m%d" % t, lo, hi)])
+        src, span = by("domt", "li1", lo, hi)
+        kept = j == LAST and "J0" in ORDER
+        op("v", lambda: V.tensor_tensor(T["m%d" % t][:, lo:hi], T.da[:, 0:hi - lo] if kept else src, T.y1[:, 16 * lo + 15:16 * hi:16], A.min),
+           r=(["da"] if kept else ["domt", span]) + [("y1", lo, hi)], w=[("m%d" % t, lo, hi)])
+
+    def HM(t, j):
+        lo, hi = SENDS[LAST]
+        src, span = by("domt", "offa%d" % t, lo, hi)
+        op("v", lambda: V.tensor_tensor(T.mo[:, lo:hi], src, T["m%d" % t][:, lo:hi], A.min),
+           r=["domt", span, ("m%d" % t, lo, hi)], w=[("mo", lo, hi)])
 
     def SD(offs, src, b):
-        op("v", lambda: V.tensor_copy(T.domt[:, 0:W].indirect(T[offs][:, 4 * b:4 * b + 4]), T[src][:, 64 * b:64 * b + 64]),
-           r=[offs, (src, 64 * b, 64 * b + 64)], w=["domt"])
+        lo, hi = BLK[b]
+        out, span = by("domt", offs, lo, hi)
+        op("v", lambda: V.tensor_copy(out, T[src][:, lo:hi]), r=[span, (src, lo, hi)], w=["domt"])
 
     def SEND(t, j):
         dst = T.cores[(rank + 1 + t % (N - 1)) % N]
         rid, pid, _ = topo.addr(dst)
-        src, land = ("offa%d" % t, "ino%d" % t) if j == 0 else ("m%d" % t, "inm%d" % t)
-        lo, hi = (0, 16) if j == 0 else SENDS[j - 1]
+        src, land = ("offa%d" % t, "ino%d" % t) if j in (0, 8, 9) else ("m%d" % t, "inm%d" % t)
+        lo, hi = {0: (0, 24), 8: (0, 8), 9: (16, 24)}[j] if j in (0, 8, 9) else SENDS[j - 1]
         sem = "in%d_%d" % (t, j)
 
         def call():
@@ -293,82 +352,87 @@ def rank_program(g, core, T, topo):
         op("p", call, r=[(src, lo, hi)], sem="loc", n=len(topo.engines(core, dst)))
         count[sem] = len(topo.engines(T.cores[(rank - 1 - t % (N - 1)) % N], core))
         done.append(("far", sem, count[sem], [], [(land, lo, hi)]))
+        TAG.append((TAG[0][0], "far", [], [(land, lo, hi)]))
 
-    def RG(t, j, o=A.min):
+    def RG(t, j):
         lo, hi = SENDS[j]
-        op("v", lambda: V.tensor_tensor(T.mr[:, lo:hi], T.domt[:, 0:W].indirect(T["ino%d" % t][:, lo // 16:hi // 16]),
-                                        T["inm%d" % t][:, lo:hi], o),
-           r=["domt", "ino%d" % t, ("inm%d" % t, lo, hi)], w=[("mr", lo, hi)])
+        src, span = by("domt", "ino%d" % t, lo, hi)
+        op("v", lambda: V.tensor_tensor(T.mr[:, lo:hi], src, T["inm%d" % t][:, lo:hi], A.min),
+           r=["domt", span, ("inm%d" % t, lo, hi)], w=[("mr", lo, hi)])
 
-    HF = 1536
+    def turned_sum(j, tab, n, bank, out, w):
+        if j == 0:
+            for c in range(n // 128):
+                op("t", lambda: PE.matmul(T[bank][:, 0:128], T[tab][:, DC + 128 * c:DC + 128 * c + 128], T.identb[:], c == 0, c == n // 128 - 1),
+                   r=[(tab, DC, DC + n), "identb"], w=[bank])
+        elif j == 1:
+            op("a", lambda: S.activation(T.sb[:], T[bank][:, 0:128], F.Copy), r=[bank], w=["sb"])
+            op("t", lambda: PE.matmul(T[bank][:, 256:258], T.sb[:], T.ones[:], True, True), r=["sb", "ones"], w=[bank])
+        else:
+            op("a", lambda: S.activation(out, T[bank][:, 256:257], F.Copy), r=[bank], w=w)
 
     def END(n, t):
+        lo, hi = SENDS[LAST]
+        nl = hi - lo
+        src, span = by("domt", "ino%d" % t, lo, hi)
         if n == "YV":
             op("s", lambda: g.sync.dma_start(T.yv[:], T["m%d" % t][:]), r=["m%d" % t], sem="st0", n=16)
-        elif n == "SV":
-            op("a", lambda: S.activation(T.x0[:, 0:NV], T.valt[:, 0:NV], F.Copy, accum_out=T.yss[:, 1:2]),
-               r=["valt"], w=["x0", ("yss", 1, 2)])
+        elif n in ("SV", "SW", "SX"):
+            turned_sum("VWX".index(n[1]), "valt", NV, "sp", T.yss[:, 1:2], [("yss", 1, 2)])
         elif n == "Z0":
-            op("v", lambda: V.memset(T.domt[:, NV:W], 0.0), w=[("domt", NV, W)])
+            op("v", lambda: V.memset(T.domt[:, 0:DC], 0.0), w=[("domt", 0, DC)])
+        elif n in ("SP", "SQ", "SR"):
+            turned_sum("PQR".index(n[1]), "domt", SUMS[0], "dd0", T.fb[:, nl + 3:nl + 4], [("fb", nl + 3, nl + 4)])
         elif n == "SA":
-            op("a", lambda: S.activation(T.x0[:, 0:HF], T.domt[:, 0:HF], F.Copy, accum_out=T.part[:, 0:1]),
-               r=[("domt", 0, HF)], w=["x0", ("part", 0, 1)])
+            op("a", lambda: S.activation(T.x0[:, SUMS[0]:SUMS[1]], T.domt[:, DC + SUMS[0]:DC + SUMS[1]], F.Copy, accum_out=T.fb[:, nl:nl + 1]),
+               r=[("domt", DC + SUMS[0], DC + SUMS[1])], w=["x0", ("fb", nl, nl + 1)])
         elif n == "SB":
-            op("v", lambda: V.tensor_reduce(T.part[:, 1:2], T.domt[:, HF:NV], AxisListType.X, A.add), r=[("domt", HF, NV)], w=[("part", 1, 2)])
+            op("v", lambda: V.tensor_reduce(T.fb[:, nl + 1:nl + 2], T.domt[:, DC + SUMS[1]:W], AxisListType.X, A.add),
+               r=[("domt", DC + SUMS[1], W)], w=[("fb", nl + 1, nl + 2)])
+        elif n == "SG":
+            op("a", lambda: S.activation(T.da[:, 0:nl], src, F.Copy, scale=-1.0, accum_out=T.fb[:, nl + 2:nl + 3]),
+               r=["domt", span], w=["da", ("fb", nl + 2, nl + 3)])
         elif n == "YT":
             for h in range(2):
-                op("t", lambda: PE.matmul(T.yq[0:8, 128 * h:128 * h + 128], T["ss%d" % h][:, 16:136:17], T.ident[:], True, True),
-                   r=["ss%d" % h, "ident"], w=["yq"])
+                op("t", lambda: PE.matmul(T.yq[0:8, 128 * h:128 * h + 128], T["ss%d" % h][:, SO + 16:SO + 136:17], T.identh[:], True, True),
+                   r=["ss%d" % h, "identh"], w=["yq"])
         elif n == "RL":
-            RG(t, 2, A.subtract)
-        elif n == "Z1":
-            op("v", lambda: ts(T.dsc[:, 0:64], T.mr[:, 192:256], 0.0, A.max, -1.0, A.mult), r=[("mr", 192, 256)], w=["dsc"])
-        elif n == "Z2":
-            op("v", lambda: V.tensor_reduce(T.part[:, 2:3], T.dsc[:, 0:64], AxisListType.X, A.add), r=["dsc"], w=[("part", 2, 3)])
+            op("v", lambda: V.tensor_tensor(T.fb[:, 0:nl], src, T["inm%d" % t][:, lo:hi], A.min),
+               r=["domt", span, ("inm%d" % t, lo, hi)], w=[("fb", 0, nl)])
         elif n == "Z3":
-            op("v", lambda: V.tensor_reduce(T.yss[:, 0:1], T.part[:, 0:3], AxisListType.X, A.add), r=["part"], w=[("yss", 0, 1)])
+            op("v", lambda: V.tensor_reduce(T.yss[:, 0:1], T.fb[:, 0:nl + 4], AxisListType.X, A.add), r=["fb"], w=[("yss", 0, 1)])
             op("s", lambda: g.sync.dma_start(T.ys[:], T.yss[:]), r=["yss"], sem="st2", n=16)
         else:
             op("a", lambda: S.activation(T.yts[:], T.yq[0:8, 0:NL], F.Identity, bias=MID), r=["yq"], w=["yts"])
             op("a", lambda: S.dma_start(T.yt[:], T.yts[:]), r=["yts"], sem="st1", n=16)
 
+    STEP = {"G": G, "S": SC, "K": KEY, "D": DS, "E": E, "U": U, "C": SG, "M": DM, "Aa": A1, "Ab": A2, "Ac": A3, "B": BC, "Q": BP,
+            "P": PG, "F": PF}
+    ROUND = {"N": GM, "T": SEND, "R": RG, "W": SW, "J": DA, "H": HM,
+             "O": lambda t, b: SD("offa%d" % t, "mo" if BLK[b][0] >= SENDS[LAST][0] and "H0" in ORDER else "m%d" % t, b),
+             "I": lambda t, b: SD("ino%d" % t, "mr", b)}
+
     def part(n, t):
-        first, last = t == 0, t == RO - 1
+        TAG[0][0] = (n, t)
+        last = t == RO - 1
         name = n.rstrip("0123456789")
         d = [int(c) for c in n[len(name):]]
-        s = 2 * t + d[0] if d else None
-        if n in ("YV", "SV", "Z0", "SA", "SB", "YT", "RL", "Z1", "Z2", "Z3", "YU"):
+        if n in ENDS:
             if last:
                 END(n, t)
-        elif name in ("E", "U", "B", "Q", "SG", "P", "F", "M") and d[0] == 2 and last or n in ("R2", "I3") and last:
-            pass
-        elif name in ("Pn", "Fn", "SGo") and first or name in ("Pf", "Ff") and not first:
-            pass
-        elif name == "SGo":
-            SG(2 * t, d[0])
-        elif name in ("G", "S", "K", "D", "E", "U", "SG", "M"):
-            {"G": G, "S": SC, "K": KEY, "D": DS, "E": E, "U": U, "SG": SG, "M": DM}[name](s, d[1])
-        elif name in ("Aa", "Ab", "Ac", "B", "Q"):
-            {"Aa": A1, "Ab": A2, "Ac": A3, "B": BC, "Q": BP}[name](d[1])
-        elif name[0] in "PF":
-            lo, hi = (128 * d[1], 128 * d[1] + 128) if len(d) > 1 else (0, NL)
-            (PG if name[0] == "P" else PF)(s, lo, hi)
-        elif name == "W":
-            SW(d[0])
-        elif name == "O":
-            SD("offa%d" % t, "m%d" % t, d[0])
-        elif name == "I":
-            SD("ino%d" % t, "mr", d[0])
-        else:
-            {"N": GM, "T": SEND, "R": RG}[name](t, d[0])
+        elif name in STEP:
+            if not (last and d[0] == 2):
+                STEP[name](2 * t + d[0], *d[1:])
+        elif not (last and n in ("R%d" % LAST, "I%d" % (len(BLK) - 1))):
+            ROUND[name](t, d[0])
 
-    E(0, 0); BC(0); BP(0); E(0, 1); BC(1); BP(1)
-    PG(0, 0, NL)
+    consts()
     consts2()
-    SG(0, 0); SG(0, 1)
-    PF(0, 0, NL); DM(0, 0); DM(0, 1)
+    for n in FIRST:
+        if n in ORDER:
+            part(n, -1)
     for t in range(RO):
-        for n in ORDER:
+        for n in ORDER if t < RO - 1 else FINAL or ORDER:
             part(n, t)
     for sem, c in count.items():
         g.wait_ge(T.sem[sem], c)

@@ -7,45 +7,50 @@ DW = 320
 MID = 1280.0
 FAR = 4096.0
 H = "float16"
-CUT = ((0, 64, 128, 192, 240, 256), (0, 40, 84, 128, 192, 240, 256))
+CUT = ((0, 72, 128, 192, 240, 256), (0, 56, 128, 192, 240, 256))
+CUTL = None
 ONV = ((0,), (0,))
-SCUT = CUT
 SENDS = ((0, 64), (64, 128), (128, 192), (192, 256))
 BLK = ((0, 64), (64, 128), (128, 192), (192, 256))
-SUMS = (768, 1536)
-SO = 17 * 32
-WBLK = BLK
-ENG = {"U": "aaaa", "J": "a", "P": "a", "F": "aavv", "B": "a"}
+WBLK = ((0, 64), (64, 128), (128, 192), (192, 256))
+KCUT = ((0, 128), (128, 256), (256, 256))
+RCUT = ((0, 128), (128, 256))
+RCUTL = ((0, 128), (128, 192), (192, 256))
+SUMS = (0, 1536)
+FLIP = 1280
+TOP = 255.0
+LOW = -5000.0
+LATE = 128
+ENG = {"U": "aaaa", "J": "a", "P": "aaaa", "F": "aavv", "B": "aaaa"}
 ORDER = """
-B01 U01 P01 F01 G01 G00 M01 Q01 K00 S00 S01 Aa00 C01 D00 Ab00 G03 D01 Ac00 W0 S03 W1 G02 S02 E10 B10 Q10 G04 K01 U10 C10 P10 S04 W2 W3
-Aa01 Ab01 Ac01 D12 G11 E11 B11 G12 U11 Q11 P11 C11 G13 G14 G15 G10 D13 S11 F10 S10 S12 N0 N1 M10 K10 D14 O0 Aa10 O1 Ab10 D15 Ac10 S13
-N2 F11 O2 SV M11 E20 K11 J0 S14 T8 T1 T2 T9 T3 S15 Z0 R1 R0 N3 T4 I1 Aa11 Ab11 I0 Ac11 H0 O3 R2 I2 SW YT YU SP B20 SA SQ U20 Q20 SG YV
-R3 I3 SB SR P20 F20 RL E21 C20 SX Z3 M20
+Q01 P00 U01 F00 M00 P01 G01 F01 C01 G04 G02 G00 K00 S00 D00 Aa00 D01 Ab00 Ac00 E10 M01 B10 Q10 G03 S01 W0 S02 W1 S04 W2 S03 C10 U10 D12 P10 K01 W3 Aa01 Ab01 F10 Ac01 G11 G10 S11 S10 D13 E11 M10 B11 U11 Q11 P11 C11 G12 N0 K10 F11 O0 D14 N1 Aa10 O1 D15 G13 G14 S12 Ab10 N2 Ac10 M11 E20 K11 B20 T8 T9 T1 T2 T3 O2 S13 S14 Q20 N3 O3 Aa11 Ab11 R0 R1 C20 U20 Ac11 I0 I2 I1 T4 I3 E21 B21
 """.split()
-FINAL = []
-FIRST = "E20 E21 B20 B21 Q20 Q21 U20 U21 P20 P21 F20 F21 M20 M21 C20 C21 D20 D21 D22 D23 D24 D25".split()
-ENDS = ("YV", "SV", "SW", "SX", "Z0", "SA", "SB", "SP", "SQ", "SR", "SG", "YT", "RL", "Z3", "YU")
+FINAL = """
+P00 U01 P01 F00 Q01 M00 F01 G01 C01 G04 G02 G00 M01 K00 S00 D00 Aa00 Ab00 D01 Ac00 E10 B10 Q10 G03 S01 W0 S02 W1 S04 W2 S03 U10 P10 C10 K01 W3 Aa01 G11 Ab01 Ac01 G10 D12 E11 B11 Q11 U11 P11 J0 C11 G12 G13 G14 S11 S10 D13 N1 N0 O0 D14 O1 D15 S12 F10 N2 F11 O2 Z0 S13 S14 T8 T2 T1 SV M10 K11 K10 R0 I0 N3 I1 SA SG0 T3 T9 Aa11 H0 SB Aa10 Ab11 Ab10 O3 Ac10 R1 SW SG1 M11 Ac11 I2 SX YV SG2 YT T4 R2 YU Z3
+""".split()
+FIRST = "B20 B21 Q20 Q21 U20 U21 P20 P21 F20 F21 M20 M21 C20 C21 D20 D21 D22 D23 D24 D25".split()
+ENDS = ("YV", "SV", "SW", "SX", "Z0", "SA", "SB", "SP", "SQ", "SR", "SG0", "SG1", "SG2", "SG3", "YT", "Z3", "YU")
 TAG = [[""]]
 
 SCRATCH = {
-    "domt": ("sbuf", [128, W], "bfloat16"), "valt": ("sbuf", [128, W], "bfloat16"),
+    "domb": ("sbuf", [128, NV], "bfloat16"), "domt": ("sbuf", [128, W], "float32"), "valt": ("sbuf", [128, W], "bfloat16"),
     "tpt": ("sbuf", [128, W], "int32"), "oct": ("sbuf", [128, W], "int32"),
-    "qi": ("sbuf", [128, 16], "int32"), "qf": ("sbuf", [128, 16], "float32"),
-    "zmin": ("sbuf", [128, 2048], "bfloat16"), "zmax": ("sbuf", [128, 2048], "bfloat16"),
+    "qi": ("sbuf", [128, 16], "int32"), "qh": ("sbuf", [128, 16], H),
+    "zmin": ("sbuf", [128, 2048], "bfloat16"), "yb": ("sbuf", [128, NL], "bfloat16"),
     "pi": ("sbuf", [128, 8], "int32"), "pf": ("sbuf", [128, 16], "float32"),
-    "jc": ("sbuf", [128, 128], "float32"), "jr": ("sbuf", [128, 128], "float32"), "jd": ("sbuf", [128, 136], "float32"),
-    "ident": ("sbuf", [128, 128], "float32"), "identb": ("sbuf", [128, 128], "bfloat16"), "mask": ("sbuf", [128, 128], "float32"),
+    "jc": ("sbuf", [128, 128], "float32"), "jr": ("sbuf", [128, 16], "float32"), "jd": ("sbuf", [128, 136], "float32"),
+    "identb": ("sbuf", [128, 128], "bfloat16"), "mask": ("sbuf", [128, 16], "float32"),
     "ones": ("sbuf", [128, 2], "float32"), "sb": ("sbuf", [128, 128], "float32"),
-    "b8": ("sbuf", [128, 8], "float32"), "g8": ("sbuf", [128, 8], "bfloat16"), "h8": ("sbuf", [128, 8], H),
-    "dmat": ("sbuf", [128, 136], H), "t1": ("sbuf", [128, 144], "float32"),
+    "g8": ("sbuf", [128, 16], "bfloat16"),
+    "dmat": ("sbuf", [128, 136], H), "t1": ("sbuf", [128, 144], H),
     "rb": ("sbuf", [128, 136], "float32"),
     "r2": ("sbuf", [128, DW], H), "identh": ("sbuf", [128, 128], H), "gs": ("sbuf", [128, 128], H),
     "jg": ("sbuf", [128, 128], "float32"), "nid": ("sbuf", [128, 8], "float32"),
     "zd": ("sbuf", [128, 2 * DW], "bfloat16"), "dsc": ("sbuf", [128, 2 * DW], "bfloat16"),
-    "sti": ("sbuf", [128, 24], "int32"), "stu": ("sbuf", [128, 24], "uint16"), "endu": ("sbuf", [128, 2], "uint16"),
-    "offc": ("sbuf", [128, 32], "uint16"), "mr": ("sbuf", [128, NL], "bfloat16"),
-    "da": ("sbuf", [128, 64], "bfloat16"), "mo": ("sbuf", [128, NL], "bfloat16"),
-    "yts": ("sbuf", [8, NL], "float32"), "yss": ("sbuf", [128, 2], "float32"), "fb": ("sbuf", [128, 72], "float32"),
+    "endu": ("sbuf", [128, 2], "uint16"),
+    "offc": ("sbuf", [128, 32], "uint16"), "mr": ("sbuf", [128, NL], "float32"),
+    "da": ("sbuf", [128, 128], "float32"), "db": ("sbuf", [128, 128], "float32"), "mo": ("sbuf", [128, NL], "float32"),
+    "yts": ("sbuf", [8, NL], "float32"), "yss": ("sbuf", [128, 2], "float32"), "fb": ("sbuf", [128, 336], "float32"),
     "yq": ("psum", [128, 512], "float32"), "sp": ("psum", [128, 512], "float32"),
 }
 for _k in range(2):
@@ -57,14 +62,14 @@ for _k in range(2):
     SCRATCH["sg%d" % _k] = ("sbuf", [128, 2 * DW], "bfloat16")
     SCRATCH["mm%d" % _k] = ("sbuf", [128, 144], "float32")
     SCRATCH["ll%d" % _k] = ("sbuf", [128, 136], "float32")
-    SCRATCH["ss%d" % _k] = ("sbuf", [128, SO + 136], H)
+    SCRATCH["ss%d" % _k] = ("sbuf", [128, 136], H)
     SCRATCH["lt%d" % _k] = ("sbuf", [128, 128], H)
     for _n in ("kd", "lp", "dd"):
         SCRATCH["%s%d" % (_n, _k)] = ("psum", [128, 512], "float32")
 for _k in range(RO):
-    SCRATCH["m%d" % _k] = ("sbuf", [128, NL], "bfloat16")
+    SCRATCH["m%d" % _k] = ("sbuf", [128, NL], "float32")
     SCRATCH["offa%d" % _k] = ("sbuf", [128, 32], "uint16")
-    SCRATCH["inm%d" % _k] = ("sbuf", [128, NL], "bfloat16")
+    SCRATCH["inm%d" % _k] = ("sbuf", [128, NL], "float32")
     SCRATCH["ino%d" % _k] = ("sbuf", [128, 32], "uint16")
 
 SEMAPHORES = (["v", "a", "t", "p", "loc"] + ["ld%d" % k for k in range(5)] + ["st%d" % k for k in range(3)]
@@ -94,8 +99,11 @@ def rank_program(g, core, T, topo):
     def op(q, call, r=(), w=(), sem=None, n=1):
         r, w = spans(r), spans(w)
         banks = [(x[0], 0, BIG) for x in r + w if x[0] in PSUM]
+        names = {x[0] for x in r + w}
         need = {}
-        for (q0, s0, c0, r0, w0) in done:
+        for (q0, s0, c0, r0, w0, names0) in done:
+            if names.isdisjoint(names0):
+                continue
             dep = meet(r, w0) or meet(w, w0) or meet(w, r0)
             if q0 == q and s0 == q:
                 dep = dep and q != "t"
@@ -112,7 +120,7 @@ def rank_program(g, core, T, topo):
         ins = call()
         if ins is not None:
             ins.then_inc(T.sem[sem], n)
-        done.append((q, sem, count[sem], r, w))
+        done.append((q, sem, count[sem], r, w, names))
         TAG.append((TAG[0][0], q, r, w))
 
     def ts(out, in0, s1, o0, s2=None, o1=None):
@@ -121,16 +129,16 @@ def rank_program(g, core, T, topo):
         return V.tensor_scalar(out, in0, s1, s2, o0, o1)
 
     def fill(name, ap, c):
-        op("a", lambda: S.activation(ap, T.jd[:, 0:ap.shape[1]], F.Identity, bias=c, scale=0.0), r=["jd"], w=[name])
+        op("a", lambda: S.activation(ap, T.jd[0:ap.shape[0], 0:ap.shape[1]], F.Identity, bias=c, scale=0.0), r=["jd"], w=[name])
 
     op("a", lambda: S.dma_start(T.qi[:], T.q[:]), w=["qi"], sem="ld0", n=16)
+    op("s", lambda: g.sync.dma_start(T.domb[:], T.dom[:]), w=["domb"], sem="ld2", n=16)
     op("s", lambda: g.sync.dma_start(T.tpt[:, DC:W], T.tp[:]), w=[("tpt", DC, W)], sem="ld1", n=16)
-    op("s", lambda: g.sync.dma_start(T.domt[:, DC:W], T.dom[:]), w=[("domt", DC, W)], sem="ld2", n=16)
     op("s", lambda: g.sync.dma_start(T.valt[:, DC:W], T.val[:]), w=[("valt", DC, W)], sem="ld4", n=16)
     op("s", lambda: g.sync.dma_start(T.oct[:, DC:W], T.oc[:]), w=[("oct", DC, W)], sem="ld3", n=16)
 
     fl = {"allow_small_or_imprecise_dtypes": True}
-    zw = 16 * max(b - a for c in SCUT for a, b in zip(c[:-1], c[1:]))
+    zw = 16 * max(b - a for c in CUT + (CUTL or CUT) for a, b in zip(c[:-1], c[1:]))
     segs = []
     for b in range(8):
         segs.append((segs[-1][1] if segs else 0, (segs[-1][1] if segs else 0) + 64 - 16 * (b % 4)))
@@ -140,87 +148,86 @@ def rank_program(g, core, T, topo):
         op("p", lambda: g.iota(T.pi[:, 0:1], [[0, 1]], 0, 1), w=[("pi", 0, 1)])
         op("p", lambda: g.iota(T.jd[:], [[16, 8], [1, 17]], 0, -1, **fl), w=["jd"])
         op("p", lambda: g.iota(T.jc[:], [[1, 128]], 0, -1, **fl), w=["jc"])
-        op("p", lambda: g.iota(T.jr[:], [[0, 8], [1, 16]], 0, 0, **fl), w=["jr"])
-        op("p", lambda: g.iota(T.sti[:, 0:16], [[1, 16]], 0, 0), w=[("sti", 0, 16)])
+        op("p", lambda: g.iota(T.jr[:], [[1, 16]], 0, 0, **fl), w=["jr"])
         op("p", lambda: g.iota(T.jg[:], [[1, 8], [0, 16]], 32, -1, **fl), w=["jg"])
-        op("v", lambda: V.memset(T.zmin[:, 0:zw], 0.0), w=["zmin"])
+        op("p", lambda: g.iota(T.zmin[:, 0:zw], [[0, zw // 16], [-255, 16]], 255, 0, **fl), w=["zmin"])
+        for k in range(2):
+            op("v", lambda: V.memset(T["li%d" % k][:], 0), w=["li%d" % k])
+        op("v", lambda: V.memset(T.zd[:, 0:DW], 0.0), w=["zd"])
         for j, (m, sh) in enumerate(((15, 0), (127, 4), (3, 0), (7, 2))):
             op("v", lambda: ts(T.pi[:, j + 1:j + 2], T.pi[:, 0:1], m, A.bitwise_and, sh, A.arith_shift_right), r=[("pi", 0, 1)], w=[("pi", j + 1, j + 2)])
-        op("v", lambda: ts(T.ident[:], T.jc[:], 0.0, A.is_equal), r=["jc"], w=["ident"])
+        op("v", lambda: V.memset(T.rb[:], 0.0), w=["rb"])
         op("v", lambda: V.tensor_copy(T.pf[:, 0:5], T.pi[:, 0:5]), r=["pi"], w=[("pf", 0, 5)])
-        op("v", lambda: V.memset(T.zd[:, 0:DW], 0.0), w=["zd"])
-        op("v", lambda: V.memset(T.zmin[:, 0:zw:16], 255.0), w=["zmin"])
-        op("v", lambda: ts(T.mask[:], T.jr[:], T.pf[:, 1:2], A.is_equal), r=["jr"] + pc, w=["mask"])
-        op("v", lambda: ts(T.b8[:], T.jr[:, 0:8], T.pf[:, 2:3], A.is_equal), r=["jr"] + pc, w=["b8"])
-        op("v", lambda: ts(T.h8[:], T.jr[:, 0:8], T.pf[:, 2:3], A.is_equal), r=["jr"] + pc, w=["h8"])
         op("v", lambda: ts(T.nid[:], T.jc[:, 0:8], 0.0, A.is_equal, -1.0, A.mult), r=["jc"], w=["nid"])
-        op("v", lambda: V.tensor_copy(T.stu[:, 0:16], T.sti[:, 0:16]), r=["sti"], w=[("stu", 0, 16)])
+        op("v", lambda: ts(T.mask[:], T.jr[:], T.pf[:, 1:2], A.is_equal), r=["jr"] + pc, w=["mask"])
+        op("v", lambda: ts(T.identh[:], T.jc[:], 0.0, A.is_equal), r=["jc"], w=["identh"])
+        op("v", lambda: ts(T.t1[:, 1:137], T.jd[:], 0.0, A.is_equal), r=["jd"], w=["t1"])
         op("v", lambda: ts(T.gs[:], T.jg[:], 0.0, A.is_equal), r=["jg"], w=["gs"])
+        op("v", lambda: V.memset(T.t1[:, 0:137:17], 0.0), w=["t1"])
         for h in range(2):
-            fill("ss%d" % h, T["ss%d" % h][:, 16:SO:17], 0.0)
-        op("a", lambda: S.activation(T.identh[:], T.ident[:], F.Copy), r=["ident"], w=["identh"])
+            fill("dd%d" % h, T["dd%d" % h][0:32, DW:DW + 128], 0.0)
+            fill("mm%d" % h, T["mm%d" % h][:, 0:1], LOW)
+            fill("kd%d" % h, T["kd%d" % h][:, 16:136:17], LOW)
+        for b, (lo, hi) in enumerate(segs):
+            op("a", lambda: S.activation(T.zd[:, lo:lo + 16], T.mask[:], F.Copy, scale=FAR), r=["mask"], w=[("zd", lo, lo + 16)])
         for b, (lo, hi) in enumerate(segs):
             op("a", lambda: S.activation(T.r2[:, lo:hi], T.jc[:, 0:hi - lo], F.Identity, bias=T.nid[:, b:b + 1], scale=0.0),
                r=["jc", "nid"], w=[("r2", lo, hi)])
-        for k in range(2):
-            op("v", lambda: V.memset(T["li%d" % k][:], 0), w=["li%d" % k])
         for h in range(2):
             op("v", lambda: ts(T.li0[:, 16 * h:16 * h + 8], T.qi[:, 8 * h:8 * h + 8], float(DC), A.add), r=["qi"], w=[("li0", 16 * h, 16 * h + 8)])
-        op("v", lambda: ts(T.qf[:], T.qi[:], -MID, A.add), r=["qi"], w=["qf"])
+        op("v", lambda: ts(T.qh[:], T.qi[:], -MID, A.add), r=["qi"], w=["qh"])
         for h in range(2):
-            op("v", lambda: V.tensor_tensor(T.pw1[:, 128 * h:128 * h + 128], T.qf[:, 0:16].indirect(T.stu[:, 8 * h:8 * h + 8]), T.mask[:], A.mult),
-               r=["qf", ("stu", 0, 16), "mask"], w=[("pw1", 128 * h, 128 * h + 128)])
-            op("t", lambda: PE.matmul(T.yq[:, 8 * h:8 * h + 8], T.pw1[:, 128 * h:128 * h + 128], T.h8[:], True, True),
-               r=[("pw1", 128 * h, 128 * h + 128), "h8"], w=["yq"])
-        op("v", lambda: ts(T.t1[:, 1:137], T.jd[:], 0.0, A.is_equal), r=["jd"], w=["t1"])
-        for h in range(2):
-            op("v", lambda: V.tensor_copy(T["ss%d" % h][:, SO + 16:SO + 136:17], T.yq[:, 8 * h:8 * h + 8]), r=["yq"], w=["ss%d" % h])
-        op("v", lambda: V.memset(T.t1[:, 0:137:17], 0.0), w=["t1"])
-        for b, (lo, hi) in enumerate(segs):
-            op("a", lambda: S.activation(T.zd[:, lo:lo + 16], T.mask[:, 0:16], F.Copy, scale=FAR), r=["mask"], w=[("zd", lo, lo + 16)])
-        op("a", lambda: S.activation(T.g8[:], T.b8[:], F.Copy), r=["b8"], w=["g8"])
-
-    def consts2():
+            dd = T["dd%d" % h]
+            op("t", lambda: PE.matmul(dd[0:8, DW:DW + 128], T.qh[:, 8 * h:8 * h + 8], T.identh[:], True, True),
+               r=["qh", "identh"], w=[("dd%d" % h, DW, DW + 128)])
+            for r in range(16):
+                op("t", lambda: PE.matmul(dd[32:40, DW + r:DW + 128:16], T.identh[:, r:128:16], T.qh[:, 8 * h:8 * h + 8], True, True),
+                   r=["qh", "identh"], w=[("dd%d" % h, DW, DW + 128)])
+        for k in range(2):
+            op("v", lambda: ts(T.g8[:, 8 * k:8 * k + 8], T.jr[:, 0:8], T.pf[:, 2:3], A.is_equal, 1.0 - 2 * k, A.mult), r=["jr"] + pc, w=[("g8", 8 * k, 8 * k + 8)])
         op("v", lambda: V.tensor_tensor(T.dmat[:], T.t1[:, 0:136], T.t1[:, 1:137], A.subtract), r=["t1"], w=["dmat"])
-        for c in range(4):
-            e = segs[c][1] - 1
-            op("v", lambda: ts(T.zd[:, e:DW:160], T.zd[:, e:DW:160], T.pf[:, 1:2], A.max, 16.0 * c, A.add), r=[("zd", e, e + 161)] + pc, w=[("zd", e, e + 1), ("zd", e + 160, e + 161)])
         op("v", lambda: ts(T.pf[:, 8:9], T.pf[:, 3:4], -8.0, A.mult, 56.0, A.add), r=pc, w=[("pf", 8, 9)])
         op("v", lambda: ts(T.pf[:, 9:10], T.pf[:, 4:5], 160.0, A.mult, 63.0, A.add), r=pc, w=[("pf", 9, 10)])
-        op("v", lambda: V.memset(T.rb[:], 0.0), w=["rb"])
-        op("v", lambda: V.memset(T.domt[:, 0:DC], 0.0), w=[("domt", 0, DC)])
-        op("v", lambda: ts(T.pf[:, 10:11], T.pf[:, 8:9], T.pf[:, 3:4], A.mult, T.pf[:, 9:10], A.add), r=[("pf", 0, 10)], w=[("pf", 10, 11)])
-        for tab in ("tpt", "oct"):
-            op("v", lambda: V.memset(T[tab][:, 0:DC], 0), w=[(tab, 0, DC)])
-        op("v", lambda: ts(T.endu[:], T.jr[:, 0:2], float(DW), A.mult, T.pf[:, 10:11], A.add), r=["jr", ("pf", 10, 11)], w=["endu"])
-        op("v", lambda: V.tensor_copy(T.zd[:, DW:2 * DW], T.zd[:, 0:DW]), r=[("zd", 0, DW)], w=[("zd", DW, 2 * DW)])
         op("v", lambda: V.memset(T.rb[:, 16:136:17], -10000.0), w=["rb"])
-        for h in range(2):
-            op("v", lambda: V.memset(T["mm%d" % h][:, 0:1], -1.0), w=["mm%d" % h])
-            op("v", lambda: V.memset(T["kd%d" % h][:, 16:136:17], -1.0), w=["kd%d" % h])
-        op("a", lambda: S.activation(T.zmax[:, 0:zw], T.zmin[:, 0:zw], F.Identity, bias=255.0, scale=-1.0), r=["zmin"], w=["zmax"])
-        op("a", lambda: S.activation(T.identb[:], T.ident[:], F.Copy), r=["ident"], w=["identb"])
+        op("v", lambda: ts(T.pf[:, 10:11], T.pf[:, 8:9], T.pf[:, 3:4], A.mult, T.pf[:, 9:10], A.add), r=[("pf", 0, 10)], w=[("pf", 10, 11)])
+        op("v", lambda: V.memset(T.domt[:, 0:DC], TOP), w=[("domt", 0, DC)])
+        op("v", lambda: ts(T.endu[:], T.jr[:, 0:2], float(DW), A.mult, T.pf[:, 10:11], A.add), r=["jr", ("pf", 10, 11)], w=["endu"])
+        for c in range(4):
+            e = segs[c][1] - 1
+            op("v", lambda: ts(T.zd[:, e:DW:160], T.zd[:, e:DW:160], T.pf[:, 1:2], A.max, 16.0 * c, A.add), r=[("zd", e, e + 161)] + pc,
+               w=[("zd", e, e + 1), ("zd", e + 160, e + 161)])
+        op("v", lambda: V.tensor_copy(T.zd[:, DW:2 * DW], T.zd[:, 0:DW]), r=[("zd", 0, DW)], w=[("zd", DW, 2 * DW)])
+        op("a", lambda: S.activation(T.identb[:], T.identh[:], F.Copy), r=["identh"], w=["identb"])
         fill("ones", T.ones[:], 1.0)
+        fill("fb", T.fb[:, c0:c0 + 1], -TOP * NV)
+        flip("a", T.domt[:, DC:DC + FLIP], T.domb[:, 0:FLIP], ["domb"], [("domt", DC, DC + FLIP)])
+        flip("v", T.domt[:, DC + FLIP:W], T.domb[:, FLIP:NV], ["domb"], [("domt", DC + FLIP, W)])
 
     def gather(q, out, src, r, w):
         op(q, (lambda: S.activation(out, src, F.Copy)) if q == "a" else (lambda: V.tensor_copy(out, src)), r=r, w=w)
+
+    def flip(q, out, src, r, w):
+        op(q, (lambda: S.activation(out, src, F.Identity, bias=TOP, scale=-1.0)) if q == "a" else (lambda: ts(out, src, -1.0, A.mult, TOP, A.add)), r=r, w=w)
+
+    def shift(q, out, src, c, r, w):
+        op(q, (lambda: S.activation(out, src, F.Identity, bias=c)) if q == "a" else (lambda: ts(out, src, c, A.add)), r=r, w=w)
 
     def by(tab, name, lo, hi):
         a, b = lo // 16 + 8 * (lo // 128), hi // 16 + 8 * (lo // 128)
         return T[tab][:, 0:W].indirect(T[name][:, a:b]), (name, a, b)
 
+    def piece(s, j):
+        return (CUTL if CUTL and s >= 2 * RO - 2 else CUT)[s % 2][j:j + 2]
+
     def PG(s, h):
         k, lo, hi = s % 2, 128 * h, 128 * h + 128
         tab = "oct" if k else "tpt"
         src, span = by(tab, "li%d" % k, lo, hi)
-        gather(ENG["P"], T["pu%d" % k][:, lo:hi], src, [tab, span], [("pu%d" % k, lo, hi)])
+        gather(ENG["P"][2 * k + h], T["pu%d" % k][:, lo:hi], src, [tab, span], [("pu%d" % k, lo, hi)])
 
     def PF(s, h):
         k, lo, hi = s % 2, 128 * h, 128 * h + 128
-        out, src = T["pw%d" % k][:, lo:hi], T["pu%d" % k][:, lo:hi]
-        q = ENG["F"][2 * k + h]
-        op(q, (lambda: ts(out, src, -MID, A.add)) if q == "v" else (lambda: S.activation(out, src, F.Identity, bias=-MID)),
-           r=[("pu%d" % k, lo, hi)], w=[("pw%d" % k, lo, hi)])
+        shift(ENG["F"][2 * k + h], T["pw%d" % k][:, lo:hi], T["pu%d" % k][:, lo:hi], -MID, [("pu%d" % k, lo, hi)], [("pw%d" % k, lo, hi)])
 
     def DM(s, h):
         k = s % 2
@@ -229,27 +236,27 @@ def rank_program(g, core, T, topo):
 
     def G(s, j):
         k = s % 2
-        lo, hi = CUT[k][j:j + 2]
+        lo, hi = piece(s, j)
         tab = "valt" if k else "domt"
-        gather("v" if j in ONV[k] else "a", T["x%d" % k][:, 16 * lo:16 * hi], T[tab][:, DC:W].indirect(T["pu%d" % k][:, lo:hi]),
-               [tab, ("pu%d" % k, lo, hi)], [("x%d" % k, lo, hi)])
+        flip("v" if j in ONV[k] else "a", T["x%d" % k][:, 16 * lo:16 * hi], T[tab][:, DC:W].indirect(T["pu%d" % k][:, lo:hi]),
+             [tab, ("pu%d" % k, lo, hi)], [("x%d" % k, lo, hi)])
 
     def SC(s, j):
         k = s % 2
-        lo, hi = SCUT[k][j:j + 2]
-        z = "zmax" if k else "zmin"
-        op("v", lambda: V.tensor_tensor_scan(T["y%d" % k][:, 16 * lo:16 * hi], T[z][:, 0:16 * (hi - lo)], T["x%d" % k][:, 16 * lo:16 * hi],
-                                             0.0, A.min if k else A.max, A.max if k else A.min),
-           r=[z, ("x%d" % k, lo, hi)], w=[("y%d" % k, lo, hi)])
+        lo, hi = piece(s, j)
+        op("v", lambda: V.tensor_tensor_scan(T["y%d" % k][:, 16 * lo:16 * hi], T.zmin[:, 0:16 * (hi - lo)], T["x%d" % k][:, 16 * lo:16 * hi],
+                                             0.0, A.max, A.min), r=["zmin", ("x%d" % k, lo, hi)], w=[("y%d" % k, lo, hi)])
 
-    def KEY(s, h):
+    def KEY(s, j):
         k = s % 2
+        lo, hi = KCUT[j]
+        h = lo // 128
         for i in range(16):
-            op("t", lambda: PE.matmul(T["kd%d" % h][:, i:136:17], T["x%d" % k][:, 2048 * h + i:2048 * h + 2048:16], T.g8[:], True, True),
-               r=[("x%d" % k, 128 * h, 128 * h + 128), "g8"], w=[("kd%d" % h, 0, 136)])
+            op("t", lambda: PE.matmul(T["kd%d" % h][lo - 128 * h:hi - 128 * h, i:136:17], T["x%d" % k][:, 16 * lo + i:16 * hi:16], T.g8[:, 8 * k:8 * k + 8], True, True),
+               r=[("x%d" % k, lo, hi), "g8"], w=[("kd%d" % h, 0, 136)])
 
     def A1(s, h):
-        op("v", lambda: V.tensor_tensor_scan(T["mm%d" % h][:, 1:137], T.rb[:], T["kd%d" % h][:, 0:136], -1.0, A.add, A.max),
+        op("v", lambda: V.tensor_tensor_scan(T["mm%d" % h][:, 1:137], T.rb[:], T["kd%d" % h][:, 0:136], LOW, A.add, A.max),
            r=["rb", ("kd%d" % h, 0, 136)], w=["mm%d" % h])
 
     def A2(s, h):
@@ -257,34 +264,29 @@ def rank_program(g, core, T, topo):
            r=[("kd%d" % h, 0, 136), "mm%d" % h], w=["ll%d" % h])
 
     def A3(s, h):
-        op("v", lambda: V.tensor_tensor_scan(T["ss%d" % h][:, SO:SO + 136], T["kd%d" % h][:, 256:392], T["ll%d" % h][:], 0.0, A.add, A.mult),
+        op("v", lambda: V.tensor_tensor_scan(T["ss%d" % h][:], T["kd%d" % h][:, 256:392], T["ll%d" % h][:], 0.0, A.add, A.mult),
            r=[("kd%d" % h, 256, 392), "ll%d" % h], w=["ss%d" % h])
 
     def E(s, h):
-        k = s % 2
         ss, dd = T["ss%d" % h], T["dd%d" % h]
-        op("t", lambda: PE.matmul(dd[0:40, DW:DW + 128], ss[:, 16:SO + 136:17], T.identh[:], True, True),
-           r=["ss%d" % h, "identh"], w=[("dd%d" % h, DW, DW + 128)])
         for r in range(16):
-            op("t", lambda: PE.matmul(dd[0:8, DW + r:DW + 128:16], T.identh[:, r:128:16], ss[:, SO + 16:SO + 136:17], True, True),
+            op("t", lambda: PE.matmul(dd[0:8, DW + r:DW + 128:16], T.identh[:, r:128:16], ss[:, 16:136:17], True, True),
                r=["ss%d" % h, "identh"], w=[("dd%d" % h, DW, DW + 128)])
+        op("t", lambda: PE.matmul(dd[32:40, DW:DW + 128], ss[:, 16:136:17], T.identh[:], True, True),
+           r=["ss%d" % h, "identh"], w=[("dd%d" % h, DW, DW + 128)])
 
     def BC(s, h):
         k = s % 2
-        out, src = T["lt%d" % h][0:40, :], T["dd%d" % h][0:40, DW:DW + 128]
-        op(ENG["B"], (lambda: V.tensor_copy(out, src)) if ENG["B"] == "v" else (lambda: S.activation(out, src, F.Copy)),
-           r=[("dd%d" % h, DW, DW + 128)], w=["lt%d" % h])
-        op("t", lambda: PE.matmul(T["lp%d" % k][:, 8 * h:8 * h + 8], T["lt%d" % h][0:40, :], T.identh[0:40, 0:8], True, True),
-           r=["lt%d" % h, "identh"], w=[("lp%d" % k, 8 * h, 8 * h + 8)])
+        gather(ENG["B"][2 * k + h], T["lt%d" % h][0:40, :], T["dd%d" % h][0:40, DW:DW + 128], [("dd%d" % h, DW, DW + 128)], ["lt%d" % h])
+        if s:
+            op("t", lambda: PE.matmul(T["lp%d" % k][:, 8 * h:8 * h + 8], T["lt%d" % h][0:40, :], T.identh[0:40, 0:8], True, True),
+               r=["lt%d" % h, "identh"], w=[("lp%d" % k, 8 * h, 8 * h + 8)])
 
     def U(s, h):
         k = s % 2
-        if s == 0:
-            return
-        out, src = T["li%d" % k][:, 16 * h:16 * h + 8], T["lp%d" % k][:, 8 * h:8 * h + 8]
-        q = ENG["U"][2 * k + h]
-        op(q, (lambda: ts(out, src, MID + DC, A.add)) if q == "v" else (lambda: S.activation(out, src, F.Identity, bias=MID + DC)),
-           r=[("lp%d" % k, 8 * h, 8 * h + 8)], w=[("li%d" % k, 16 * h, 16 * h + 8)])
+        if s:
+            shift(ENG["U"][2 * k + h], T["li%d" % k][:, 16 * h:16 * h + 8], T["lp%d" % k][:, 8 * h:8 * h + 8], MID + DC,
+                  [("lp%d" % k, 8 * h, 8 * h + 8)], [("li%d" % k, 16 * h, 16 * h + 8)])
 
     def BP(s, h):
         lt, dd = T["lt%d" % h], T["dd%d" % h]
@@ -316,6 +318,10 @@ def rank_program(g, core, T, topo):
         op("v", lambda: V.tensor_copy(out, T.y0[:, 16 * lo + 15:16 * hi:16]), r=[span, ("y0", lo, hi)], w=["valt"])
 
     LAST = len(SENDS) - 1
+    OWN = SENDS[LAST][0]
+
+    def rmw(t):
+        return "J0" in (ORDER if t < RO - 1 else FINAL)
 
     def DA(t, j):
         lo, hi = SENDS[LAST]
@@ -325,20 +331,33 @@ def rank_program(g, core, T, topo):
     def GM(t, j):
         lo, hi = SENDS[j]
         src, span = by("domt", "li1", lo, hi)
-        kept = j == LAST and "J0" in ORDER
-        op("v", lambda: V.tensor_tensor(T["m%d" % t][:, lo:hi], T.da[:, 0:hi - lo] if kept else src, T.y1[:, 16 * lo + 15:16 * hi:16], A.min),
+        kept = j == LAST and rmw(t)
+        op("v", lambda: V.tensor_tensor(T["m%d" % t][:, lo:hi], T.da[:, 0:hi - lo] if kept else src, T.y1[:, 16 * lo + 15:16 * hi:16], A.max),
            r=(["da"] if kept else ["domt", span]) + [("y1", lo, hi)], w=[("m%d" % t, lo, hi)])
 
-    def HM(t, j):
-        lo, hi = SENDS[LAST]
-        src, span = by("domt", "offa%d" % t, lo, hi)
-        op("v", lambda: V.tensor_tensor(T.mo[:, lo:hi], src, T["m%d" % t][:, lo:hi], A.min),
-           r=["domt", span, ("m%d" % t, lo, hi)], w=[("mo", lo, hi)])
+    def summed(t, own, lo, hi):
+        if t == RO - 1 and (lo >= OWN if own else lo >= LATE):
+            o = -OWN if own else NL - OWN - LATE
+            return "fb", lo + o, hi + o
 
-    def SD(offs, src, b):
+    def old(t, own, lo, hi):
+        src, span = by("domt", ("offa%d" if own else "ino%d") % t, lo, hi)
+        m, keep = ("m%d" % t, "mo") if own else ("inm%d" % t, "mr")
+        out = summed(t, own, lo, hi)
+        if out:
+            op("v", lambda: V.tensor_tensor(T.fb[:, out[1]:out[2]], src, T[m][:, lo:hi], A.max), r=["domt", span, (m, lo, hi)], w=[out])
+        else:
+            gather("a", T[keep][:, lo:hi], src, ["domt", span], [(keep, lo, hi)])
+
+    def SD(t, own, b):
         lo, hi = BLK[b]
-        out, span = by("domt", offs, lo, hi)
-        op("v", lambda: V.tensor_copy(out, T[src][:, lo:hi]), r=[span, (src, lo, hi)], w=["domt"])
+        out, span = by("domt", ("offa%d" if own else "ino%d") % t, lo, hi)
+        m, keep = ("m%d" % t, "mo") if own else ("inm%d" % t, "mr")
+        src = summed(t, own, lo, hi) or (own and (lo < OWN or not rmw(t)) and (m, lo, hi))
+        if src:
+            op("v", lambda: V.tensor_copy(out, T[src[0]][:, src[1]:src[2]]), r=[span, src], w=["domt"])
+        else:
+            op("v", lambda: V.tensor_tensor(out, T[keep][:, lo:hi], T[m][:, lo:hi], A.max), r=[span, (keep, lo, hi), (m, lo, hi)], w=["domt"])
 
     def SEND(t, j):
         dst = T.cores[(rank + 1 + t % (N - 1)) % N]
@@ -351,14 +370,8 @@ def rank_program(g, core, T, topo):
             g.remote_dma(T[land][:, lo:hi], T[src][:, lo:hi], T.sem[sem], T.sem.loc, pid, rid, topo.mask(core, dst))
         op("p", call, r=[(src, lo, hi)], sem="loc", n=len(topo.engines(core, dst)))
         count[sem] = len(topo.engines(T.cores[(rank - 1 - t % (N - 1)) % N], core))
-        done.append(("far", sem, count[sem], [], [(land, lo, hi)]))
+        done.append(("far", sem, count[sem], [], [(land, lo, hi)], {land}))
         TAG.append((TAG[0][0], "far", [], [(land, lo, hi)]))
-
-    def RG(t, j):
-        lo, hi = SENDS[j]
-        src, span = by("domt", "ino%d" % t, lo, hi)
-        op("v", lambda: V.tensor_tensor(T.mr[:, lo:hi], src, T["inm%d" % t][:, lo:hi], A.min),
-           r=["domt", span, ("inm%d" % t, lo, hi)], w=[("mr", lo, hi)])
 
     def turned_sum(j, tab, n, bank, out, w):
         if j == 0:
@@ -371,36 +384,35 @@ def rank_program(g, core, T, topo):
         else:
             op("a", lambda: S.activation(out, T[bank][:, 256:257], F.Copy), r=[bank], w=w)
 
+    late = [(True,) + SENDS[LAST]] + [(False,) + p for p in SENDS if p[0] >= LATE]
+    c0 = 2 * NL - OWN - LATE
+
     def END(n, t):
-        lo, hi = SENDS[LAST]
-        nl = hi - lo
-        src, span = by("domt", "ino%d" % t, lo, hi)
         if n == "YV":
-            op("s", lambda: g.sync.dma_start(T.yv[:], T["m%d" % t][:]), r=["m%d" % t], sem="st0", n=16)
+            flip("a", T.yb[:], T["m%d" % t][:], ["m%d" % t], ["yb"])
+            op("s", lambda: g.sync.dma_start(T.yv[:], T.yb[:]), r=["yb"], sem="st0", n=16)
         elif n in ("SV", "SW", "SX"):
             turned_sum("VWX".index(n[1]), "valt", NV, "sp", T.yss[:, 1:2], [("yss", 1, 2)])
         elif n == "Z0":
-            op("v", lambda: V.memset(T.domt[:, 0:DC], 0.0), w=[("domt", 0, DC)])
-        elif n in ("SP", "SQ", "SR"):
-            turned_sum("PQR".index(n[1]), "domt", SUMS[0], "dd0", T.fb[:, nl + 3:nl + 4], [("fb", nl + 3, nl + 4)])
+            op("v", lambda: V.memset(T.domt[:, 0:DC], TOP), w=[("domt", 0, DC)])
         elif n == "SA":
-            op("a", lambda: S.activation(T.x0[:, SUMS[0]:SUMS[1]], T.domt[:, DC + SUMS[0]:DC + SUMS[1]], F.Copy, accum_out=T.fb[:, nl:nl + 1]),
-               r=[("domt", DC + SUMS[0], DC + SUMS[1])], w=["x0", ("fb", nl, nl + 1)])
+            op("a", lambda: S.activation(T.x0[:, SUMS[0]:SUMS[1]], T.domt[:, DC + SUMS[0]:DC + SUMS[1]], F.Copy, accum_out=T.fb[:, c0 + 1:c0 + 2]),
+               r=[("domt", DC + SUMS[0], DC + SUMS[1])], w=["x0", ("fb", c0 + 1, c0 + 2)])
         elif n == "SB":
-            op("v", lambda: V.tensor_reduce(T.fb[:, nl + 1:nl + 2], T.domt[:, DC + SUMS[1]:W], AxisListType.X, A.add),
-               r=[("domt", DC + SUMS[1], W)], w=[("fb", nl + 1, nl + 2)])
-        elif n == "SG":
-            op("a", lambda: S.activation(T.da[:, 0:nl], src, F.Copy, scale=-1.0, accum_out=T.fb[:, nl + 2:nl + 3]),
-               r=["domt", span], w=["da", ("fb", nl + 2, nl + 3)])
+            op("v", lambda: V.tensor_reduce(T.fb[:, c0 + 2:c0 + 3], T.domt[:, DC + SUMS[1]:W], AxisListType.X, A.add),
+               r=[("domt", DC + SUMS[1], W)], w=[("fb", c0 + 2, c0 + 3)])
+        elif n[:2] == "SG":
+            own, lo, hi = late[int(n[2])]
+            src, span = by("domt", ("offa%d" if own else "ino%d") % t, lo, hi)
+            c = c0 + 3 + int(n[2])
+            op("a", lambda: S.activation(T.db[:, 0:hi - lo], src, F.Copy, scale=-1.0, accum_out=T.fb[:, c:c + 1]),
+               r=["domt", span], w=["db", ("fb", c, c + 1)])
         elif n == "YT":
             for h in range(2):
-                op("t", lambda: PE.matmul(T.yq[0:8, 128 * h:128 * h + 128], T["ss%d" % h][:, SO + 16:SO + 136:17], T.identh[:], True, True),
+                op("t", lambda: PE.matmul(T.yq[0:8, 128 * h:128 * h + 128], T["ss%d" % h][:, 16:136:17], T.identh[:], True, True),
                    r=["ss%d" % h, "identh"], w=["yq"])
-        elif n == "RL":
-            op("v", lambda: V.tensor_tensor(T.fb[:, 0:nl], src, T["inm%d" % t][:, lo:hi], A.min),
-               r=["domt", span, ("inm%d" % t, lo, hi)], w=[("fb", 0, nl)])
         elif n == "Z3":
-            op("v", lambda: V.tensor_reduce(T.yss[:, 0:1], T.fb[:, 0:nl + 4], AxisListType.X, A.add), r=["fb"], w=[("yss", 0, 1)])
+            op("v", lambda: V.tensor_reduce(T.yss[:, 0:1], T.fb[:, 0:c0 + 3 + len(late)], AxisListType.X, A.add, negate=True), r=["fb"], w=[("yss", 0, 1)])
             op("s", lambda: g.sync.dma_start(T.ys[:], T.yss[:]), r=["yss"], sem="st2", n=16)
         else:
             op("a", lambda: S.activation(T.yts[:], T.yq[0:8, 0:NL], F.Identity, bias=MID), r=["yq"], w=["yts"])
@@ -408,9 +420,8 @@ def rank_program(g, core, T, topo):
 
     STEP = {"G": G, "S": SC, "K": KEY, "D": DS, "E": E, "U": U, "C": SG, "M": DM, "Aa": A1, "Ab": A2, "Ac": A3, "B": BC, "Q": BP,
             "P": PG, "F": PF}
-    ROUND = {"N": GM, "T": SEND, "R": RG, "W": SW, "J": DA, "H": HM,
-             "O": lambda t, b: SD("offa%d" % t, "mo" if BLK[b][0] >= SENDS[LAST][0] and "H0" in ORDER else "m%d" % t, b),
-             "I": lambda t, b: SD("ino%d" % t, "mr", b)}
+    ROUND = {"N": GM, "T": SEND, "W": SW, "J": DA, "H": lambda t, j: old(t, True, *SENDS[LAST]), "R": lambda t, j: old(t, False, *(RCUT if t < RO - 1 else RCUTL)[j]),
+             "O": lambda t, b: SD(t, True, b), "I": lambda t, b: SD(t, False, b)}
 
     def part(n, t):
         TAG[0][0] = (n, t)
@@ -421,13 +432,12 @@ def rank_program(g, core, T, topo):
             if last:
                 END(n, t)
         elif name in STEP:
-            if not (last and d[0] == 2):
+            if not (last and d[0] == 2) and (name, 2 * t + d[0]) != ("E", 0):
                 STEP[name](2 * t + d[0], *d[1:])
-        elif not (last and n in ("R%d" % LAST, "I%d" % (len(BLK) - 1))):
+        elif not (last and n == "I%d" % (len(BLK) - 1)):
             ROUND[name](t, d[0])
 
     consts()
-    consts2()
     for n in FIRST:
         if n in ORDER:
             part(n, -1)

@@ -1,3 +1,4 @@
+from concourse.bass import DstId, RemoteDMATransfer
 from concourse.mybir import AluOpType, AxisListType, ActivationFunctionType
 
 NV, NL, RO, N = 2560, 256, 4, 4
@@ -7,28 +8,28 @@ DW = 320
 MID = 1280.0
 FAR = 4096.0
 H = "float16"
-CUT = ((0, 72, 128, 192, 240, 256), (0, 56, 128, 192, 240, 256))
-CUTL = None
+CUT = ((0, 64, 128, 192, 238, 256), (0, 86, 128, 192, 224, 256))
+CUTL = ((0, 64, 128, 192, 238, 256), (0, 84, 128, 192, 224, 256))
 ONV = ((0,), (0,))
 SENDS = ((0, 64), (64, 128), (128, 192), (192, 256))
 BLK = ((0, 64), (64, 128), (128, 192), (192, 256))
 WBLK = ((0, 64), (64, 128), (128, 192), (192, 256))
-KCUT = ((0, 128), (128, 256), (256, 256))
+KCUT = (((0, 128), (128, 256)), ((0, 128), (128, 224), (224, 256)))
 RCUT = ((0, 128), (128, 256))
 RCUTL = ((0, 128), (128, 192), (192, 256))
-SUMS = (0, 1536)
-FLIP = 1280
+SUMS = (0, 1280)
+FLIP = 1408
 TOP = 255.0
 LOW = -5000.0
-LATE = 128
-ENG = {"U": "aaaa", "J": "a", "P": "aaaa", "F": "aavv", "B": "aaaa"}
+LATE = 192
+ENG = {"U": "aaaa", "J": "a", "P": "aaaa", "F": "pppp", "B": "aaaa", "Y": "ppppp"}
 ORDER = """
-Q01 P00 U01 F00 M00 P01 G01 F01 C01 G04 G02 G00 K00 S00 D00 Aa00 D01 Ab00 Ac00 E10 M01 B10 Q10 G03 S01 W0 S02 W1 S04 W2 S03 C10 U10 D12 P10 K01 W3 Aa01 Ab01 F10 Ac01 G11 G10 S11 S10 D13 E11 M10 B11 U11 Q11 P11 C11 G12 N0 K10 F11 O0 D14 N1 Aa10 O1 D15 G13 G14 S12 Ab10 N2 Ac10 M11 E20 K11 B20 T8 T9 T1 T2 T3 O2 S13 S14 Q20 N3 O3 Aa11 Ab11 R0 R1 C20 U20 Ac11 I0 I2 I1 T4 I3 E21 B21
+F00 M00 F01 G01 G02 G00 D04 S00 S01 K00 M01 Aa00 D05 Ab00 W0 Ac00 E10 G03 B10 Q10 S02 W1 G04 K01 S03 W2 U10 P10 C10 S04 W3 Aa01 D12 Ab01 D13 F10 Ac01 G11 G10 S11 M10 E11 B11 L0 U11 Q11 P11 C11 G12 K10 T8 F11 S10 Aa10 D14 Ab10 D15 Y0 O0 Ac10 T1 Y1 T9 M11 E20 G13 S12 O1 Y2 T2 K11 G14 K12 L1 B20 T3 Q20 X U20 C20 S13 S14 O2 N3 T4 Aa11 O3 R1 Ab11 Ac11 D22 R0 E21 I1 I2 B21 P20 Q21 D23 I0 U21 P21 C21 I3
 """.split()
 FINAL = """
-P00 U01 P01 F00 Q01 M00 F01 G01 C01 G04 G02 G00 M01 K00 S00 D00 Aa00 Ab00 D01 Ac00 E10 B10 Q10 G03 S01 W0 S02 W1 S04 W2 S03 U10 P10 C10 K01 W3 Aa01 G11 Ab01 Ac01 G10 D12 E11 B11 Q11 U11 P11 J0 C11 G12 G13 G14 S11 S10 D13 N1 N0 O0 D14 O1 D15 S12 F10 N2 F11 O2 Z0 S13 S14 T8 T2 T1 SV M10 K11 K10 R0 I0 N3 I1 SA SG0 T3 T9 Aa11 H0 SB Aa10 Ab11 Ab10 O3 Ac10 R1 SW SG1 M11 Ac11 I2 SX YV SG2 YT T4 R2 YU Z3
+F00 M00 F01 M01 G01 G02 G00 D04 S00 S01 K00 Aa00 W1 Ab00 D05 Ac00 E10 G03 B10 Q10 W0 S02 G04 K01 S03 W2 U10 P10 C10 S04 W3 Z0 Aa01 D12 Ab01 D13 F10 Ac01 G11 G10 S11 M10 E11 B11 H0 U11 Q11 P11 C11 G12 K10 T8 F11 G13 M11 SV K11 S10 D14 N0 Aa10 O0 Ab10 N1 D15 S12 O1 G14 K12 H1 T2 T9 T1 S13 N2 T3 S14 O2 N3 T4 O3 Aa11 Ac10 R0 R1 SW SX YV Ab11 I1 I0 I2 Ac11 YT SA SG0 YU SB R2 Z3
 """.split()
-FIRST = "B20 B21 Q20 Q21 U20 U21 P20 P21 F20 F21 M20 M21 C20 C21 D20 D21 D22 D23 D24 D25".split()
+FIRST = "B20 B21 B22 Q20 Q21 C20 C21 D20 D21 D22 D23 D24 D25 U20 U21 U22 P20 P21 P22 F20 F21 F22 M20 M21".split()
 ENDS = ("YV", "SV", "SW", "SX", "Z0", "SA", "SB", "SP", "SQ", "SR", "SG0", "SG1", "SG2", "SG3", "YT", "Z3", "YU")
 TAG = [[""]]
 
@@ -39,15 +40,18 @@ SCRATCH = {
     "zmin": ("sbuf", [128, 2048], "bfloat16"), "yb": ("sbuf", [128, NL], "bfloat16"),
     "pi": ("sbuf", [128, 8], "int32"), "pf": ("sbuf", [128, 16], "float32"),
     "jc": ("sbuf", [128, 128], "float32"), "jr": ("sbuf", [128, 16], "float32"), "jd": ("sbuf", [128, 136], "float32"),
-    "identb": ("sbuf", [128, 128], "bfloat16"), "mask": ("sbuf", [128, 16], "float32"),
+    "identb": ("sbuf", [128, 128], "bfloat16"), "ident": ("sbuf", [128, 128], "float32"), "mask": ("sbuf", [128, 16], "float32"),
     "ones": ("sbuf", [128, 2], "float32"), "sb": ("sbuf", [128, 128], "float32"),
     "g8": ("sbuf", [128, 16], "bfloat16"),
+    "dmf": ("sbuf", [128, 136], "float32"), "less": ("sbuf", [128, 136], H),
+    "pf0": ("sbuf", [128, NL], "float32"), "pf1": ("sbuf", [128, NL], "float32"),
     "dmat": ("sbuf", [128, 136], H), "t1": ("sbuf", [128, 144], H),
-    "rb": ("sbuf", [128, 136], "float32"),
+    "rb": ("sbuf", [128, 136], "float32"), "ll": ("sbuf", [128, 272], "float32"),
+    "ss0": ("sbuf", [128, 2432], H), "ss1": ("sbuf", [128, 2432], H), "lt": ("sbuf", [128, NL], H),
     "r2": ("sbuf", [128, DW], H), "identh": ("sbuf", [128, 128], H), "gs": ("sbuf", [128, 128], H),
     "jg": ("sbuf", [128, 128], "float32"), "nid": ("sbuf", [128, 8], "float32"),
     "zd": ("sbuf", [128, 2 * DW], "bfloat16"), "dsc": ("sbuf", [128, 2 * DW], "bfloat16"),
-    "endu": ("sbuf", [128, 2], "uint16"),
+    "endu": ("sbuf", [128, 4], "uint16"),
     "offc": ("sbuf", [128, 32], "uint16"), "mr": ("sbuf", [128, NL], "float32"),
     "da": ("sbuf", [128, 128], "float32"), "db": ("sbuf", [128, 128], "float32"), "mo": ("sbuf", [128, NL], "float32"),
     "yts": ("sbuf", [8, NL], "float32"), "yss": ("sbuf", [128, 2], "float32"), "fb": ("sbuf", [128, 336], "float32"),
@@ -61,14 +65,12 @@ for _k in range(2):
     SCRATCH["li%d" % _k] = ("sbuf", [128, 32], "uint16")
     SCRATCH["sg%d" % _k] = ("sbuf", [128, 2 * DW], "bfloat16")
     SCRATCH["mm%d" % _k] = ("sbuf", [128, 144], "float32")
-    SCRATCH["ll%d" % _k] = ("sbuf", [128, 136], "float32")
-    SCRATCH["ss%d" % _k] = ("sbuf", [128, 136], H)
-    SCRATCH["lt%d" % _k] = ("sbuf", [128, 128], H)
     for _n in ("kd", "lp", "dd"):
         SCRATCH["%s%d" % (_n, _k)] = ("psum", [128, 512], "float32")
 for _k in range(RO):
     SCRATCH["m%d" % _k] = ("sbuf", [128, NL], "float32")
     SCRATCH["offa%d" % _k] = ("sbuf", [128, 32], "uint16")
+    SCRATCH["dg%d" % _k] = ("sbuf", [128, NL], "float32")
     SCRATCH["inm%d" % _k] = ("sbuf", [128, NL], "float32")
     SCRATCH["ino%d" % _k] = ("sbuf", [128, 32], "uint16")
 
@@ -139,6 +141,7 @@ def rank_program(g, core, T, topo):
 
     fl = {"allow_small_or_imprecise_dtypes": True}
     zw = 16 * max(b - a for c in CUT + (CUTL or CUT) for a, b in zip(c[:-1], c[1:]))
+    zw = 2048 if "S09" in ORDER or "S19" in ORDER else zw
     segs = []
     for b in range(8):
         segs.append((segs[-1][1] if segs else 0, (segs[-1][1] if segs else 0) + 64 - 16 * (b % 4)))
@@ -186,25 +189,31 @@ def rank_program(g, core, T, topo):
         for k in range(2):
             op("v", lambda: ts(T.g8[:, 8 * k:8 * k + 8], T.jr[:, 0:8], T.pf[:, 2:3], A.is_equal, 1.0 - 2 * k, A.mult), r=["jr"] + pc, w=[("g8", 8 * k, 8 * k + 8)])
         op("v", lambda: V.tensor_tensor(T.dmat[:], T.t1[:, 0:136], T.t1[:, 1:137], A.subtract), r=["t1"], w=["dmat"])
+        for h in range(2):
+            op("v", lambda: V.memset(T["ss%d" % h][:, 1:2432:17], 0.0), w=["ss%d" % h])
+        if "p" in ENG["F"]:
+            op("v", lambda: V.tensor_tensor(T.dmf[:], T.t1[:, 0:136], T.t1[:, 1:137], A.subtract), r=["t1"], w=["dmf"])
+            fill("less", T.less[:], 0.0)
+            fill("less", T.less[:, 16:136:17], -MID)
         op("v", lambda: ts(T.pf[:, 8:9], T.pf[:, 3:4], -8.0, A.mult, 56.0, A.add), r=pc, w=[("pf", 8, 9)])
         op("v", lambda: ts(T.pf[:, 9:10], T.pf[:, 4:5], 160.0, A.mult, 63.0, A.add), r=pc, w=[("pf", 9, 10)])
-        op("v", lambda: V.memset(T.rb[:, 16:136:17], -10000.0), w=["rb"])
-        op("v", lambda: ts(T.pf[:, 10:11], T.pf[:, 8:9], T.pf[:, 3:4], A.mult, T.pf[:, 9:10], A.add), r=[("pf", 0, 10)], w=[("pf", 10, 11)])
-        op("v", lambda: V.memset(T.domt[:, 0:DC], TOP), w=[("domt", 0, DC)])
-        op("v", lambda: ts(T.endu[:], T.jr[:, 0:2], float(DW), A.mult, T.pf[:, 10:11], A.add), r=["jr", ("pf", 10, 11)], w=["endu"])
-        for c in range(4):
-            e = segs[c][1] - 1
-            op("v", lambda: ts(T.zd[:, e:DW:160], T.zd[:, e:DW:160], T.pf[:, 1:2], A.max, 16.0 * c, A.add), r=[("zd", e, e + 161)] + pc,
-               w=[("zd", e, e + 1), ("zd", e + 160, e + 161)])
-        op("v", lambda: V.tensor_copy(T.zd[:, DW:2 * DW], T.zd[:, 0:DW]), r=[("zd", 0, DW)], w=[("zd", DW, 2 * DW)])
-        op("a", lambda: S.activation(T.identb[:], T.identh[:], F.Copy), r=["identh"], w=["identb"])
-        fill("ones", T.ones[:], 1.0)
-        fill("fb", T.fb[:, c0:c0 + 1], -TOP * NV)
         flip("a", T.domt[:, DC:DC + FLIP], T.domb[:, 0:FLIP], ["domb"], [("domt", DC, DC + FLIP)])
         flip("v", T.domt[:, DC + FLIP:W], T.domb[:, FLIP:NV], ["domb"], [("domt", DC + FLIP, W)])
+        op("v", lambda: ts(T.pf[:, 10:11], T.pf[:, 8:9], T.pf[:, 3:4], A.mult, T.pf[:, 9:10], A.add), r=[("pf", 0, 10)], w=[("pf", 10, 11)])
+        for c in range(4):
+            ends = [("zd", e - 1, e) for e in (segs[c][1], segs[c + 4][1])]
+            view = T.zd[:, segs[c][1] - 1:DW:160]
+            op("v", lambda: ts(view, view, T.pf[:, 1:2], A.max, 16.0 * c, A.add), r=ends + pc, w=ends)
+        op("v", lambda: ts(T.endu[:, 0:2], T.jr[:, 0:2], float(DW), A.mult, T.pf[:, 10:11], A.add), r=["jr", ("pf", 10, 11)], w=[("endu", 0, 2)])
+        op("v", lambda: V.tensor_copy(T.zd[:, DW:2 * DW], T.zd[:, 0:DW]), r=[("zd", 0, DW)], w=[("zd", DW, 2 * DW)])
+        op("v", lambda: V.memset(T.rb[:, 16:136:17], -10000.0), w=["rb"])
+        op("v", lambda: V.memset(T.domt[:, 0:DC], TOP), w=[("domt", 0, DC)])
 
     def gather(q, out, src, r, w):
-        op(q, (lambda: S.activation(out, src, F.Copy)) if q == "a" else (lambda: V.tensor_copy(out, src)), r=r, w=w)
+        if q == "p":
+            op(q, lambda: g.affine_select(out, src, [[0, out.shape[1]]], A.is_ge, 0.0, 0, 0), r=r, w=w)
+        else:
+            op(q, (lambda: S.activation(out, src, F.Copy)) if q == "a" else (lambda: V.tensor_copy(out, src)), r=r, w=w)
 
     def flip(q, out, src, r, w):
         op(q, (lambda: S.activation(out, src, F.Identity, bias=TOP, scale=-1.0)) if q == "a" else (lambda: ts(out, src, -1.0, A.mult, TOP, A.add)), r=r, w=w)
@@ -213,26 +222,38 @@ def rank_program(g, core, T, topo):
         op(q, (lambda: S.activation(out, src, F.Identity, bias=c)) if q == "a" else (lambda: ts(out, src, c, A.add)), r=r, w=w)
 
     def by(tab, name, lo, hi):
-        a, b = lo // 16 + 8 * (lo // 128), hi // 16 + 8 * (lo // 128)
+        gap = 8 * (lo // 128)
+        a, b = lo // 16 + gap, hi // 16 + gap
         return T[tab][:, 0:W].indirect(T[name][:, a:b]), (name, a, b)
 
     def piece(s, j):
         return (CUTL if CUTL and s >= 2 * RO - 2 else CUT)[s % 2][j:j + 2]
 
-    def PG(s, h):
-        k, lo, hi = s % 2, 128 * h, 128 * h + 128
+    def halves(j, n):
+        return n * (j % 2), n * min(j + 1, 2)
+
+    def PG(s, j):
+        k, (lo, hi) = s % 2, halves(j, 128)
         tab = "oct" if k else "tpt"
         src, span = by(tab, "li%d" % k, lo, hi)
-        gather(ENG["P"][2 * k + h], T["pu%d" % k][:, lo:hi], src, [tab, span], [("pu%d" % k, lo, hi)])
+        gather(ENG["P"][2 * k + j % 2], T["pu%d" % k][:, lo:hi], src, [tab, span], [("pu%d" % k, lo, hi)])
 
-    def PF(s, h):
-        k, lo, hi = s % 2, 128 * h, 128 * h + 128
-        shift(ENG["F"][2 * k + h], T["pw%d" % k][:, lo:hi], T["pu%d" % k][:, lo:hi], -MID, [("pu%d" % k, lo, hi)], [("pw%d" % k, lo, hi)])
+    def PF(s, j):
+        k, (lo, hi) = s % 2, halves(j, 128)
+        if ENG["F"][2 * k + j] == "p":
+            op("p", lambda: g.affine_select(T["pf%d" % k][:, lo:hi], T["pu%d" % k][:, lo:hi], [[0, hi - lo]], A.is_ge, 0.0, 0, 0),
+               r=[("pu%d" % k, lo, hi)], w=[("pf%d" % k, lo, hi)])
+        else:
+            shift(ENG["F"][2 * k + j], T["pw%d" % k][:, lo:hi], T["pu%d" % k][:, lo:hi], -MID, [("pu%d" % k, lo, hi)], [("pw%d" % k, lo, hi)])
 
     def DM(s, h):
-        k = s % 2
-        op("t", lambda: PE.matmul(T["kd%d" % h][:, 256:392], T["pw%d" % k][:, 128 * h:128 * h + 128], T.dmat[:], True, True),
-           r=[("pw%d" % k, 128 * h, 128 * h + 128), "dmat"], w=[("kd%d" % h, 256, 392)])
+        k, lo, hi = s % 2, 128 * h, 128 * h + 128
+        out, w = T["kd%d" % h][:, 256:392], [("kd%d" % h, 256, 392)]
+        if ENG["F"][2 * k + h] == "p":
+            op("t", lambda: PE.matmul(out, T.identh[:], T.less[:], True, False), r=["identh", "less"], w=w)
+            op("t", lambda: PE.matmul(out, T["pf%d" % k][:, lo:hi], T.dmf[:], False, True), r=[("pf%d" % k, lo, hi), "dmf"], w=w)
+        else:
+            op("t", lambda: PE.matmul(out, T["pw%d" % k][:, lo:hi], T.dmat[:], True, True), r=[("pw%d" % k, lo, hi), "dmat"], w=w)
 
     def G(s, j):
         k = s % 2
@@ -243,57 +264,72 @@ def rank_program(g, core, T, topo):
 
     def SC(s, j):
         k = s % 2
-        lo, hi = piece(s, j)
+        lo, hi = (0, 128) if j == 9 else piece(s, j)
         op("v", lambda: V.tensor_tensor_scan(T["y%d" % k][:, 16 * lo:16 * hi], T.zmin[:, 0:16 * (hi - lo)], T["x%d" % k][:, 16 * lo:16 * hi],
                                              0.0, A.max, A.min), r=["zmin", ("x%d" % k, lo, hi)], w=[("y%d" % k, lo, hi)])
 
     def KEY(s, j):
         k = s % 2
-        lo, hi = KCUT[j]
+        lo, hi = KCUT[k][j]
         h = lo // 128
         for i in range(16):
-            op("t", lambda: PE.matmul(T["kd%d" % h][lo - 128 * h:hi - 128 * h, i:136:17], T["x%d" % k][:, 16 * lo + i:16 * hi:16], T.g8[:, 8 * k:8 * k + 8], True, True),
-               r=[("x%d" % k, lo, hi), "g8"], w=[("kd%d" % h, 0, 136)])
+            op("t", lambda: PE.matmul(T["kd%d" % h][lo - 128 * h:hi - 128 * h, i:136:17], T["x%d" % k][:, 16 * lo + i:16 * hi:16],
+                                      T.g8[:, 8 * k:8 * k + 8], True, True), r=[("x%d" % k, lo, hi), "g8"], w=[("kd%d" % h, 0, 136)])
 
     def A1(s, h):
         op("v", lambda: V.tensor_tensor_scan(T["mm%d" % h][:, 1:137], T.rb[:], T["kd%d" % h][:, 0:136], LOW, A.add, A.max),
            r=["rb", ("kd%d" % h, 0, 136)], w=["mm%d" % h])
 
     def A2(s, h):
-        op("v", lambda: V.tensor_tensor(T["ll%d" % h][:], T["kd%d" % h][:, 0:136], T["mm%d" % h][:, 0:136], A.is_le),
-           r=[("kd%d" % h, 0, 136), "mm%d" % h], w=["ll%d" % h])
+        lo, hi = halves(h, 136)
+        op("v", lambda: V.tensor_tensor(T.ll[:, lo:hi], T["kd%d" % h][:, 0:136], T["mm%d" % h][:, 0:136], A.is_le),
+           r=[("kd%d" % h, 0, 136), "mm%d" % h], w=[("ll", lo, hi)])
 
     def A3(s, h):
-        op("v", lambda: V.tensor_tensor_scan(T["ss%d" % h][:], T["kd%d" % h][:, 256:392], T["ll%d" % h][:], 0.0, A.add, A.mult),
-           r=[("kd%d" % h, 256, 392), "ll%d" % h], w=["ss%d" % h])
+        lo, hi = halves(h, 136)
+        op("v", lambda: V.tensor_tensor_scan(T["ss%d" % h][:, 0:2176:16], T["kd%d" % h][:, 256:392], T.ll[:, lo:hi], 0.0, A.add, A.mult),
+           r=[("kd%d" % h, 256, 392), ("ll", lo, hi)], w=["ss%d" % h])
+
+    def chosen(h):
+        return T["ss%d" % h][:, 256:2176:272]
+
+    def direct(s, h):
+        return "V1%d" % h in ORDER if s % 2 else "V2%d" % h in ORDER or "V0%d" % h in ORDER
+
+    def LV(s, h):
+        k = s % 2
+        for r in range(16) if s else ():
+            op("t", lambda: PE.matmul(T["lp%d" % k][:, 8 * h:8 * h + 8], T["ss%d" % h][:, 256 - 17 * r:2432 - 17 * r:17], T.identh[:, r:128:16],
+                                      r == 0, r == 15), r=["ss%d" % h, "identh"], w=[("lp%d" % k, 8 * h, 8 * h + 8)])
 
     def E(s, h):
-        ss, dd = T["ss%d" % h], T["dd%d" % h]
+        (lo, hi), dd = halves(h, 136), T["dd%d" % h]
         for r in range(16):
-            op("t", lambda: PE.matmul(dd[0:8, DW + r:DW + 128:16], T.identh[:, r:128:16], ss[:, 16:136:17], True, True),
+            op("t", lambda: PE.matmul(dd[0:8, DW + r:DW + 128:16], T.identh[:, r:128:16], chosen(h), True, True),
                r=["ss%d" % h, "identh"], w=[("dd%d" % h, DW, DW + 128)])
-        op("t", lambda: PE.matmul(dd[32:40, DW:DW + 128], ss[:, 16:136:17], T.identh[:], True, True),
+        op("t", lambda: PE.matmul(dd[32:40, DW:DW + 128], chosen(h), T.identh[:], True, True),
            r=["ss%d" % h, "identh"], w=[("dd%d" % h, DW, DW + 128)])
 
-    def BC(s, h):
-        k = s % 2
-        gather(ENG["B"][2 * k + h], T["lt%d" % h][0:40, :], T["dd%d" % h][0:40, DW:DW + 128], [("dd%d" % h, DW, DW + 128)], ["lt%d" % h])
-        if s:
-            op("t", lambda: PE.matmul(T["lp%d" % k][:, 8 * h:8 * h + 8], T["lt%d" % h][0:40, :], T.identh[0:40, 0:8], True, True),
-               r=["lt%d" % h, "identh"], w=[("lp%d" % k, 8 * h, 8 * h + 8)])
+    def BC(s, j):
+        k, (lo, hi) = s % 2, halves(j, 128)
+        gather(ENG["B"][2 * k + j], T.lt[0:40, lo:hi], T["dd%d" % j][0:40, DW:DW + 128], [("dd%d" % j, DW, DW + 128)], [("lt", lo, hi)])
+        for h in range(*halves(j, 1)) if s and not direct(s, j) else ():
+            op("t", lambda: PE.matmul(T["lp%d" % k][:, 8 * h:8 * h + 8], T.lt[0:40, 128 * h:128 * h + 128], T.identh[0:40, 0:8], True, True),
+               r=[("lt", lo, hi), "identh"], w=[("lp%d" % k, 8 * h, 8 * h + 8)])
 
-    def U(s, h):
-        k = s % 2
+    def U(s, j):
+        k, (lo, hi) = s % 2, halves(j, 8)
+        a = 2 * lo
         if s:
-            shift(ENG["U"][2 * k + h], T["li%d" % k][:, 16 * h:16 * h + 8], T["lp%d" % k][:, 8 * h:8 * h + 8], MID + DC,
-                  [("lp%d" % k, 8 * h, 8 * h + 8)], [("li%d" % k, 16 * h, 16 * h + 8)])
+            shift(ENG["U"][2 * k + j % 2], T["li%d" % k][:, a:a + hi - lo], T["lp%d" % k][:, lo:hi], MID + DC,
+                  [("lp%d" % k, lo, hi)], [("li%d" % k, a, a + hi - lo)])
 
     def BP(s, h):
-        lt, dd = T["lt%d" % h], T["dd%d" % h]
-        op("t", lambda: PE.matmul(dd[:, 0:DW], lt[0:40, :], T.r2[0:40, :], True, False), r=["lt%d" % h, "r2"], w=[("dd%d" % h, 0, DW)])
+        dd, a = T["dd%d" % h], 128 * h
+        op("t", lambda: PE.matmul(dd[:, 0:DW], T.lt[0:40, a:a + 128], T.r2[0:40, :], True, False), r=[("lt", a, a + 128), "r2"], w=[("dd%d" % h, 0, DW)])
         for b, (lo, hi) in enumerate(segs):
-            op("t", lambda: PE.matmul(dd[:, lo:hi], T.gs[0:40, :], lt[0:40, 16 * b:16 * b + hi - lo], False, b == 7),
-               r=["lt%d" % h, "gs"], w=[("dd%d" % h, 0, DW)])
+            op("t", lambda: PE.matmul(dd[:, lo:hi], T.gs[0:40, :], T.lt[0:40, a + 16 * b:a + 16 * b + hi - lo], False, b == 7),
+               r=[("lt", a, a + 128), "gs"], w=[("dd%d" % h, 0, DW)])
 
     def SG(s, h):
         k = s % 2
@@ -309,8 +345,10 @@ def rank_program(g, core, T, topo):
             op("v", lambda: V.tensor_tensor_scan(T.dsc[:, lo:hi], T["sg%d" % k][:, lo:hi], T.zd[:, lo:hi], 1.0, A.min, A.max),
                r=[("sg%d" % k, lo, hi), "zd"], w=[("dsc", lo, hi)])
         else:
-            op("v", lambda: V.tensor_tensor(T[off][:, 16 * h0:16 * h1], T.dsc[:, lo:hi].indirect(T.endu[:, 0:h1 - h0]), T["li%d" % k][:, 16 * h0:16 * h1], A.min),
-               r=[("dsc", lo, hi), "endu", ("li%d" % k, 16 * h0, 16 * h1)], w=[(off, 16 * h0, 16 * h1)])
+            a, b = 16 * h0, 16 * h1
+            ends = T.endu[:, 0:h1 - h0]
+            op("v", lambda: V.tensor_tensor(T[off][:, a:b], T.dsc[:, lo:hi].indirect(ends), T["li%d" % k][:, a:b], A.min),
+               r=[("dsc", lo, hi), "endu", ("li%d" % k, a, b)], w=[(off, a, b)])
 
     def SW(t, b):
         lo, hi = WBLK[b]
@@ -322,6 +360,17 @@ def rank_program(g, core, T, topo):
 
     def rmw(t):
         return "J0" in (ORDER if t < RO - 1 else FINAL)
+
+    def folds(t):
+        return "Y0" in (ORDER if t < RO - 1 else FINAL)
+
+    def DG(t, h):
+        src, span = by("domt", "li1", 128 * h, 128 * h + 128)
+        gather("a", T["dg%d" % t][:, 128 * h:128 * h + 128], src, ["domt", span], [("dg%d" % t, 128 * h, 128 * h + 128)])
+
+    def YC(t, j):
+        lo, hi = SENDS[j]
+        gather(ENG["Y"][j], T["m%d" % t][:, lo:hi], T.y1[:, 16 * lo + 15:16 * hi:16], [("y1", lo, hi)], [("m%d" % t, lo, hi)])
 
     def DA(t, j):
         lo, hi = SENDS[LAST]
@@ -336,8 +385,8 @@ def rank_program(g, core, T, topo):
            r=(["da"] if kept else ["domt", span]) + [("y1", lo, hi)], w=[("m%d" % t, lo, hi)])
 
     def summed(t, own, lo, hi):
-        if t == RO - 1 and (lo >= OWN if own else lo >= LATE):
-            o = -OWN if own else NL - OWN - LATE
+        if t == RO - 1 and (lo >= OWN and rmw(t) if own else lo >= LATE):
+            o = -OWN if own else (NL - OWN) * rmw(t) - LATE
             return "fb", lo + o, hi + o
 
     def old(t, own, lo, hi):
@@ -350,10 +399,14 @@ def rank_program(g, core, T, topo):
             gather("a", T[keep][:, lo:hi], src, ["domt", span], [(keep, lo, hi)])
 
     def SD(t, own, b):
-        lo, hi = BLK[b]
+        lo, hi = (BLK if own else SENDS)[b]
         out, span = by("domt", ("offa%d" if own else "ino%d") % t, lo, hi)
         m, keep = ("m%d" % t, "mo") if own else ("inm%d" % t, "mr")
         src = summed(t, own, lo, hi) or (own and (lo < OWN or not rmw(t)) and (m, lo, hi))
+        if own and t == RO - 1 and "H1" in FINAL:
+            src = None
+        if own and folds(t) and "Y%d" % b in ORDER:
+            src, keep = None, "dg%d" % t
         if src:
             op("v", lambda: V.tensor_copy(out, T[src[0]][:, src[1]:src[2]]), r=[span, src], w=["domt"])
         else:
@@ -366,35 +419,44 @@ def rank_program(g, core, T, topo):
         lo, hi = {0: (0, 24), 8: (0, 8), 9: (16, 24)}[j] if j in (0, 8, 9) else SENDS[j - 1]
         sem = "in%d_%d" % (t, j)
 
+        both = folds(t) and "Y%d" % (j - 1) in ORDER
+
         def call():
-            g.remote_dma(T[land][:, lo:hi], T[src][:, lo:hi], T.sem[sem], T.sem.loc, pid, rid, topo.mask(core, dst))
-        op("p", call, r=[(src, lo, hi)], sem="loc", n=len(topo.engines(core, dst)))
+            if both:
+                g.remote_dma_fused([RemoteDMATransfer(dst_ids=[DstId(rid=rid, pnc=pid)], dma_engine_mask=topo.mask(core, dst), remote_sem=T.sem[sem],
+                                                      srcs=[T[src][:, lo:hi], T["dg%d" % t][:, lo:hi]], dsts=[T[land][:, lo:hi]], alu_op=2)],
+                                   local_sem=T.sem.loc)
+            else:
+                g.remote_dma(T[land][:, lo:hi], T[src][:, lo:hi], T.sem[sem], T.sem.loc, pid, rid, topo.mask(core, dst))
+        op("p", call, r=[(src, lo, hi)] + [("dg%d" % t, lo, hi)] * both, sem="loc", n=len(topo.engines(core, dst)))
         count[sem] = len(topo.engines(T.cores[(rank - 1 - t % (N - 1)) % N], core))
         done.append(("far", sem, count[sem], [], [(land, lo, hi)], {land}))
         TAG.append((TAG[0][0], "far", [], [(land, lo, hi)]))
 
-    def turned_sum(j, tab, n, bank, out, w):
+    def turned_sum(j, tab, ident, n, bank, out, w):
         if j == 0:
             for c in range(n // 128):
-                op("t", lambda: PE.matmul(T[bank][:, 0:128], T[tab][:, DC + 128 * c:DC + 128 * c + 128], T.identb[:], c == 0, c == n // 128 - 1),
-                   r=[(tab, DC, DC + n), "identb"], w=[bank])
+                op("t", lambda: PE.matmul(T[bank][:, 0:128], T[tab][:, DC + 128 * c:DC + 128 * c + 128], T[ident][:], c == 0, c == n // 128 - 1),
+                   r=[(tab, DC, DC + n), ident], w=[bank])
         elif j == 1:
             op("a", lambda: S.activation(T.sb[:], T[bank][:, 0:128], F.Copy), r=[bank], w=["sb"])
             op("t", lambda: PE.matmul(T[bank][:, 256:258], T.sb[:], T.ones[:], True, True), r=["sb", "ones"], w=[bank])
         else:
             op("a", lambda: S.activation(out, T[bank][:, 256:257], F.Copy), r=[bank], w=w)
 
-    late = [(True,) + SENDS[LAST]] + [(False,) + p for p in SENDS if p[0] >= LATE]
-    c0 = 2 * NL - OWN - LATE
+    late = [(True,) + SENDS[LAST]] * rmw(RO - 1) + [(False,) + p for p in SENDS if p[0] >= LATE]
+    c0 = (NL - OWN) * rmw(RO - 1) + NL - LATE
 
     def END(n, t):
         if n == "YV":
             flip("a", T.yb[:], T["m%d" % t][:], ["m%d" % t], ["yb"])
             op("s", lambda: g.sync.dma_start(T.yv[:], T.yb[:]), r=["yb"], sem="st0", n=16)
         elif n in ("SV", "SW", "SX"):
-            turned_sum("VWX".index(n[1]), "valt", NV, "sp", T.yss[:, 1:2], [("yss", 1, 2)])
+            turned_sum("VWX".index(n[1]), "valt", "identb", NV, "sp", T.yss[:, 1:2], [("yss", 1, 2)])
+        elif n in ("SP", "SQ", "SR"):
+            turned_sum("PQR".index(n[1]), "domt", "ident", SUMS[0], "lp0", T.fb[:, c0 + 6:c0 + 7], [("fb", c0 + 6, c0 + 7)])
         elif n == "Z0":
-            op("v", lambda: V.memset(T.domt[:, 0:DC], TOP), w=[("domt", 0, DC)])
+            op("p", lambda: g.iota(T.domt[:, 0:DC], [[0, DC]], int(TOP), 0, **fl), w=[("domt", 0, DC)])
         elif n == "SA":
             op("a", lambda: S.activation(T.x0[:, SUMS[0]:SUMS[1]], T.domt[:, DC + SUMS[0]:DC + SUMS[1]], F.Copy, accum_out=T.fb[:, c0 + 1:c0 + 2]),
                r=[("domt", DC + SUMS[0], DC + SUMS[1])], w=["x0", ("fb", c0 + 1, c0 + 2)])
@@ -409,18 +471,18 @@ def rank_program(g, core, T, topo):
                r=["domt", span], w=["db", ("fb", c, c + 1)])
         elif n == "YT":
             for h in range(2):
-                op("t", lambda: PE.matmul(T.yq[0:8, 128 * h:128 * h + 128], T["ss%d" % h][:, 16:136:17], T.identh[:], True, True),
+                op("t", lambda: PE.matmul(T.yq[0:8, 128 * h:128 * h + 128], chosen(h), T.identh[:], True, True),
                    r=["ss%d" % h, "identh"], w=["yq"])
         elif n == "Z3":
-            op("v", lambda: V.tensor_reduce(T.yss[:, 0:1], T.fb[:, 0:c0 + 3 + len(late)], AxisListType.X, A.add, negate=True), r=["fb"], w=[("yss", 0, 1)])
+            op("v", lambda: V.tensor_reduce(T.yss[:, 0:1], T.fb[:, 0:c0 + 7], AxisListType.X, A.add, negate=True), r=["fb"], w=[("yss", 0, 1)])
             op("s", lambda: g.sync.dma_start(T.ys[:], T.yss[:]), r=["yss"], sem="st2", n=16)
         else:
             op("a", lambda: S.activation(T.yts[:], T.yq[0:8, 0:NL], F.Identity, bias=MID), r=["yq"], w=["yts"])
             op("a", lambda: S.dma_start(T.yt[:], T.yts[:]), r=["yts"], sem="st1", n=16)
 
     STEP = {"G": G, "S": SC, "K": KEY, "D": DS, "E": E, "U": U, "C": SG, "M": DM, "Aa": A1, "Ab": A2, "Ac": A3, "B": BC, "Q": BP,
-            "P": PG, "F": PF}
-    ROUND = {"N": GM, "T": SEND, "W": SW, "J": DA, "H": lambda t, j: old(t, True, *SENDS[LAST]), "R": lambda t, j: old(t, False, *(RCUT if t < RO - 1 else RCUTL)[j]),
+            "P": PG, "F": PF, "V": LV}
+    ROUND = {"L": DG, "Y": YC, "N": GM, "T": SEND, "W": SW, "J": DA, "H": lambda t, j: old(t, True, *(SENDS[LAST] if rmw(t) else halves(j, 128))), "R": lambda t, j: old(t, False, *(RCUT if t < RO - 1 else RCUTL)[j]),
              "O": lambda t, b: SD(t, True, b), "I": lambda t, b: SD(t, False, b)}
 
     def part(n, t):
@@ -431,10 +493,18 @@ def rank_program(g, core, T, topo):
         if n in ENDS:
             if last:
                 END(n, t)
+        elif n == "X":
+            if t == 0:
+                op("a", lambda: S.activation(T.identb[:], T.identh[:], F.Copy), r=["identh"], w=["identb"])
+                fill("ones", T.ones[:], 1.0)
+                fill("fb", T.fb[:, c0:c0 + 1], -TOP * NV)
+            if t == 1:
+                op("a", lambda: S.activation(T.ident[:], T.identh[:], F.Copy), r=["identh"], w=["ident"])
+                fill("fb", T.fb[:, c0 + 1:c0 + 7], 0.0)
         elif name in STEP:
             if not (last and d[0] == 2) and (name, 2 * t + d[0]) != ("E", 0):
                 STEP[name](2 * t + d[0], *d[1:])
-        elif not (last and n == "I%d" % (len(BLK) - 1)):
+        elif not (last and n == "I%d" % LAST):
             ROUND[name](t, d[0])
 
     consts()

from concourse.bass import DstId, RemoteDMATransfer
from concourse.mybir import AluOpType, AxisListType, ActivationFunctionType

NV, NL, RO, N = 2560, 256, 4, 4
DC = 64
W = DC + NV
DW = 320
MID = 1280.0
FAR = 4096.0
H = "float16"
CUT = ((0, 64, 128, 192, 238, 256), (0, 86, 128, 192, 224, 256))
CUTL = ((0, 64, 128, 192, 238, 256), (0, 84, 128, 192, 224, 256))
ONV = ((0,), (0,))
SENDS = ((0, 64), (64, 128), (128, 192), (192, 256))
BLK = ((0, 64), (64, 128), (128, 192), (192, 256))
WBLK = ((0, 64), (64, 128), (128, 192), (192, 256))
KCUT = (((0, 128), (128, 256)), ((0, 128), (128, 224), (224, 256)))
RCUT = ((0, 128), (128, 256))
RCUTL = ((0, 128), (128, 192), (192, 256))
SUMS = (0, 1280)
FLIP = 1408
TOP = 255.0
LOW = -5000.0
LATE = 192
ENG = {"U": "aaaa", "J": "a", "P": "aaaa", "F": "pppp", "B": "aaaa", "Y": "ppppp"}
ORDER = """
F00 M00 F01 G01 G02 G00 D04 S00 S01 K00 M01 Aa00 D05 Ab00 W0 Ac00 E10 G03 B10 Q10 S02 W1 G04 K01 S03 W2 U10 P10 C10 S04 W3 Aa01 D12 Ab01 D13 F10 Ac01 G11 G10 S11 M10 E11 B11 L0 U11 Q11 P11 C11 G12 K10 T8 F11 S10 Aa10 D14 Ab10 D15 Y0 O0 Ac10 T1 Y1 T9 M11 E20 G13 S12 O1 Y2 T2 K11 G14 K12 L1 B20 T3 Q20 X U20 C20 S13 S14 O2 N3 T4 Aa11 O3 R1 Ab11 Ac11 D22 R0 E21 I1 I2 B21 P20 Q21 D23 I0 U21 P21 C21 I3
""".split()
FINAL = """
F00 M00 F01 M01 G01 G02 G00 D04 S00 S01 K00 Aa00 W1 Ab00 D05 Ac00 E10 G03 B10 Q10 W0 S02 G04 K01 S03 W2 U10 P10 C10 S04 W3 Z0 Aa01 D12 Ab01 D13 F10 Ac01 G11 G10 S11 M10 E11 B11 H0 U11 Q11 P11 C11 G12 K10 T8 F11 G13 M11 SV K11 S10 D14 N0 Aa10 O0 Ab10 N1 D15 S12 O1 G14 K12 H1 T2 T9 T1 S13 N2 T3 S14 O2 N3 T4 O3 Aa11 Ac10 R0 R1 SW SX YV Ab11 I1 I0 I2 Ac11 YT SA SG0 YU SB R2 Z3
""".split()
FIRST = "B20 B21 B22 Q20 Q21 C20 C21 D20 D21 D22 D23 D24 D25 U20 U21 U22 P20 P21 P22 F20 F21 F22 M20 M21".split()
ENDS = ("YV", "SV", "SW", "SX", "Z0", "SA", "SB", "SP", "SQ", "SR", "SG0", "SG1", "SG2", "SG3", "YT", "Z3", "YU")
TAG = [[""]]

SCRATCH = {
    "domb": ("sbuf", [128, NV], "bfloat16"), "domt": ("sbuf", [128, W], "float32"), "valt": ("sbuf", [128, W], "bfloat16"),
    "tpt": ("sbuf", [128, W], "int32"), "oct": ("sbuf", [128, W], "int32"),
    "qi": ("sbuf", [128, 16], "int32"), "qh": ("sbuf", [128, 16], H),
    "zmin": ("sbuf", [128, 2048], "bfloat16"), "yb": ("sbuf", [128, NL], "bfloat16"),
    "pi": ("sbuf", [128, 8], "int32"), "pf": ("sbuf", [128, 16], "float32"),
    "jc": ("sbuf", [128, 128], "float32"), "jr": ("sbuf", [128, 16], "float32"), "jd": ("sbuf", [128, 136], "float32"),
    "identb": ("sbuf", [128, 128], "bfloat16"), "ident": ("sbuf", [128, 128], "float32"), "mask": ("sbuf", [128, 16], "float32"),
    "ones": ("sbuf", [128, 2], "float32"), "sb": ("sbuf", [128, 128], "float32"),
    "g8": ("sbuf", [128, 16], "bfloat16"),
    "dmf": ("sbuf", [128, 136], "float32"), "less": ("sbuf", [128, 136], H),
    "pf0": ("sbuf", [128, NL], "float32"), "pf1": ("sbuf", [128, NL], "float32"),
    "dmat": ("sbuf", [128, 136], H), "t1": ("sbuf", [128, 144], H),
    "rb": ("sbuf", [128, 136], "float32"), "ll": ("sbuf", [128, 272], "float32"),
    "ss0": ("sbuf", [128, 2432], H), "ss1": ("sbuf", [128, 2432], H), "lt": ("sbuf", [128, NL], H),
    "r2": ("sbuf", [128, DW], H), "identh": ("sbuf", [128, 128], H), "gs": ("sbuf", [128, 128], H),
    "jg": ("sbuf", [128, 128], "float32"), "nid": ("sbuf", [128, 8], "float32"),
    "zd": ("sbuf", [128, 2 * DW], "bfloat16"), "dsc": ("sbuf", [128, 2 * DW], "bfloat16"),
    "endu": ("sbuf", [128, 4], "uint16"),
    "offc": ("sbuf", [128, 32], "uint16"), "mr": ("sbuf", [128, NL], "float32"),
    "da": ("sbuf", [128, 128], "float32"), "db": ("sbuf", [128, 128], "float32"), "mo": ("sbuf", [128, NL], "float32"),
    "yts": ("sbuf", [8, NL], "float32"), "yss": ("sbuf", [128, 2], "float32"), "fb": ("sbuf", [128, 336], "float32"),
    "yq": ("psum", [128, 512], "float32"), "sp": ("psum", [128, 512], "float32"),
}
for _k in range(2):
    SCRATCH["x%d" % _k] = ("sbuf", [128, 16 * NL], "bfloat16")
    SCRATCH["y%d" % _k] = ("sbuf", [128, 16 * NL], "bfloat16")
    SCRATCH["pu%d" % _k] = ("sbuf", [128, NL], "uint16")
    SCRATCH["pw%d" % _k] = ("sbuf", [128, NL], H)
    SCRATCH["li%d" % _k] = ("sbuf", [128, 32], "uint16")
    SCRATCH["sg%d" % _k] = ("sbuf", [128, 2 * DW], "bfloat16")
    SCRATCH["mm%d" % _k] = ("sbuf", [128, 144], "float32")
    for _n in ("kd", "lp", "dd"):
        SCRATCH["%s%d" % (_n, _k)] = ("psum", [128, 512], "float32")
for _k in range(RO):
    SCRATCH["m%d" % _k] = ("sbuf", [128, NL], "float32")
    SCRATCH["offa%d" % _k] = ("sbuf", [128, 32], "uint16")
    SCRATCH["dg%d" % _k] = ("sbuf", [128, NL], "float32")
    SCRATCH["inm%d" % _k] = ("sbuf", [128, NL], "float32")
    SCRATCH["ino%d" % _k] = ("sbuf", [128, 32], "uint16")

SEMAPHORES = (["v", "a", "t", "p", "loc"] + ["ld%d" % k for k in range(5)] + ["st%d" % k for k in range(3)]
              + ["in%d_%d" % (t, k) for t in range(RO) for k in range(10)])
PSUM = ("yq", "sp", "kd0", "kd1", "lp0", "lp1", "dd0", "dd1")
BIG = 1 << 20
A = AluOpType
F = ActivationFunctionType


def rank_program(g, core, T, topo):
    rank = T.rank_of(core)
    if rank is None:
        return
    Q = {"v": g.vector, "a": g.scalar, "t": g.tensor, "p": g, "s": g.sync}
    V, S, PE = g.vector, g.scalar, g.tensor
    done = []
    count = {}
    waited = {k: {} for k in Q}

    def spans(xs):
        return [(x, 0, BIG) if isinstance(x, str) else x for x in xs]

    def meet(xs, ys):
        return any(a[0] == b[0] and a[1] < b[2] and b[1] < a[2] for a in xs for b in ys)

    def op(q, call, r=(), w=(), sem=None, n=1):
        r, w = spans(r), spans(w)
        banks = [(x[0], 0, BIG) for x in r + w if x[0] in PSUM]
        names = {x[0] for x in r + w}
        need = {}
        for (q0, s0, c0, r0, w0, names0) in done:
            if names.isdisjoint(names0):
                continue
            dep = meet(r, w0) or meet(w, w0) or meet(w, r0)
            if q0 == q and s0 == q:
                dep = dep and q != "t"
            else:
                dep = dep or meet(banks, r0 + w0)
            if dep:
                need[s0] = max(need.get(s0, 0), c0)
        for s0, c0 in need.items():
            if waited[q].get(s0, 0) < c0:
                Q[q].wait_ge(T.sem[s0], c0)
                waited[q][s0] = c0
        sem = sem or q
        count[sem] = count.get(sem, 0) + n
        ins = call()
        if ins is not None:
            ins.then_inc(T.sem[sem], n)
        done.append((q, sem, count[sem], r, w, names))
        TAG.append((TAG[0][0], q, r, w))

    def ts(out, in0, s1, o0, s2=None, o1=None):
        if o1 is None:
            return V.tensor_scalar(out, in0, s1, None, o0)
        return V.tensor_scalar(out, in0, s1, s2, o0, o1)

    def fill(name, ap, c):
        op("a", lambda: S.activation(ap, T.jd[0:ap.shape[0], 0:ap.shape[1]], F.Identity, bias=c, scale=0.0), r=["jd"], w=[name])

    op("a", lambda: S.dma_start(T.qi[:], T.q[:]), w=["qi"], sem="ld0", n=16)
    op("s", lambda: g.sync.dma_start(T.domb[:], T.dom[:]), w=["domb"], sem="ld2", n=16)
    op("s", lambda: g.sync.dma_start(T.tpt[:, DC:W], T.tp[:]), w=[("tpt", DC, W)], sem="ld1", n=16)
    op("s", lambda: g.sync.dma_start(T.valt[:, DC:W], T.val[:]), w=[("valt", DC, W)], sem="ld4", n=16)
    op("s", lambda: g.sync.dma_start(T.oct[:, DC:W], T.oc[:]), w=[("oct", DC, W)], sem="ld3", n=16)

    fl = {"allow_small_or_imprecise_dtypes": True}
    zw = 16 * max(b - a for c in CUT + (CUTL or CUT) for a, b in zip(c[:-1], c[1:]))
    zw = 2048 if "S09" in ORDER or "S19" in ORDER else zw
    segs = []
    for b in range(8):
        segs.append((segs[-1][1] if segs else 0, (segs[-1][1] if segs else 0) + 64 - 16 * (b % 4)))
    pc = [("pf", 0, 5)]

    def consts():
        op("p", lambda: g.iota(T.pi[:, 0:1], [[0, 1]], 0, 1), w=[("pi", 0, 1)])
        op("p", lambda: g.iota(T.jd[:], [[16, 8], [1, 17]], 0, -1, **fl), w=["jd"])
        op("p", lambda: g.iota(T.jc[:], [[1, 128]], 0, -1, **fl), w=["jc"])
        op("p", lambda: g.iota(T.jr[:], [[1, 16]], 0, 0, **fl), w=["jr"])
        op("p", lambda: g.iota(T.jg[:], [[1, 8], [0, 16]], 32, -1, **fl), w=["jg"])
        op("p", lambda: g.iota(T.zmin[:, 0:zw], [[0, zw // 16], [-255, 16]], 255, 0, **fl), w=["zmin"])
        for k in range(2):
            op("v", lambda: V.memset(T["li%d" % k][:], 0), w=["li%d" % k])
        op("v", lambda: V.memset(T.zd[:, 0:DW], 0.0), w=["zd"])
        for j, (m, sh) in enumerate(((15, 0), (127, 4), (3, 0), (7, 2))):
            op("v", lambda: ts(T.pi[:, j + 1:j + 2], T.pi[:, 0:1], m, A.bitwise_and, sh, A.arith_shift_right), r=[("pi", 0, 1)], w=[("pi", j + 1, j + 2)])
        op("v", lambda: V.memset(T.rb[:], 0.0), w=["rb"])
        op("v", lambda: V.tensor_copy(T.pf[:, 0:5], T.pi[:, 0:5]), r=["pi"], w=[("pf", 0, 5)])
        op("v", lambda: ts(T.nid[:], T.jc[:, 0:8], 0.0, A.is_equal, -1.0, A.mult), r=["jc"], w=["nid"])
        op("v", lambda: ts(T.mask[:], T.jr[:], T.pf[:, 1:2], A.is_equal), r=["jr"] + pc, w=["mask"])
        op("v", lambda: ts(T.identh[:], T.jc[:], 0.0, A.is_equal), r=["jc"], w=["identh"])
        op("v", lambda: ts(T.t1[:, 1:137], T.jd[:], 0.0, A.is_equal), r=["jd"], w=["t1"])
        op("v", lambda: ts(T.gs[:], T.jg[:], 0.0, A.is_equal), r=["jg"], w=["gs"])
        op("v", lambda: V.memset(T.t1[:, 0:137:17], 0.0), w=["t1"])
        for h in range(2):
            fill("dd%d" % h, T["dd%d" % h][0:32, DW:DW + 128], 0.0)
            fill("mm%d" % h, T["mm%d" % h][:, 0:1], LOW)
            fill("kd%d" % h, T["kd%d" % h][:, 16:136:17], LOW)
        for b, (lo, hi) in enumerate(segs):
            op("a", lambda: S.activation(T.zd[:, lo:lo + 16], T.mask[:], F.Copy, scale=FAR), r=["mask"], w=[("zd", lo, lo + 16)])
        for b, (lo, hi) in enumerate(segs):
            op("a", lambda: S.activation(T.r2[:, lo:hi], T.jc[:, 0:hi - lo], F.Identity, bias=T.nid[:, b:b + 1], scale=0.0),
               r=["jc", "nid"], w=[("r2", lo, hi)])
        for h in range(2):
            op("v", lambda: ts(T.li0[:, 16 * h:16 * h + 8], T.qi[:, 8 * h:8 * h + 8], float(DC), A.add), r=["qi"], w=[("li0", 16 * h, 16 * h + 8)])
        op("v", lambda: ts(T.qh[:], T.qi[:], -MID, A.add), r=["qi"], w=["qh"])
        for h in range(2):
            dd = T["dd%d" % h]
            op("t", lambda: PE.matmul(dd[0:8, DW:DW + 128], T.qh[:, 8 * h:8 * h + 8], T.identh[:], True, True),
               r=["qh", "identh"], w=[("dd%d" % h, DW, DW + 128)])
            for r in range(16):
                op("t", lambda: PE.matmul(dd[32:40, DW + r:DW + 128:16], T.identh[:, r:128:16], T.qh[:, 8 * h:8 * h + 8], True, True),
                   r=["qh", "identh"], w=[("dd%d" % h, DW, DW + 128)])
        for k in range(2):
            op("v", lambda: ts(T.g8[:, 8 * k:8 * k + 8], T.jr[:, 0:8], T.pf[:, 2:3], A.is_equal, 1.0 - 2 * k, A.mult), r=["jr"] + pc, w=[("g8", 8 * k, 8 * k + 8)])
        op("v", lambda: V.tensor_tensor(T.dmat[:], T.t1[:, 0:136], T.t1[:, 1:137], A.subtract), r=["t1"], w=["dmat"])
        for h in range(2):
            op("v", lambda: V.memset(T["ss%d" % h][:, 1:2432:17], 0.0), w=["ss%d" % h])
        if "p" in ENG["F"]:
            op("v", lambda: V.tensor_tensor(T.dmf[:], T.t1[:, 0:136], T.t1[:, 1:137], A.subtract), r=["t1"], w=["dmf"])
            fill("less", T.less[:], 0.0)
            fill("less", T.less[:, 16:136:17], -MID)
        op("v", lambda: ts(T.pf[:, 8:9], T.pf[:, 3:4], -8.0, A.mult, 56.0, A.add), r=pc, w=[("pf", 8, 9)])
        op("v", lambda: ts(T.pf[:, 9:10], T.pf[:, 4:5], 160.0, A.mult, 63.0, A.add), r=pc, w=[("pf", 9, 10)])
        flip("a", T.domt[:, DC:DC + FLIP], T.domb[:, 0:FLIP], ["domb"], [("domt", DC, DC + FLIP)])
        flip("v", T.domt[:, DC + FLIP:W], T.domb[:, FLIP:NV], ["domb"], [("domt", DC + FLIP, W)])
        op("v", lambda: ts(T.pf[:, 10:11], T.pf[:, 8:9], T.pf[:, 3:4], A.mult, T.pf[:, 9:10], A.add), r=[("pf", 0, 10)], w=[("pf", 10, 11)])
        for c in range(4):
            ends = [("zd", e - 1, e) for e in (segs[c][1], segs[c + 4][1])]
            view = T.zd[:, segs[c][1] - 1:DW:160]
            op("v", lambda: ts(view, view, T.pf[:, 1:2], A.max, 16.0 * c, A.add), r=ends + pc, w=ends)
        op("v", lambda: ts(T.endu[:, 0:2], T.jr[:, 0:2], float(DW), A.mult, T.pf[:, 10:11], A.add), r=["jr", ("pf", 10, 11)], w=[("endu", 0, 2)])
        op("v", lambda: V.tensor_copy(T.zd[:, DW:2 * DW], T.zd[:, 0:DW]), r=[("zd", 0, DW)], w=[("zd", DW, 2 * DW)])
        op("v", lambda: V.memset(T.rb[:, 16:136:17], -10000.0), w=["rb"])
        op("v", lambda: V.memset(T.domt[:, 0:DC], TOP), w=[("domt", 0, DC)])

    def gather(q, out, src, r, w):
        if q == "p":
            op(q, lambda: g.affine_select(out, src, [[0, out.shape[1]]], A.is_ge, 0.0, 0, 0), r=r, w=w)
        else:
            op(q, (lambda: S.activation(out, src, F.Copy)) if q == "a" else (lambda: V.tensor_copy(out, src)), r=r, w=w)

    def flip(q, out, src, r, w):
        op(q, (lambda: S.activation(out, src, F.Identity, bias=TOP, scale=-1.0)) if q == "a" else (lambda: ts(out, src, -1.0, A.mult, TOP, A.add)), r=r, w=w)

    def shift(q, out, src, c, r, w):
        op(q, (lambda: S.activation(out, src, F.Identity, bias=c)) if q == "a" else (lambda: ts(out, src, c, A.add)), r=r, w=w)

    def by(tab, name, lo, hi):
        gap = 8 * (lo // 128)
        a, b = lo // 16 + gap, hi // 16 + gap
        return T[tab][:, 0:W].indirect(T[name][:, a:b]), (name, a, b)

    def piece(s, j):
        return (CUTL if CUTL and s >= 2 * RO - 2 else CUT)[s % 2][j:j + 2]

    def halves(j, n):
        return n * (j % 2), n * min(j + 1, 2)

    def PG(s, j):
        k, (lo, hi) = s % 2, halves(j, 128)
        tab = "oct" if k else "tpt"
        src, span = by(tab, "li%d" % k, lo, hi)
        gather(ENG["P"][2 * k + j % 2], T["pu%d" % k][:, lo:hi], src, [tab, span], [("pu%d" % k, lo, hi)])

    def PF(s, j):
        k, (lo, hi) = s % 2, halves(j, 128)
        if ENG["F"][2 * k + j] == "p":
            op("p", lambda: g.affine_select(T["pf%d" % k][:, lo:hi], T["pu%d" % k][:, lo:hi], [[0, hi - lo]], A.is_ge, 0.0, 0, 0),
               r=[("pu%d" % k, lo, hi)], w=[("pf%d" % k, lo, hi)])
        else:
            shift(ENG["F"][2 * k + j], T["pw%d" % k][:, lo:hi], T["pu%d" % k][:, lo:hi], -MID, [("pu%d" % k, lo, hi)], [("pw%d" % k, lo, hi)])

    def DM(s, h):
        k, lo, hi = s % 2, 128 * h, 128 * h + 128
        out, w = T["kd%d" % h][:, 256:392], [("kd%d" % h, 256, 392)]
        if ENG["F"][2 * k + h] == "p":
            op("t", lambda: PE.matmul(out, T.identh[:], T.less[:], True, False), r=["identh", "less"], w=w)
            op("t", lambda: PE.matmul(out, T["pf%d" % k][:, lo:hi], T.dmf[:], False, True), r=[("pf%d" % k, lo, hi), "dmf"], w=w)
        else:
            op("t", lambda: PE.matmul(out, T["pw%d" % k][:, lo:hi], T.dmat[:], True, True), r=[("pw%d" % k, lo, hi), "dmat"], w=w)

    def G(s, j):
        k = s % 2
        lo, hi = piece(s, j)
        tab = "valt" if k else "domt"
        flip("v" if j in ONV[k] else "a", T["x%d" % k][:, 16 * lo:16 * hi], T[tab][:, DC:W].indirect(T["pu%d" % k][:, lo:hi]),
             [tab, ("pu%d" % k, lo, hi)], [("x%d" % k, lo, hi)])

    def SC(s, j):
        k = s % 2
        lo, hi = (0, 128) if j == 9 else piece(s, j)
        op("v", lambda: V.tensor_tensor_scan(T["y%d" % k][:, 16 * lo:16 * hi], T.zmin[:, 0:16 * (hi - lo)], T["x%d" % k][:, 16 * lo:16 * hi],
                                             0.0, A.max, A.min), r=["zmin", ("x%d" % k, lo, hi)], w=[("y%d" % k, lo, hi)])

    def KEY(s, j):
        k = s % 2
        lo, hi = KCUT[k][j]
        h = lo // 128
        for i in range(16):
            op("t", lambda: PE.matmul(T["kd%d" % h][lo - 128 * h:hi - 128 * h, i:136:17], T["x%d" % k][:, 16 * lo + i:16 * hi:16],
                                      T.g8[:, 8 * k:8 * k + 8], True, True), r=[("x%d" % k, lo, hi), "g8"], w=[("kd%d" % h, 0, 136)])

    def A1(s, h):
        op("v", lambda: V.tensor_tensor_scan(T["mm%d" % h][:, 1:137], T.rb[:], T["kd%d" % h][:, 0:136], LOW, A.add, A.max),
           r=["rb", ("kd%d" % h, 0, 136)], w=["mm%d" % h])

    def A2(s, h):
        lo, hi = halves(h, 136)
        op("v", lambda: V.tensor_tensor(T.ll[:, lo:hi], T["kd%d" % h][:, 0:136], T["mm%d" % h][:, 0:136], A.is_le),
           r=[("kd%d" % h, 0, 136), "mm%d" % h], w=[("ll", lo, hi)])

    def A3(s, h):
        lo, hi = halves(h, 136)
        op("v", lambda: V.tensor_tensor_scan(T["ss%d" % h][:, 0:2176:16], T["kd%d" % h][:, 256:392], T.ll[:, lo:hi], 0.0, A.add, A.mult),
           r=[("kd%d" % h, 256, 392), ("ll", lo, hi)], w=["ss%d" % h])

    def chosen(h):
        return T["ss%d" % h][:, 256:2176:272]

    def direct(s, h):
        return "V1%d" % h in ORDER if s % 2 else "V2%d" % h in ORDER or "V0%d" % h in ORDER

    def LV(s, h):
        k = s % 2
        for r in range(16) if s else ():
            op("t", lambda: PE.matmul(T["lp%d" % k][:, 8 * h:8 * h + 8], T["ss%d" % h][:, 256 - 17 * r:2432 - 17 * r:17], T.identh[:, r:128:16],
                                      r == 0, r == 15), r=["ss%d" % h, "identh"], w=[("lp%d" % k, 8 * h, 8 * h + 8)])

    def E(s, h):
        (lo, hi), dd = halves(h, 136), T["dd%d" % h]
        for r in range(16):
            op("t", lambda: PE.matmul(dd[0:8, DW + r:DW + 128:16], T.identh[:, r:128:16], chosen(h), True, True),
               r=["ss%d" % h, "identh"], w=[("dd%d" % h, DW, DW + 128)])
        op("t", lambda: PE.matmul(dd[32:40, DW:DW + 128], chosen(h), T.identh[:], True, True),
           r=["ss%d" % h, "identh"], w=[("dd%d" % h, DW, DW + 128)])

    def BC(s, j):
        k, (lo, hi) = s % 2, halves(j, 128)
        gather(ENG["B"][2 * k + j], T.lt[0:40, lo:hi], T["dd%d" % j][0:40, DW:DW + 128], [("dd%d" % j, DW, DW + 128)], [("lt", lo, hi)])
        for h in range(*halves(j, 1)) if s and not direct(s, j) else ():
            op("t", lambda: PE.matmul(T["lp%d" % k][:, 8 * h:8 * h + 8], T.lt[0:40, 128 * h:128 * h + 128], T.identh[0:40, 0:8], True, True),
               r=[("lt", lo, hi), "identh"], w=[("lp%d" % k, 8 * h, 8 * h + 8)])

    def U(s, j):
        k, (lo, hi) = s % 2, halves(j, 8)
        a = 2 * lo
        if s:
            shift(ENG["U"][2 * k + j % 2], T["li%d" % k][:, a:a + hi - lo], T["lp%d" % k][:, lo:hi], MID + DC,
                  [("lp%d" % k, lo, hi)], [("li%d" % k, a, a + hi - lo)])

    def BP(s, h):
        dd, a = T["dd%d" % h], 128 * h
        op("t", lambda: PE.matmul(dd[:, 0:DW], T.lt[0:40, a:a + 128], T.r2[0:40, :], True, False), r=[("lt", a, a + 128), "r2"], w=[("dd%d" % h, 0, DW)])
        for b, (lo, hi) in enumerate(segs):
            op("t", lambda: PE.matmul(dd[:, lo:hi], T.gs[0:40, :], T.lt[0:40, a + 16 * b:a + 16 * b + hi - lo], False, b == 7),
               r=[("lt", a, a + 128), "gs"], w=[("dd%d" % h, 0, DW)])

    def SG(s, h):
        k = s % 2
        op("a", lambda: S.activation(T["sg%d" % k][:, DW * h:DW * h + DW], T["dd%d" % h][:, 0:DW], F.Abs, scale=FAR),
           r=[("dd%d" % h, 0, DW)], w=[("sg%d" % k, DW * h, DW * h + DW)])

    def DS(s, j):
        k = s % 2
        off = "offa%d" % (s // 2) if k else "offc"
        h0, h1 = ((0, 2), (0, 1), (1, 2))[j // 2]
        lo, hi = DW * h0, DW * h1
        if j % 2 == 0:
            op("v", lambda: V.tensor_tensor_scan(T.dsc[:, lo:hi], T["sg%d" % k][:, lo:hi], T.zd[:, lo:hi], 1.0, A.min, A.max),
               r=[("sg%d" % k, lo, hi), "zd"], w=[("dsc", lo, hi)])
        else:
            a, b = 16 * h0, 16 * h1
            ends = T.endu[:, 0:h1 - h0]
            op("v", lambda: V.tensor_tensor(T[off][:, a:b], T.dsc[:, lo:hi].indirect(ends), T["li%d" % k][:, a:b], A.min),
               r=[("dsc", lo, hi), "endu", ("li%d" % k, a, b)], w=[(off, a, b)])

    def SW(t, b):
        lo, hi = WBLK[b]
        out, span = by("valt", "offc", lo, hi)
        op("v", lambda: V.tensor_copy(out, T.y0[:, 16 * lo + 15:16 * hi:16]), r=[span, ("y0", lo, hi)], w=["valt"])

    LAST = len(SENDS) - 1
    OWN = SENDS[LAST][0]

    def rmw(t):
        return "J0" in (ORDER if t < RO - 1 else FINAL)

    def folds(t):
        return "Y0" in (ORDER if t < RO - 1 else FINAL)

    def DG(t, h):
        src, span = by("domt", "li1", 128 * h, 128 * h + 128)
        gather("a", T["dg%d" % t][:, 128 * h:128 * h + 128], src, ["domt", span], [("dg%d" % t, 128 * h, 128 * h + 128)])

    def YC(t, j):
        lo, hi = SENDS[j]
        gather(ENG["Y"][j], T["m%d" % t][:, lo:hi], T.y1[:, 16 * lo + 15:16 * hi:16], [("y1", lo, hi)], [("m%d" % t, lo, hi)])

    def DA(t, j):
        lo, hi = SENDS[LAST]
        src, span = by("domt", "li1", lo, hi)
        gather(ENG["J"], T.da[:, 0:hi - lo], src, ["domt", span], ["da"])

    def GM(t, j):
        lo, hi = SENDS[j]
        src, span = by("domt", "li1", lo, hi)
        kept = j == LAST and rmw(t)
        op("v", lambda: V.tensor_tensor(T["m%d" % t][:, lo:hi], T.da[:, 0:hi - lo] if kept else src, T.y1[:, 16 * lo + 15:16 * hi:16], A.max),
           r=(["da"] if kept else ["domt", span]) + [("y1", lo, hi)], w=[("m%d" % t, lo, hi)])

    def summed(t, own, lo, hi):
        if t == RO - 1 and (lo >= OWN and rmw(t) if own else lo >= LATE):
            o = -OWN if own else (NL - OWN) * rmw(t) - LATE
            return "fb", lo + o, hi + o

    def old(t, own, lo, hi):
        src, span = by("domt", ("offa%d" if own else "ino%d") % t, lo, hi)
        m, keep = ("m%d" % t, "mo") if own else ("inm%d" % t, "mr")
        out = summed(t, own, lo, hi)
        if out:
            op("v", lambda: V.tensor_tensor(T.fb[:, out[1]:out[2]], src, T[m][:, lo:hi], A.max), r=["domt", span, (m, lo, hi)], w=[out])
        else:
            gather("a", T[keep][:, lo:hi], src, ["domt", span], [(keep, lo, hi)])

    def SD(t, own, b):
        lo, hi = (BLK if own else SENDS)[b]
        out, span = by("domt", ("offa%d" if own else "ino%d") % t, lo, hi)
        m, keep = ("m%d" % t, "mo") if own else ("inm%d" % t, "mr")
        src = summed(t, own, lo, hi) or (own and (lo < OWN or not rmw(t)) and (m, lo, hi))
        if own and t == RO - 1 and "H1" in FINAL:
            src = None
        if own and folds(t) and "Y%d" % b in ORDER:
            src, keep = None, "dg%d" % t
        if src:
            op("v", lambda: V.tensor_copy(out, T[src[0]][:, src[1]:src[2]]), r=[span, src], w=["domt"])
        else:
            op("v", lambda: V.tensor_tensor(out, T[keep][:, lo:hi], T[m][:, lo:hi], A.max), r=[span, (keep, lo, hi), (m, lo, hi)], w=["domt"])

    def SEND(t, j):
        dst = T.cores[(rank + 1 + t % (N - 1)) % N]
        rid, pid, _ = topo.addr(dst)
        src, land = ("offa%d" % t, "ino%d" % t) if j in (0, 8, 9) else ("m%d" % t, "inm%d" % t)
        lo, hi = {0: (0, 24), 8: (0, 8), 9: (16, 24)}[j] if j in (0, 8, 9) else SENDS[j - 1]
        sem = "in%d_%d" % (t, j)

        both = folds(t) and "Y%d" % (j - 1) in ORDER

        def call():
            if both:
                g.remote_dma_fused([RemoteDMATransfer(dst_ids=[DstId(rid=rid, pnc=pid)], dma_engine_mask=topo.mask(core, dst), remote_sem=T.sem[sem],
                                                      srcs=[T[src][:, lo:hi], T["dg%d" % t][:, lo:hi]], dsts=[T[land][:, lo:hi]], alu_op=2)],
                                   local_sem=T.sem.loc)
            else:
                g.remote_dma(T[land][:, lo:hi], T[src][:, lo:hi], T.sem[sem], T.sem.loc, pid, rid, topo.mask(core, dst))
        op("p", call, r=[(src, lo, hi)] + [("dg%d" % t, lo, hi)] * both, sem="loc", n=len(topo.engines(core, dst)))
        count[sem] = len(topo.engines(T.cores[(rank - 1 - t % (N - 1)) % N], core))
        done.append(("far", sem, count[sem], [], [(land, lo, hi)], {land}))
        TAG.append((TAG[0][0], "far", [], [(land, lo, hi)]))

    def turned_sum(j, tab, ident, n, bank, out, w):
        if j == 0:
            for c in range(n // 128):
                op("t", lambda: PE.matmul(T[bank][:, 0:128], T[tab][:, DC + 128 * c:DC + 128 * c + 128], T[ident][:], c == 0, c == n // 128 - 1),
                   r=[(tab, DC, DC + n), ident], w=[bank])
        elif j == 1:
            op("a", lambda: S.activation(T.sb[:], T[bank][:, 0:128], F.Copy), r=[bank], w=["sb"])
            op("t", lambda: PE.matmul(T[bank][:, 256:258], T.sb[:], T.ones[:], True, True), r=["sb", "ones"], w=[bank])
        else:
            op("a", lambda: S.activation(out, T[bank][:, 256:257], F.Copy), r=[bank], w=w)

    late = [(True,) + SENDS[LAST]] * rmw(RO - 1) + [(False,) + p for p in SENDS if p[0] >= LATE]
    c0 = (NL - OWN) * rmw(RO - 1) + NL - LATE

    def END(n, t):
        if n == "YV":
            flip("a", T.yb[:], T["m%d" % t][:], ["m%d" % t], ["yb"])
            op("s", lambda: g.sync.dma_start(T.yv[:], T.yb[:]), r=["yb"], sem="st0", n=16)
        elif n in ("SV", "SW", "SX"):
            turned_sum("VWX".index(n[1]), "valt", "identb", NV, "sp", T.yss[:, 1:2], [("yss", 1, 2)])
        elif n in ("SP", "SQ", "SR"):
            turned_sum("PQR".index(n[1]), "domt", "ident", SUMS[0], "lp0", T.fb[:, c0 + 6:c0 + 7], [("fb", c0 + 6, c0 + 7)])
        elif n == "Z0":
            op("p", lambda: g.iota(T.domt[:, 0:DC], [[0, DC]], int(TOP), 0, **fl), w=[("domt", 0, DC)])
        elif n == "SA":
            op("a", lambda: S.activation(T.x0[:, SUMS[0]:SUMS[1]], T.domt[:, DC + SUMS[0]:DC + SUMS[1]], F.Copy, accum_out=T.fb[:, c0 + 1:c0 + 2]),
               r=[("domt", DC + SUMS[0], DC + SUMS[1])], w=["x0", ("fb", c0 + 1, c0 + 2)])
        elif n == "SB":
            op("v", lambda: V.tensor_reduce(T.fb[:, c0 + 2:c0 + 3], T.domt[:, DC + SUMS[1]:W], AxisListType.X, A.add),
               r=[("domt", DC + SUMS[1], W)], w=[("fb", c0 + 2, c0 + 3)])
        elif n[:2] == "SG":
            own, lo, hi = late[int(n[2])]
            src, span = by("domt", ("offa%d" if own else "ino%d") % t, lo, hi)
            c = c0 + 3 + int(n[2])
            op("a", lambda: S.activation(T.db[:, 0:hi - lo], src, F.Copy, scale=-1.0, accum_out=T.fb[:, c:c + 1]),
               r=["domt", span], w=["db", ("fb", c, c + 1)])
        elif n == "YT":
            for h in range(2):
                op("t", lambda: PE.matmul(T.yq[0:8, 128 * h:128 * h + 128], chosen(h), T.identh[:], True, True),
                   r=["ss%d" % h, "identh"], w=["yq"])
        elif n == "Z3":
            op("v", lambda: V.tensor_reduce(T.yss[:, 0:1], T.fb[:, 0:c0 + 7], AxisListType.X, A.add, negate=True), r=["fb"], w=[("yss", 0, 1)])
            op("s", lambda: g.sync.dma_start(T.ys[:], T.yss[:]), r=["yss"], sem="st2", n=16)
        else:
            op("a", lambda: S.activation(T.yts[:], T.yq[0:8, 0:NL], F.Identity, bias=MID), r=["yq"], w=["yts"])
            op("a", lambda: S.dma_start(T.yt[:], T.yts[:]), r=["yts"], sem="st1", n=16)

    STEP = {"G": G, "S": SC, "K": KEY, "D": DS, "E": E, "U": U, "C": SG, "M": DM, "Aa": A1, "Ab": A2, "Ac": A3, "B": BC, "Q": BP,
            "P": PG, "F": PF, "V": LV}
    ROUND = {"L": DG, "Y": YC, "N": GM, "T": SEND, "W": SW, "J": DA, "H": lambda t, j: old(t, True, *(SENDS[LAST] if rmw(t) else halves(j, 128))), "R": lambda t, j: old(t, False, *(RCUT if t < RO - 1 else RCUTL)[j]),
             "O": lambda t, b: SD(t, True, b), "I": lambda t, b: SD(t, False, b)}

    def part(n, t):
        TAG[0][0] = (n, t)
        last = t == RO - 1
        name = n.rstrip("0123456789")
        d = [int(c) for c in n[len(name):]]
        if n in ENDS:
            if last:
                END(n, t)
        elif n == "X":
            if t == 0:
                op("a", lambda: S.activation(T.identb[:], T.identh[:], F.Copy), r=["identh"], w=["identb"])
                fill("ones", T.ones[:], 1.0)
                fill("fb", T.fb[:, c0:c0 + 1], -TOP * NV)
            if t == 1:
                op("a", lambda: S.activation(T.ident[:], T.identh[:], F.Copy), r=["identh"], w=["ident"])
                fill("fb", T.fb[:, c0 + 1:c0 + 7], 0.0)
        elif name in STEP:
            if not (last and d[0] == 2) and (name, 2 * t + d[0]) != ("E", 0):
                STEP[name](2 * t + d[0], *d[1:])
        elif not (last and n == "I%d" % LAST):
            ROUND[name](t, d[0])

    consts()
    for n in FIRST:
        if n in ORDER:
            part(n, -1)
    for t in range(RO):
        for n in ORDER if t < RO - 1 else FINAL or ORDER:
            part(n, t)
    for sem, c in count.items():
        g.wait_ge(T.sem[sem], c)
